import numpy as np, ml_dtypes
CORES = [6,15,38,47]
N = 4
import mx_ref
BF = ml_dtypes.bfloat16
def tile(rs):
    return np.stack(rs, axis=2).reshape(128, -1).astype(BF)
def pick(q, e):
    c = np.concatenate([q[0].reshape(128, -1, 4), np.zeros((128, 1, 4), np.uint8)], axis=1); s = np.concatenate([q[1], np.ones((16, 1), np.uint8)], axis=1)
    return (np.ascontiguousarray(c[:, e].reshape(128, -1)), np.ascontiguousarray(s[:, e]))
def join(*qs):
    return (np.concatenate([q[0] for q in qs], axis=1), np.concatenate([q[1] for q in qs], axis=1))
def put(q, e, v):
    c, s = q[0].reshape(128, -1, 4).copy(), q[1].copy(); c[:, e] = v[0].reshape(128, -1, 4); s[:, e] = v[1]
    return (c.reshape(128, -1), s)
def pk(c, s):
    return (np.ascontiguousarray(c), mx_ref.live(s))
def emit(q):
    return q[0], q[1]
def packed(v, rng):
    q = [mx_ref.quantize(np.ascontiguousarray(v[r])) for r in range(N)]
    return np.stack([a for a, b in q]), np.stack([mx_ref.plane(b, rng) for a, b in q])
def values_of_codes():
    e, c = np.zeros((128, 128, 4), np.float32), np.zeros((128, 2, 4), np.uint8)
    e[np.arange(128), np.arange(128), 0] = 1
    c[:127, :, 0] = np.arange(256).reshape(2, 128).T[:127]
    return mx_ref.matmul(mx_ref.quantize(e.reshape(128, 512).astype(BF)), (c.reshape(128, 8), np.full((16, 2), 127, np.uint8))).T.reshape(-1).astype(np.float64)
CODE_VALUE, SCALE_VALUE = values_of_codes(), 2.0 ** (np.arange(256) - 127.0)
def decode(q):
    return (CODE_VALUE[q[0]].reshape(16, 8, -1, 4) * SCALE_VALUE[q[1]][:, None, :, None] + 0.0).reshape(128, -1).astype(np.float32)
def f(rng, *shape):
    return mx_ref.flush((rng.standard_normal(shape, dtype=np.float32) * np.exp2(rng.integers(-2, 3, shape[:-1] + (1,)))).astype(BF))
def wide(rng, *shape, cols=0):
    v = rng.standard_normal(shape, dtype=np.float32) * np.exp2(rng.integers(-12, 13, shape)).astype(np.float32)
    if cols: v *= np.repeat(np.exp2(rng.integers(-cols, cols + 1, shape[:-2] + (1, shape[-1] // 4))) * (rng.random(shape[:-2] + (1, shape[-1] // 4)) > 0.0625), 4, axis=-1).astype(np.float32)
    return mx_ref.flush(v.astype(BF))
C, H = 288, 144
MASK = [1, 2, 3]
def numbers_of(rng):
    return {"x": np.array(f(rng, N, 128, 4 * C)), "u": np.array(f(rng, N, 128, 512)), "v": np.array(f(rng, N, 128, 512))}
def layers(rng, still=[]):
    w = np.array(mx_ref.flush((np.clip(f(rng, N, 128, 2048).astype(np.float32), -4, 4) * np.float32(0.125)).astype(BF))).reshape(N, 8, 16, 4, 8, 16, 4)
    for i in still: w[:, :, :, :, :, i] = 0
    return w
def weights(rng, w):
    c, p = packed(np.ascontiguousarray(w).reshape(N, 128, 2048), rng)
    return {"wc": c, "ws": p}
def setup_inputs(rng):
    return {**numbers_of(rng), **weights(rng, layers(rng))}
def setup_inputs_ties(rng):
    d = numbers_of(rng)
    o = rng.permutation(N)
    x = d["x"].reshape(N, 8, 16, C, 4)
    k = rng.integers(0, 3, (N, 8, C)) - 4 * (o % 2)[:, None, None]
    k[o == 2] = np.arange(8)[:, None]
    x[:, :, 0] = 0
    x[:, :, 0, :, 0] = k.astype(np.float32).astype(BF)
    z = 1 + 32 * rng.permutation(C // 32)[np.arange(C) // 32] + rng.permutation(32)[np.arange(C) % 32]
    z = 4 * z[None, :] + ((np.arange(8) + int(rng.choice([2, 4, 6]))) % 8 // 2)[:, None]
    for r in range(N):
        if o[r] == 3: x[r, :, 0] = (-((z[:, :, None] >> (3 * np.arange(4))) & 7)).astype(np.float32).astype(BF)
    n = (N, 8, 8, C, 4)
    a = (129 + 2 * rng.integers(0, 64, n)) * np.exp2(-7.0 - rng.integers(8, 15, n)) * (rng.integers(0, 2, n) * 2.0 - 1.0)
    a[:, :, 0, :, 0] = 1.96875
    a = a * np.exp2(1.0 * rng.integers(-2, 3, (N, 8, 1, C, 1)))
    x[:, :, 8:] = a.astype(np.float32).astype(BF)
    u = d["u"].reshape(N, 128, 128, 4)
    u[:, :, ::16] = 0
    for r in range(N):
        for h in range(0, 128, 16):
            u[r, h, h, 0] = 0.0 if o[r] == 0 else -1.0 if o[r] == 1 else 1.0
            if o[r] == 3: u[r, h, h] = np.exp2(3.0 * np.arange(4)).astype(np.float32).astype(BF)
    return {"x": x.reshape(N, 128, 4 * C), "u": u.reshape(N, 128, 512), "v": d["v"], **weights(rng, layers(rng, [0] + [*range(8, 16)]))}
def setup_inputs_near(rng):
    d = numbers_of(rng)
    x = d["x"].astype(np.float32).reshape(N, 8, 16, C, 4)
    x[:, :, 0] = 0
    x[:, :, 8:] = 0
    u = d["u"].reshape(N, 128, 128, 4)
    u[:, :, ::16] = 0
    o = rng.permutation(N) % 4
    for r in range(N):
        s = rng.integers(0, 16, (8, C, 1))
        if o[r] < 3: x[r, :, 8] = ((s >> np.arange(4)) & 1) * np.exp2(np.arange(4) - 23.0)
        if o[r] < 2:
            x[r, :, 0, :, 0] = rng.integers(0, 2, (8, C)) * 2.0 - 1.0
            x[r, :, 11, :, 0] = 2.0 ** -10
        if o[r] == 2:
            e = rng.permutation(8)
            x[r, e[0], 0, :, 0] = 1.0
            x[r, e[1], 0, :, 0] = -1.0
        if o[r] == 3:
            x[r, :4, 10, :, 0] = rng.choice([1.0, 2.0], (4, C)) * 2.0 ** -30
            x[r, 4:, 10, :, 0] = rng.choice([1.125, 2.0], (4, C)) * 2.0 ** -30
            t = rng.permutation(C)[:C // 4]
            z = rng.integers(0, 2, (8, C // 4)) * 0.25
            c = np.where(np.arange(8) < 4, 1.0, 1.125)[:, None]
            x[r][:, 10, t, 0] = (c + z) * 2.0 ** -30
            x[r][:, 12, t, 0] = (c - z - 2.125) * 2.0 ** -30
        k = 1.0 if o[r] == 0 else 2.0 ** -30
        for h in range(0, 128, 16):
            u[r, h, h, 0] = 1.0 if o[r] == 2 else k
            u[r, h + 8, h] = k
            u[r, h + 11, h, 0] = k
            u[r, h + 10, h, 0] = k if o[r] < 3 else k * 1.25 if h < 64 else k * 1.125
            u[r, h + 12, h, 0] = 0.0 if o[r] < 3 else k * 1.125 if h < 64 else k * 1.25
    return {"x": x.reshape(N, 128, 4 * C).astype(BF), "u": u.reshape(N, 128, 512), "v": d["v"], **weights(rng, layers(rng, [0] + [*range(8, 16)]))}
def setup_inputs_huge(rng):
    d = numbers_of(rng)
    o = rng.permutation(N) % 2
    c = rng.integers(0, 2, (N, 1, 1, C, 1)) * 2.0 - 1.0
    c[o == 0] = -1.0
    x = (0.6 + 0.08 * rng.random((N, 8, 16, C, 4))) * 2.0 ** 30 * c
    a = 2.0 ** 30 * (1.0 - 0.1 * rng.random((N, 128, 8, 4)))
    a[o == 1] *= rng.choice([-1.0, 1.0], (N // 2, 1, 8, 1))
    u = d["u"].reshape(N, 128, 128, 4)
    u[:, :, ::16] = a.astype(np.float32).astype(BF)
    w = rng.integers(1, 3, (N, 8, 16, 4, 8, 16, 4)) * 2.0 ** -9 * rng.choice([-1.0, 1.0], (N, 1, 1, 4, 8, 16, 1))
    return {"x": x.astype(np.float32).reshape(N, 128, 4 * C).astype(BF), "u": u.reshape(N, 128, 512), "v": d["v"], **weights(rng, w.astype(np.float32).astype(BF))}
def setup_inputs_ends(rng):
    d = numbers_of(rng)
    o = rng.permutation(N) % 4
    most, least = 255.0 * 2.0 ** 22, 2.0 ** -30
    x = np.full((N, 8, C), least)
    u = d["u"].reshape(N, 8, 16, 128, 4)
    v = rng.choice([-1.0, 1.0], (N, 128, 512))
    for r in range(N):
        a = np.ones((8, 16, 8, 4)) * (2.0 ** -30 if o[r] == 2 else 2.0 ** 30)
        if o[r] == 0:
            x[r] = -most
            for g in rng.permutation(8)[:4]: a[:, :, g] *= rng.choice([0.5, 1.0], (8, 16, 4))
        else: a *= rng.choice([-1.0, 1.0], (8, 1, 8, 1))
        if o[r] == 1: x[r] = most * rng.choice([-1.0, 1.0], (1, C))
        if o[r] == 3: x[r] = np.where(rng.random((8, C)) < 0.5, least, most * rng.choice([-1.0, 1.0], (8, C)))
        u[r][:, :, ::16] = a.astype(np.float32).astype(BF)
        v[r] *= 2.0 ** 30 if o[r] % 2 == 0 else 2.0 ** -30
    x = x[:, :, None, :, None] * np.ones((1, 1, 16, 1, 4))
    w = rng.choice([-1.0, 1.0], (N, 8, 16, 1, 8, 2, 1, 4)) * np.full((1, 1, 1, 4, 1, 1, 8, 1), least)
    return {"x": x.astype(np.float32).reshape(N, 128, 4 * C).astype(BF), "u": u.reshape(N, 128, 512), "v": v.astype(np.float32).astype(BF), **weights(rng, w.astype(np.float32).astype(BF))}
def setup_inputs_spread(rng):
    d = setup_inputs(rng)
    d["x"] = wide(rng, N, 128, 4 * C, cols=2)
    return d
def check_inputs(d):
    b = []
    for k in ("x", "u", "v"):
        a = np.abs(d[k].astype(np.float32))
        if not (np.isfinite(a).all() and ((a == 0) | (a >= 2.0 ** -30) & (a <= 2.0 ** 30)).all()): b.append("a value of " + k)
    none, least, most = [emit(mx_ref.quantize(np.full((128, 16), k, np.float32).astype(BF)))[1][0, 0] for k in (0.0, 2.0 ** -30, 2.0 ** 30)]
    top = 0.0
    for r in range(N):
        if ((d["wc"][r] == 0x7F) | (d["wc"][r] == 0xFF)).any(): b.append("wc: a code that is no number")
        s = mx_ref.live(d["ws"][r])
        if ((s != none) & ((s < least) | (s > most))).any(): b.append("ws: a scale out of range")
        top = max(top, float(np.abs(decode(pk(d["wc"][r], d["ws"][r]))).max()))
    if not float(np.abs(d["x"].astype(np.float32)).max()) * (1.0 + 32.0 * top) * (1.0 + 32.0 * top) * (1.0 + 32.0 * top) <= 2.0 ** 30: b.append("x and W: too large together")
    return b
def reference(x, u, v, wc, ws):
    qu = [mx_ref.quantize(u[r]) for r in range(N)]
    lay = [pk(wc[r], ws[r]) for r in range(N)]
    now = [x[r] for r in range(N)]
    place = np.zeros((N, 8 * C), np.int64)
    for m in MASK:
        seats, made = [], []
        for r in range(N):
            q = mx_ref.quantize(now[r])
            own = decode(q).astype(BF).reshape(8, 16, C, 4)
            s = mx_ref.matmul(qu[r], q)[::16] + np.float32(0.0)
            o = np.argsort(-s.reshape(-1), kind="stable")
            place[r, o] = np.arange(8 * C)
            t = own[o // C, :, o % C].reshape(C, 8, 16, 4).transpose(1, 2, 0, 3)
            seats.append(mx_ref.quantize(np.ascontiguousarray(t).reshape(128, 4 * C)))
        for r in range(N):
            q = join(pick(seats[r ^ m], np.arange(H)), pick(seats[r], np.arange(H, C)))
            a = decode(q)
            t = tile([np.maximum(mx_ref.matmul(pick(lay[r], np.arange(128 * b, 128 * b + 128)), q), np.float32(0.0)) * np.float32(0.03125) + a[:, b::4] for b in range(4)])
            n = place[r].reshape(8, C)
            home = t.reshape(8, 16, C, 4)[n % 8, :, n // 8]
            made.append(np.ascontiguousarray(home.transpose(0, 2, 1, 3)).reshape(128, 4 * C))
        now = made
    y, pl = np.zeros((N, 128, C), np.float32), np.zeros((N, 8, C), np.float32)
    oc, osc = np.zeros((N, 128, 4 * C), np.uint8), np.zeros((N, 16, C), np.uint8)
    for r in range(N):
        q = mx_ref.quantize(now[r])
        y[r] = mx_ref.matmul(mx_ref.quantize(v[r]), q)
        pl[r] = place[r].reshape(8, C)
        oc[r], osc[r] = emit(q)
    return {"y": y, "pl": pl, "oc": oc, "osc": osc}

@@ -1,0 +1,477 @@
+from concourse.mybir import dt, AluOpType, AxisListType, ActivationFunctionType
+
+OP = AluOpType
+ACT = ActivationFunctionType
+C = 288
+H = 144
+BIG = 1.0e29
+EPS = 2.0 ** -24 + 2.0 ** -40
+DELTA = 2.0 ** -100
+MASKS = [1, 2, 3]
+
+SCRATCH = {}
+for _t, _s in (
+        ("float32", "pf 16 gm 8 it0 320 it1 320 it2 320 neg8 8 own8 8 offadd 144 offt 144 offe 144 offo 144 msel 144 mselt 144 cvf 288 bigm 288 ssb 288 sst 288 sr 2304 dm 288 sc 288 rs 18 rk 18 pof 18 nc 144 sort 288 spm 16 spv 4 sp8 24 wm 288 wr 288 wn 72 wt 72 off32 144 off33 144 ntf 32 ntt 32 en 504 rt 1152"),
+        ("int32", "pi 8 ii 256 nt 32 ph 96"),
+        ("uint16", "clist 18 ul 72 wl 64 posl 18 off 144 phl 18 tl 72 hl 72"),
+        ("bfloat16", "dump 1152 mk16 288 mk17 288 kp16 288 kp17 288 kp4 144 cval 288 ones 64 zer 2304 ef 4096 ob 512 zb 1024 zz 1792 xt 1152 ut 512 vt 512 ml 5760 mc 2304 mf 2304 iw0 2304 iw1 2304 iw2 2304 itr 2304 fw 2304 ow 1152 tt 1152 o2 1152 tw 2304"),
+        ("mx", "ef 1024 ob 128 zb 256 zz 448 u 128 v 128 up 1152 w 512 wl 1024 x 288 ml 1440 mc 576 mf 576 tb 144 ta0 144 ta1 144 ta2 144 lc0 144 lc1 144 lc2 144")):
+    _s = _s.split()
+    for _n, _w in zip(_s[::2], _s[1::2]):
+        if _t == "mx":
+            SCRATCH[_n + "_q"] = ("sbuf", [128, int(_w)], "float8_e4m3fn_x4")
+            SCRATCH[_n + "_s"] = ("sbuf", [128, int(_w)], "uint8")
+        else:
+            SCRATCH[_n] = ("sbuf", [128, int(_w)], _t)
+for _m in range(8):
+    SCRATCH["p%d" % _m] = ("psum", [128, 512], "float32")
+
+SEMAPHORES = "sv sa st sg lx lu lw ls lv z0 z1 z2 z3 z4 z5 z6 outd arr0 arr1 arr2 sent0 sent1 sent2".split()
+
+
+def rank_program(g, core, T, topo):
+    rank = T.rank_of(core)
+    if rank is None:
+        return
+    wait = {"V": g.vector.wait_ge, "S": g.scalar.wait_ge, "T": g.tensor.wait_ge, "G": g.wait_ge, "Y": g.sync.wait_ge}
+    own = {"V": "sv", "S": "sa", "T": "st", "G": "sg"}
+    total, snaps, hist = {}, {}, {}
+    known = {q: {} for q in "VSTGYR"}
+
+    def view(name, c0, c1, st=1, p0=0, p1=128):
+        if p0 == 0 and p1 == 128:
+            ap = T[name][:, c0:c1] if st == 1 else T[name][:, c0:c1:st]
+        else:
+            ap = T[name][p0:p1, c0:c1] if st == 1 else T[name][p0:p1, c0:c1:st]
+        return (name, p0, p1, c0, c1, st, ap)
+
+    def clash(a, b):
+        if a[1] >= b[2] or b[1] >= a[2] or a[3] >= b[4] or b[3] >= a[4]:
+            return False
+        return not (a[5] == b[5] and a[5] > 1 and (a[3] - b[3]) % a[5])
+
+    def covers(a, b):
+        return a[1] <= b[1] and a[2] >= b[2] and a[3] <= b[3] and a[4] >= b[4] and (a[5] == 1 or (a[5] == b[5] and (a[3] - b[3]) % a[5] == 0))
+
+    def settle(q, reads, writes, group=False):
+        need = {}
+        for kind, vs in (("r", reads), ("w", writes)):
+            for v in vs:
+                bank = SCRATCH[v[0]][0] == "psum"
+                for (k2, q2, v2, sem, val) in hist.get(v[0], []):
+                    if q2 == q and q in "VSTG":
+                        if (kind == "r" and k2 == "r") or (group and bank) or not clash(v, v2):
+                            continue
+                    elif not bank and ((kind == "r" and k2 == "r") or not clash(v, v2)):
+                        continue
+                    need[sem] = max(need.get(sem, 0), val)
+        kn = known[q]
+        for sem, val in sorted(need.items(), key=lambda e: -e[1]):
+            if kn.get(sem, 0) >= val:
+                continue
+            wait[q](T.sem[sem], val)
+            kn[sem] = val
+            for s2, v2 in snaps.get((sem, val), {}).items():
+                kn[s2] = max(kn.get(s2, 0), v2)
+
+    def note(q, sem, val, reads, writes):
+        snaps[(sem, val)] = dict(known[q])
+        for k, vs in (("w", writes), ("r", reads)):
+            for v in vs:
+                h = hist.setdefault(v[0], [])
+                if k == "w":
+                    h[:] = [e for e in h if not covers(v, e[2])]
+                else:
+                    h[:] = [e for e in h if not (e[0] == "r" and e[1] == q and q in "VSTG" and covers(v, e[2]))]
+                h.append((k, q, v, sem, val))
+
+    def run(q, call, reads, writes, group=False):
+        settle(q, reads, writes, group)
+        sem = own[q]
+        total[sem] = total.get(sem, 0) + 1
+        call().then_inc(T.sem[sem], 1)
+        note(q, sem, total[sem], reads, writes)
+
+    def dma(sem, out, in_, reads, writes):
+        settle("Y", reads, writes)
+        total[sem] = total.get(sem, 0) + 16
+        g.sync.dma_start(out, in_).then_inc(T.sem[sem], 16)
+        note("Y", sem, total[sem], reads, writes)
+
+    def ap(x):
+        return x[6] if isinstance(x, tuple) else x
+
+    def rd(*xs):
+        return [x for x in xs if isinstance(x, tuple)]
+
+    def ts(out, a, s1, op0, s2=None, op1=None):
+        if op1 is None:
+            run("V", lambda: g.vector.tensor_scalar(out[6], a[6], ap(s1), None, op0), rd(a, s1), [out])
+        else:
+            run("V", lambda: g.vector.tensor_scalar(out[6], a[6], ap(s1), ap(s2), op0, op1), rd(a, s1, s2), [out])
+
+    def tt(out, a, b, op):
+        run("V", lambda: g.vector.tensor_tensor(out[6], a[6], b[6], op), [a, b], [out])
+
+    def tc(out, a):
+        run("V", lambda: g.vector.tensor_copy(out[6], a[6]), [a], [out])
+
+    def fill(out, c):
+        run("V", lambda: g.vector.memset(out[6], c), [], [out])
+
+    def sums(out, keep, a):
+        run("V", lambda: g.vector.tensor_tensor_scan(out[6], keep[6], a[6], 0.0, OP.mult, OP.add), [keep, a], [out])
+
+    def fetch(out, win, off):
+        run("S", lambda: g.scalar.activation(out[6], win[6].indirect(off[6]), ACT.Copy), [win, off], [out])
+
+    def gather2(out, c0, win, off, o0, n):
+        m = n // 2
+        a, e = view(out, c0, c0 + 16 * m), view(off, o0, o0 + m)
+        run("V", lambda: g.vector.tensor_copy(a[6], win[6].indirect(e[6])), [win, e], [a])
+        fetch(view(out, c0 + 16 * m, c0 + 16 * n), win, view(off, o0 + m, o0 + n))
+
+    def fused(out, win, off, b, op):
+        run("V", lambda: g.vector.tensor_tensor(out[6], win[6].indirect(off[6]), b[6], op), [win, off, b], [out])
+
+    def scatter(win, off, a):
+        run("V", lambda: g.vector.tensor_copy(win[6].indirect(off[6]), a[6]), [a, off], [win])
+
+    def turn(out, a):
+        run("V", lambda: g.vector.transpose(out[6], a[6]), [a], [out])
+
+    def quant(n, a, c0, c1):
+        o, p = view(n + "_q", c0, c1), view(n + "_s", c0, c1)
+        run("V", lambda: g.vector.quantize_mx(o[6], p[6], a[6]), [a], [o, p])
+
+    def act(out, a, f=ACT.Copy, scale=1.0, bias=0.0):
+        if isinstance(scale, tuple):
+            run("S", lambda: g.scalar.activation(out[6], a[6], f, scale=scale[6]), [a, scale], [out])
+        elif bias:
+            run("S", lambda: g.scalar.activation(out[6], a[6], ACT.Identity, bias=bias, scale=scale), [a], [out])
+        elif scale == 1.0:
+            run("S", lambda: g.scalar.activation(out[6], a[6], f), [a], [out])
+        else:
+            run("S", lambda: g.scalar.activation(out[6], a[6], f, scale=scale), [a], [out])
+
+    def iota(out, pattern, base=0, cm=0, f=True):
+        if f:
+            run("G", lambda: g.iota(out[6], pattern, base, cm, allow_small_or_imprecise_dtypes=True), [], [out])
+        else:
+            run("G", lambda: g.iota(out[6], pattern, base, cm), [], [out])
+
+    def mm(bank, n, l, l0, r, r0, start=True, stop=True):
+        o = view("p%d" % bank, 0, n)
+        lq, ls, rq, rs = view(l + "_q", l0, l0 + 128), view(l + "_s", l0, l0 + 128), view(r + "_q", r0, r0 + n), view(r + "_s", r0, r0 + n)
+        run("T", lambda: g.tensor.matmul_mx(o[6], lq[6], ls[6], rq[6], rs[6], start, stop), [lq, ls, rq, rs], [o], group=not start)
+
+    def ps(bank, c0, c1, st=1):
+        return view("p%d" % bank, c0, c1, st)
+
+    def pick(dst, src, n0, n1, w, off):
+        o, i, o2, i2 = view(dst + "_q", n0, n1), view(src + "_q", 0, w), view(dst + "_s", n0, n1), view(src + "_s", 0, w)
+        run("V", lambda: g.vector.tensor_copy(o[6].bitcast(dt.uint32), i[6].bitcast(dt.uint32).indirect(off[6])), [i, off], [o])
+        fetch(o2, i2, off)
+
+    for sem, name, src, w in (("lx", "xt", T.x, 1152), ("lu", "ut", T.u, 512)):
+        dma(sem, T[name][:, 0:w], src[:], [], [view(name, 0, w)])
+    dma("lw", T.w_q[:, 0:512].bitcast(dt.uint8), T.wc[:], [], [view("w_q", 0, 512)])
+    dma("ls", T.w_s[:, 0:512], T.ws[:], [], [view("w_s", 0, 512)])
+    dma("lv", T.vt[:, 0:512], T.v[:], [], [view("vt", 0, 512)])
+    pf = [view("pf", k, k + 1) for k in range(11)]
+    kappa, group, parity, kap4 = pf[1], pf[2], pf[3], pf[5]
+    pi = [view("pi", k, k + 1) for k in range(8)]
+    iota(pi[0], [[0, 1]], 0, 1, f=False)
+    iota(view("ii", 0, 8), [[16, 8]], f=False)
+    iota(view("ii", 8, 72), [[16, 8], [0, 8]], f=False)
+    iota(view("it0", 0, 288), [[0, 18], [1, 16]])
+    iota(view("it1", 144, 152), [[1, 8]])
+    iota(view("ii", 72, 90), [[16, 18]], 15, 0, f=False)
+    iota(view("it1", 0, 144), [[1, 8], [0, 18]])
+    iota(view("it2", 0, 289), [[0, 17], [1, 17]])
+    iota(view("cvf", 0, 288), [[1, 288]], -144, 0)
+    iota(view("it1", 160, 304), [[0, 36], [1, 4]])
+    iota(view("ii", 96, 160), [[16, 8], [128, 4], [0, 2]], f=False)
+
+    fill(view("zer", 0, 2304), 0.0)
+    for sem, name, c0, c1 in (("z0", "ef", 0, 2304), ("z1", "ef", 2304, 4096), ("z5", "zb", 0, 1024), ("z6", "zz", 0, 1792), ("z2", "iw0", 0, 2304), ("z3", "iw1", 0, 2304), ("z4", "iw2", 0, 2304)):
+        dma(sem, T[name][:, c0:c1], T.zer[:, 0:c1 - c0], [view("zer", 0, c1 - c0)], [view(name, c0, c1)])
+    fill(view("ones", 0, 64), 1.0)
+    fill(view("rs", 0, 1), 0.0)
+    act(view("ml", 0, 512), view("zer", 0, 512))
+    act(view("ml", 1152, 1664), view("zer", 0, 512))
+    for al, b, c, w in ((2, 0, 144, 192), (2, 1, 160, 192), (2, 2, 176, 192), (3, 0, 208, 256), (3, 1, 224, 256), (3, 2, 240, 256), (4, 0, 272, 288), (4, 3, 0, 288)):
+        act(view("ml", 1152 * al + 4 * c + b, 1152 * al + 4 * w, 4), view("zer", 0, w - c))
+    tc(view("ul", 0, 72), view("ii", 0, 72))
+    ts(pi[1], pi[0], 15, OP.bitwise_and)
+    ts(pi[2], pi[0], 4, OP.logical_shift_right)
+    ts(pi[3], pi[0], 4, OP.logical_shift_right, 1, OP.bitwise_and)
+    ts(pi[4], pi[0], 5, OP.logical_shift_right)
+    ts(pi[5], pi[0], 15, OP.bitwise_and, 2, OP.logical_shift_right)
+    ts(pi[6], pi[0], 4, OP.bitwise_and, 2, OP.logical_shift_right)
+    tc(view("pf", 0, 7), view("pi", 0, 7))
+    act(pf[7], pf[4], ACT.Identity, 576.0, 144.0)
+    act(pf[8], pf[4], ACT.Identity, 576.0, 432.0)
+    act(pf[9], pf[6], ACT.Copy, 4096.0)
+    act(pf[10], pf[6], ACT.Identity, -4096.0, 4096.0)
+    ts(view("mk16", 0, 288), view("it0", 0, 288), kappa, OP.is_equal)
+    ts(view("kp16", 0, 288), view("it0", 0, 288), 0.0, OP.not_equal)
+    ts(view("gm", 0, 8), view("it1", 144, 152), group, OP.is_equal)
+    for h in range(8):
+        for t in range(4):
+            o, i = view("ef", 512 * h + 128 * t + t, 512 * h + 128 * t + 128, 4), view("ones", 0, 32)
+            run("G", lambda: g.affine_select(o[6], i[6], [[0, 2], [-1, 16]], OP.is_equal, 0.0, -16 * h, 1), [i], [o])
+    quant("u", view("ut", 0, 512), 0, 128)
+    pick("up", "u", 0, 128, 128, view("ul", 0, 8))
+
+    def constants_0():
+        ts(view("bigm", 0, 288), view("it0", 0, 288), kappa, OP.is_le, BIG, OP.mult)
+        tc(view("clist", 0, 18), view("ii", 72, 90))
+
+    def constants_1():
+        pick("up", "u", 128, 1152, 128, view("ul", 8, 72))
+        for k in range(8):
+            act(view("ob", 64 * k, 64 * k + 64), view("ones", 0, 64), ACT.Copy, view("gm", k, k + 1))
+        quant("ob", view("ob", 0, 512), 0, 128)
+        for z in range(4):
+            for b in range(4):
+                act(view("zb", 512 * (z // 2) + 16 * z + 5 * b, 512 * (z // 2) + 512, 64), view("gm", 0, 8))
+
+    def constants_2():
+        for w in range(2):
+            for b in range(4):
+                act(view("zz", 896 * w + 384 + 5 * b, 896 * w + 512, 16), view("ones", 0, 8), ACT.Copy, 16.0 if w else 1.0)
+        act(view("cval", 0, 288), view("cvf", 0, 288))
+        ts(view("neg8", 0, 8), view("it1", 144, 152), group, OP.is_lt, -1.0, OP.mult)
+        ts(view("own8", 0, 8), view("it1", 144, 152), group, OP.is_equal, -BIG, OP.mult)
+        ts(view("offadd", 0, 144), view("it1", 0, 144), group, OP.is_lt, 24.0, OP.mult)
+        ts(view("offt", 0, 144), view("it1", 0, 144), group, OP.is_equal, 48.0, OP.mult)
+        ts(view("kp17", 0, 288), view("it2", 0, 288), 0.0, OP.not_equal)
+        tt(view("offadd", 0, 144), view("offadd", 0, 144), view("offt", 0, 144), OP.add)
+        ts(view("kp4", 0, 144), view("it1", 160, 304), 0.0, OP.not_equal)
+        ts(view("offe", 0, 144), view("offadd", 0, 144), pf[9], OP.subtract)
+        ts(view("offo", 0, 144), view("offadd", 0, 144), pf[10], OP.subtract)
+        ts(view("mk17", 0, 288), view("it2", 0, 288), kappa, OP.is_equal)
+        fill(view("wn", 0, 48), 0.0)
+        fill(view("wn", 48, 72), -BIG)
+        ts(view("msel", 0, 144), view("it1", 160, 304), kap4, OP.is_equal)
+        ts(view("mselt", 0, 144), view("msel", 0, 144), parity, OP.mult)
+        quant("ef", view("ef", 0, 2048), 0, 512)
+        tt(view("mselt", 0, 72), view("msel", 0, 72), view("mselt", 0, 72), OP.subtract)
+        quant("ef", view("ef", 2048, 4096), 512, 1024)
+        quant("zb", view("zb", 0, 1024), 0, 256)
+        quant("zz", view("zz", 0, 1792), 0, 448)
+        fill(view("cval", 144, 145), 0.25)
+
+    def constants_3():
+        ts(view("ii", 160, 224), view("ii", 96, 160), kappa, OP.add)
+        tc(view("wl", 0, 64), view("ii", 160, 224))
+        pick("wl", "w", 0, 1024, 512, view("wl", 0, 64))
+        quant("v", view("vt", 0, 512), 0, 128)
+
+    def places(rnd):
+        mm(0, C, "up", 0, "x", 0)
+        if rnd == 0:
+            constants_0()
+        tt(view("dm", 0, 288), ps(0, 0, 288), view("mk16", 0, 288), OP.mult)
+        tc(view("ssb", 0, 288), ps(0, 0, 288))
+        sums(view("sc", 0, 288), view("kp16", 0, 288), view("dm", 0, 288))
+        tt(view("sst", 0, 288), ps(0, 0, 288), view("bigm", 0, 288), OP.add)
+        if rnd == 0:
+            constants_1()
+
+        def sr_rows(ks):
+            for k in ks:
+                act(view("sr", 288 * k, 288 * k + 288), ps(2 + k % 4, 0, 288))
+
+        for k in range(4):
+            mm(2 + k % 4, C, "up", 128 + 128 * k, "x", 0)
+        sr_rows(range(4))
+        for k in range(4, 8):
+            mm(2 + k % 4, C, "up", 128 + 128 * k, "x", 0)
+        for al in (4, 3, 2, 1, 0):
+            w = C if al == 4 else max(128, 64 * al + 64)
+            aa = range(4 * al, min(18, 4 * al + 4))
+            for a in aa:
+                ts(view("ml", 1152 * al + a % 4, 1152 * al + 64 * a + 64, 4), view("ssb", 0, 16 * a + 16), view("sc", 16 * a + 15, 16 * a + 16), OP.is_lt)
+            if al == 4:
+                fused(view("ml", 4 * 1152 + 2, 5760, 4), view("sc", 0, 288), view("clist", 0, 18), view("sst", 0, 288), OP.is_equal)
+            quant("ml", view("ml", 1152 * al, 1152 * al + 4 * w), 288 * al, 288 * al + w)
+            mm(1, w, "ob", 0, "ml", 288 * al, al == 4, al == 0)
+            for a in aa:
+                if a:
+                    i, o, acc = view("ml", 1152 * al + a % 4, 1152 * al + 64 * a, 4), view("dump", 288 * (a % 4), 288 * (a % 4) + 16 * a), view("rs", a, a + 1)
+                    run("S", lambda: g.scalar.activation(o[6], i[6], ACT.Identity, bias=1.0, scale=-1.0, accum_out=acc[6]), [i], [o, acc])
+        sr_rows(range(4, 8))
+        if rnd == 0:
+            constants_2()
+        for k in range(8):
+            mm(2 + k % 4, C, "ef", 128 * k, "x", 0)
+            act(view("fw", 288 * k, 288 * k + 288), ps(2 + k % 4, 0, 288))
+        for k, gr in enumerate((2, 3, 6, 7)):
+            mm(2 + k, C, "up", 128 + 128 * gr, "x", 0)
+        tt(view("dm", 0, 288), ps(1, 0, 288), view("mk16", 0, 288), OP.mult)
+        sums(view("wm", 0, 288), view("kp16", 0, 288), view("dm", 0, 288))
+        rk = view("rk", 0, 18)
+        tt(rk, view("wm", 15, 288, 16), view("rs", 0, 18), OP.add)
+        tc(view("posl", 0, 18), rk)
+        scatter(view("sort", 0, 288), view("posl", 0, 18), view("ssb", 0, 288))
+        sm = view("spm", 0, 16)
+        tt(sm, view("sort", 16, 288, 17), view("mk16", 0, 16), OP.mult)
+        sp, spa, dec = view("spv", 0, 1), view("spv", 1, 2), view("spv", 2, 3)
+        run("V", lambda: g.vector.tensor_reduce(spa[6], sm[6], AxisListType.X, OP.add, apply_absolute_value=True), [sm], [spa])
+        run("V", lambda: g.vector.tensor_reduce(sp[6], sm[6], AxisListType.X, OP.add), [sm], [sp])
+        ts(dec, spa, EPS, OP.mult, DELTA, OP.add)
+        ts(view("sp8", 0, 8), view("neg8", 0, 8), dec, OP.mult, sp, OP.add)
+        tt(view("sp8", 8, 16), view("sp8", 0, 8), view("own8", 0, 8), OP.add)
+        ts(view("sp8", 16, 24), view("sp8", 8, 16), dec, OP.add)
+        v = view("wr", 15, 288, 17)
+        runs = [lambda: tt(view("wm", 0, 288), view("sort", 0, 288), view("mk17", 0, 288), OP.mult),
+                lambda: sums(view("wr", 0, 288), view("kp17", 0, 288), view("wm", 0, 288)),
+                lambda: [ts(view("wt", 0, 17), v, EPS, OP.mult, -DELTA, OP.add), ts(view("wt", 24, 41), v, -EPS, OP.mult, -DELTA, OP.add)],
+                lambda: tc(view("wn", 0, 17), v),
+                lambda: tt(view("wt", 48, 65), view("wt", 0, 17), view("wt", 24, 41), OP.min),
+                lambda: tt(view("wn", 24, 41), v, view("wt", 48, 65), OP.add)]
+        for gr in range(8):
+            o, i = view("mc", 288 * gr, 288 * gr + 288), view("sr", 288 * gr, 288 * gr + 288)
+            if gr % 4 >= 2:
+                s, b = view("dump", 288 * (gr % 4), 288 * (gr % 4) + 288), view("sp8", 16 + gr, 17 + gr)
+                run("S", lambda: g.scalar.activation(s[6], i[6], ACT.Sign, bias=b[6], scale=-1.0), [i, b], [s])
+                act(o, s, ACT.Relu)
+            else:
+                ts(o, i, view("sp8", 8 + gr, 9 + gr), OP.is_le)
+            if gr < 6:
+                runs[gr]()
+            if gr % 4 == 3:
+                hf = gr // 4
+                quant("mc", view("mc", 1152 * hf, 1152 * hf + 1152), 288 * hf, 288 * hf + 288)
+                for z in range(2):
+                    mm(6 + hf, 286, "zb", 128 * z, "mc", 288 * hf + 2 * z, z == 0, z == 1)
+        for k in range(4):
+            for w in range(2):
+                mm(1, H, "zz", 224 * w + 96 - 32 * k, "mc", 144 * k, k == 0 and w == 0, False)
+        for hf in range(2):
+            c0, c1 = 72 * hf, 72 * hf + 72
+            o, o2 = view("off32", c0, c1), view("off33", c0, c1)
+            tt(o, ps(6 + hf, 0, 286, 4), view("offe", c0, c1), OP.add)
+            tt(o2, ps(6 + hf, 1, 286, 4), view("offo", c0, c1), OP.add)
+            tt(o, o, o2, OP.max)
+            tc(view("off", c0, c1), o)
+            w = view("wn", 0, 72)
+            fetch(view("rt", 576 * hf, 576 * hf + 576), w, view("off", c0 + 36, c1))
+            for k in (2 * hf, 2 * hf + 1):
+                m = view("mf", 576 * k, 576 * k + 576)
+                if k % 2 == 0:
+                    fused(m, w, view("off", 36 * k, 36 * k + 36), view("sr", 576 * k, 576 * k + 576), OP.is_ge)
+                else:
+                    for e in range(2):
+                        c = 576 * hf + 288 * e
+                        tt(view("mf", 576 * k + 288 * e, 576 * k + 288 * e + 288), view("rt", c, c + 288), ps(2 + 2 * hf + e, 0, 288), OP.is_ge)
+                quant("mf", m, 144 * k, 144 * k + 144)
+                mm(1, H, "zz", 96 - 32 * k, "mf", 144 * k, False, k == 3)
+        tt(view("wm", 0, 144), ps(1, 0, 144), view("mselt", 0, 144), OP.mult)
+        sums(view("nc", 0, 144), view("kp4", 0, 144), view("wm", 0, 144))
+        tt(view("pof", 0, 18), view("nc", 3, 72, 4), view("nc", 75, 144, 4), OP.add)
+        tt(view("nt", 0, 18), view("pof", 0, 18), rk, OP.add)
+
+    def seats(rnd):
+        n = view("nt", 0, 18)
+        ph = [view("ph", 18 * k, 18 * k + 18) for k in range(5)]
+        ts(ph[0], n, 1, OP.logical_shift_right)
+        ts(ph[1], n, 1, OP.logical_shift_right, 65520, OP.bitwise_and)
+        ts(ph[2], n, 16, OP.mult)
+        ts(ph[3], ph[0], -31, OP.mult)
+        tt(ph[2], ph[2], ph[1], OP.add)
+        tt(ph[4], ph[2], ph[3], OP.add)
+        tc(view("phl", 0, 18), ph[4])
+        iw = view("iw%d" % rnd, 0, 2304)
+        scatter(iw, view("phl", 0, 18), view("cval", 0, 288))
+        turn(view("itr", 0, 2304), iw)
+        e = [(72 * k, 72 * k + 72) for k in range(7)]
+        i0, i1 = view("itr", 0, 2304, 32), view("itr", 16, 2304, 32)
+        ts(view("en", *e[0]), i0, 0.0, OP.not_equal, pf[7], OP.mult)
+        ts(view("en", *e[1]), i1, 0.0, OP.not_equal, pf[8], OP.mult)
+        tt(view("en", *e[2]), view("en", *e[0]), i0, OP.add)
+        tt(view("en", *e[3]), view("en", *e[1]), i1, OP.add)
+        tt(view("en", *e[4]), view("en", *e[2]), view("en", *e[3]), OP.add)
+        tc(view("en", *e[5], p1=64), view("en", *e[4], p0=64))
+        tt(view("en", *e[6], p1=64), view("en", *e[4], p1=64), view("en", *e[5], p1=64), OP.add)
+        tc(view("en", *e[0], p1=32), view("en", *e[6], p0=32, p1=64))
+        tt(view("en", *e[1], p1=32), view("en", *e[6], p1=32), view("en", *e[0], p1=32), OP.add)
+        for t in range(4):
+            tc(view("tl", 0, 72, p0=32 * t, p1=32 * t + 32), view("en", *e[1], p1=32))
+
+    def native(dst, dc, src, sc, n, sst, order):
+        for k, (q, t) in enumerate(order):
+            o = view(dst, dc + t, dc + 4 * n, 4, 32 * q, 32 * q + 32)
+            if sst == 1:
+                i = view(src, sc + n * q, sc + n * q + n, 1, 32 * t, 32 * t + 32)
+            else:
+                i = view(src, sc + q, sc + 4 * n, 4, 32 * t, 32 * t + 32)
+            if k % 8 in (2, 5, 6):
+                act(o, i)
+            else:
+                tc(o, i)
+
+    ALL = [(q, t) for q in range(4) for t in range(4)]
+
+    def layer(src, half):
+        for h in range(8):
+            a, b = (2 * h) % 8, (2 * h + 1) % 8
+            mm(a, H, "wl", 128 * h, src, 0)
+            mm(b, H, "ef", 128 * h, src, 0)
+            r = view("rt", 144 * h, 144 * h + 144)
+            act(r, ps(a, 0, 144), ACT.Relu, 0.03125)
+            tt(view("tw", 1152 * half + h, 1152 * half + 1152, 8), ps(b, 0, 144), r, OP.add)
+
+    for rnd in range(3):
+        quant("x", view("xt", 0, 1152), 0, 288)
+        places(rnd)
+        seats(rnd)
+        ta, lc = "ta%d" % rnd, "lc%d" % rnd
+        gather2("ow", 0, view("fw", 0, 2304), "tl", 0, 36)
+        native("tt", 0, "ow", 0, 144, 4, ALL)
+        quant(ta, view("tt", 0, 576), 0, 144)
+        dst = T.cores[rank ^ MASKS[rnd]]
+        rid, pid = topo.addr(dst)[0], topo.addr(dst)[1]
+        mask, ne = topo.mask(core, dst), len(topo.engines(core, dst))
+        settle("G", [view(ta + "_q", 0, 144), view(ta + "_s", 0, 144)], [])
+        arr, sent = "arr%d" % rnd, "sent%d" % rnd
+        g.remote_dma(T[lc + "_q"][:, 0:144].bitcast(dt.uint8), T[ta + "_q"][:, 0:144].bitcast(dt.uint8), T.sem[arr], T.sem[sent], pid, rid, mask)
+        g.remote_dma(T[lc + "_s"][:, 0:144], T[ta + "_s"][:, 0:144], T.sem[arr], T.sem[sent], pid, rid, mask)
+        total[arr] = total[sent] = 2 * ne
+        note("R", arr, 2 * ne, [], [view(lc + "_q", 0, 144), view(lc + "_s", 0, 144)])
+        gather2("ow", 576, view("fw", 0, 2304), "tl", 36, 36)
+        native("tt", 576, "ow", 576, 144, 4, ALL)
+        quant("tb", view("tt", 576, 1152), 0, 144)
+        if rnd == 0:
+            constants_3()
+        for q in range(4):
+            tc(view("hl", 18 * q, 18 * q + 18, p1=32), view("nt", 0, 18, p0=32 * q, p1=32 * q + 32))
+        for t in range(1, 4):
+            tc(view("hl", 0, 72, p0=32 * t, p1=32 * t + 32), view("hl", 0, 72, p1=32))
+        layer("tb", 1)
+        if rnd == 2:
+            fill(view("ntf", 18, 32), 0.0)
+            tc(view("ntf", 0, 18), view("nt", 0, 18))
+            turn(view("ntt", 0, 32), view("ntf", 0, 32))
+            for gr in range(8):
+                v = view("ntt", 16 * (gr % 2), 16 * (gr % 2) + 16, 1, 32 * (gr // 2), 32 * (gr // 2) + 18)
+                dma("outd", T.pl[gr:gr + 1, :], v[6], [v], [])
+        layer(lc, 0)
+        for k in range(2):
+            gather2("o2", 576 * k, view("tw", 0, 2304), "hl", 36 * k, 36)
+            native("xt", 0, "o2", 0, 288, 1, ALL[8 * k:8 * k + 8])
+    quant("x", view("xt", 0, 1152), 0, 288)
+    mm(0, C, "v", 0, "x", 0)
+    v = view("x_q", 0, 288)
+    dma("outd", T.oc[:], v[6].bitcast(dt.uint8), [v], [])
+    for k in range(4):
+        v = view("x_s", 0, 288, 1, 32 * k, 32 * k + 4)
+        dma("outd", T.osc[4 * k:4 * k + 4, :], v[6], [v], [])
+    tc(view("dm", 0, 288), ps(0, 0, 288))
+    v = view("dm", 0, 288)
+    dma("outd", T.y[:], v[6], [v], [])
+    for sem in SEMAPHORES:
+        if known["G"].get(sem, 0) < total[sem]:
+            g.wait_ge(T.sem[sem], total[sem])

@@ -5,17 +5,22 @@ ACT = ActivationFunctionType
 C = 288
 H = 144
 BIG = 1.0e29
-EPS = 2.0 ** -24 + 2.0 ** -40
-DELTA = 2.0 ** -100
+EPS = 2.0 ** -24 + 2.0 ** -32
+DELTA = 2.0 ** -120
+STEP = 4096.0
+EMPTY = -32768.0
 MASKS = [1, 2, 3]
+ML = [0, 128, 256, 448, 704, 992]
+BY_SCALAR = (17, 16, 15)
+SB = [2, 3, 4, 0, 5, 6, 7]
 
 SCRATCH = {}
 for _t, _s in (
-        ("float32", "pf 16 gm 8 it0 320 it1 320 it2 320 neg8 8 own8 8 offadd 144 offt 144 offe 144 offo 144 msel 144 mselt 144 cvf 288 bigm 288 ssb 288 sst 288 sr 2304 dm 288 sc 288 rs 18 rk 18 pof 18 nc 144 sort 288 spm 16 spv 4 sp8 24 wm 288 wr 288 wn 72 wt 72 off32 144 off33 144 ntf 32 ntt 32 en 504 rt 1152"),
-        ("int32", "pi 8 ii 256 nt 32 ph 96"),
-        ("uint16", "clist 18 ul 72 wl 64 posl 18 off 144 phl 18 tl 72 hl 72"),
-        ("bfloat16", "dump 1152 mk16 288 mk17 288 kp16 288 kp17 288 kp4 144 cval 288 ones 64 zer 2304 ef 4096 ob 512 zb 1024 zz 1792 xt 1152 ut 512 vt 512 ml 5760 mc 2304 mf 2304 iw0 2304 iw1 2304 iw2 2304 itr 2304 fw 2304 ow 1152 tt 1152 o2 1152 tw 2304"),
-        ("mx", "ef 1024 ob 128 zb 256 zz 448 u 128 v 128 up 1152 w 512 wl 1024 x 288 ml 1440 mc 576 mf 576 tb 144 ta0 144 ta1 144 ta2 144 lc0 144 lc1 144 lc2 144")):
+        ("float32", "pf 16 i16 288 i16s 288 i17 296 gi 256 sgr 8 sgo 128 pata 288 patb 288 patr 288 pats 288 cst 8 offadd 128 hpat 56 dm 288 sc 288 ssb 288 rs 24 rk 24 scn 288 sort 288 wr 312 dec 24 sp8 8 wn 48 off32 128 s7 288 rt 1728 base 72 hb 56 hs 56 n2 24 en 504 ntf 32 ntt 32 rl 1152"),
+        ("int32", "pi 8 ii 96"),
+        ("uint16", "ul 16 wl 64 posl 18 off 128 phl 18 tl 72 hl 72"),
+        ("bfloat16", "dump 864 cval 288 ones 256 zer 1024 neg 768 gx 256 idx 256 ef 4096 ob 512 zr 2048 cn 1024 rc 1024 rq 800 xt 1152 ut 512 vt 512 ml 3968 mc 2048 mf 2304 iw0 2304 iw1 2304 iw2 2304 itr 2304 fw 2304 ow 1152 tt 1152 o2 1152 tw 2304"),
+        ("mx", "ef 1024 ob 128 zr 512 cn 256 rc 256 rq 200 u 128 v 128 up 256 w 512 wl 1024 x 288 ml 992 mc 512 mf 576 tb 144 ta0 144 ta1 144 ta2 144 lc0 144 lc1 144 lc2 144")):
     _s = _s.split()
     for _n, _w in zip(_s[::2], _s[1::2]):
         if _t == "mx":
@@ -26,7 +31,7 @@ for _t, _s in (
 for _m in range(8):
     SCRATCH["p%d" % _m] = ("psum", [128, 512], "float32")
 
-SEMAPHORES = "sv sa st sg lx lu lw ls lv z0 z1 z2 z3 z4 z5 z6 outd arr0 arr1 arr2 sent0 sent1 sent2".split()
+SEMAPHORES = "sv sa st sg lx lu lw ls lv z0 z1 z2 z3 z4 z5 outd arr0 arr1 arr2 sent0 sent1 sent2".split()
 
 
 def rank_program(g, core, T, topo):
@@ -64,6 +69,8 @@ def rank_program(g, core, T, topo):
                             continue
                     elif not bank and ((kind == "r" and k2 == "r") or not clash(v, v2)):
                         continue
+                    if sem[0] == "z":
+                        val = total[sem]
                     need[sem] = max(need.get(sem, 0), val)
         kn = known[q]
         for sem, val in sorted(need.items(), key=lambda e: -e[1]):
@@ -119,17 +126,14 @@ def rank_program(g, core, T, topo):
     def fill(out, c):
         run("V", lambda: g.vector.memset(out[6], c), [], [out])
 
-    def sums(out, keep, a):
-        run("V", lambda: g.vector.tensor_tensor_scan(out[6], keep[6], a[6], 0.0, OP.mult, OP.add), [keep, a], [out])
+    def scan(out, pat, a, op0, op1):
+        run("V", lambda: g.vector.tensor_tensor_scan(out[6], pat[6], a[6], 0.0, op0, op1), [pat, a], [out])
 
     def fetch(out, win, off):
         run("S", lambda: g.scalar.activation(out[6], win[6].indirect(off[6]), ACT.Copy), [win, off], [out])
 
-    def gather2(out, c0, win, off, o0, n):
-        m = n // 2
-        a, e = view(out, c0, c0 + 16 * m), view(off, o0, o0 + m)
-        run("V", lambda: g.vector.tensor_copy(a[6], win[6].indirect(e[6])), [win, e], [a])
-        fetch(view(out, c0 + 16 * m, c0 + 16 * n), win, view(off, o0 + m, o0 + n))
+    def vfetch(out, win, off):
+        run("V", lambda: g.vector.tensor_copy(out[6], win[6].indirect(off[6])), [win, off], [out])
 
     def fused(out, win, off, b, op):
         run("V", lambda: g.vector.tensor_tensor(out[6], win[6].indirect(off[6]), b[6], op), [win, off, b], [out])
@@ -144,21 +148,24 @@ def rank_program(g, core, T, topo):
         o, p = view(n + "_q", c0, c1), view(n + "_s", c0, c1)
         run("V", lambda: g.vector.quantize_mx(o[6], p[6], a[6]), [a], [o, p])
 
-    def act(out, a, f=ACT.Copy, scale=1.0, bias=0.0):
-        if isinstance(scale, tuple):
-            run("S", lambda: g.scalar.activation(out[6], a[6], f, scale=scale[6]), [a, scale], [out])
-        elif bias:
-            run("S", lambda: g.scalar.activation(out[6], a[6], ACT.Identity, bias=bias, scale=scale), [a], [out])
-        elif scale == 1.0:
-            run("S", lambda: g.scalar.activation(out[6], a[6], f), [a], [out])
-        else:
-            run("S", lambda: g.scalar.activation(out[6], a[6], f, scale=scale), [a], [out])
+    def act(out, a, f=ACT.Copy, scale=1.0, bias=0.0, acc=None):
+        kw = {}
+        if isinstance(scale, tuple) or scale != 1.0:
+            kw["scale"] = ap(scale)
+        if isinstance(bias, tuple) or bias != 0.0:
+            kw["bias"] = ap(bias)
+        if acc is not None:
+            kw["accum_out"] = acc[6]
+        run("S", lambda: g.scalar.activation(out[6], a[6], f, **kw), rd(a, scale, bias), rd(out, acc))
 
     def iota(out, pattern, base=0, cm=0, f=True):
         if f:
             run("G", lambda: g.iota(out[6], pattern, base, cm, allow_small_or_imprecise_dtypes=True), [], [out])
         else:
             run("G", lambda: g.iota(out[6], pattern, base, cm), [], [out])
+
+    def select(out, a, pattern, base):
+        run("G", lambda: g.affine_select(out[6], a[6], pattern, OP.is_equal, 0.0, base, 1), [a], [out])
 
     def mm(bank, n, l, l0, r, r0, start=True, stop=True):
         o = view("p%d" % bank, 0, n)
@@ -175,262 +182,286 @@ def rank_program(g, core, T, topo):
 
     for sem, name, src, w in (("lx", "xt", T.x, 1152), ("lu", "ut", T.u, 512)):
         dma(sem, T[name][:, 0:w], src[:], [], [view(name, 0, w)])
+    pf = [view("pf", k, k + 1) for k in range(9)]
+    kappa, group, quad, kmid, rest, rkc, basec, ec0, ec1 = pf
+    pi = [view("pi", k, k + 1) for k in range(4)]
+    iota(pi[3], [[0, 1]], 0, 1, f=False)
+    iota(view("ii", 0, 16), [[0, 2], [16, 8]], f=False)
+    iota(view("i16", 0, 288), [[0, 18], [1, 16]])
+    iota(view("gi", 0, 256), [[0, 2], [1, 8], [0, 16]])
+    iota(view("i17", 0, 289), [[0, 17], [1, 17]])
+    iota(view("sgr", 0, 8), [[1, 8]], 1)
+    iota(view("sgo", 0, 126), [[1, 7], [0, 18]], 1)
+
+    fill(view("zer", 0, 1024), 0.0)
+    fill(view("ones", 0, 256), 1.0)
+    fill(view("neg", 0, 768), EMPTY)
+    zer = view("zer", 0, 1024)
+    for k in range(2):
+        dma("z0", T.zr[:, 1024 * k:1024 * k + 1024], zer[6], [zer], [view("zr", 1024 * k, 1024 * k + 1024)])
+    for k in range(4):
+        dma("z1", T.ef[:, 1024 * k:1024 * k + 1024], zer[6], [zer], [view("ef", 1024 * k, 1024 * k + 1024)])
+    dma("z2", T.rq[:, 0:800], T.zer[:, 0:800], [zer], [view("rq", 0, 800)])
     dma("lw", T.w_q[:, 0:512].bitcast(dt.uint8), T.wc[:], [], [view("w_q", 0, 512)])
     dma("ls", T.w_s[:, 0:512], T.ws[:], [], [view("w_s", 0, 512)])
     dma("lv", T.vt[:, 0:512], T.v[:], [], [view("vt", 0, 512)])
-    pf = [view("pf", k, k + 1) for k in range(11)]
-    kappa, group, parity, kap4 = pf[1], pf[2], pf[3], pf[5]
-    pi = [view("pi", k, k + 1) for k in range(8)]
-    iota(pi[0], [[0, 1]], 0, 1, f=False)
-    iota(view("ii", 0, 8), [[16, 8]], f=False)
-    iota(view("ii", 8, 72), [[16, 8], [0, 8]], f=False)
-    iota(view("it0", 0, 288), [[0, 18], [1, 16]])
-    iota(view("it1", 144, 152), [[1, 8]])
-    iota(view("ii", 72, 90), [[16, 18]], 15, 0, f=False)
-    iota(view("it1", 0, 144), [[1, 8], [0, 18]])
-    iota(view("it2", 0, 289), [[0, 17], [1, 17]])
-    iota(view("cvf", 0, 288), [[1, 288]], -144, 0)
-    iota(view("it1", 160, 304), [[0, 36], [1, 4]])
-    iota(view("ii", 96, 160), [[16, 8], [128, 4], [0, 2]], f=False)
-
-    fill(view("zer", 0, 2304), 0.0)
-    for sem, name, c0, c1 in (("z0", "ef", 0, 2304), ("z1", "ef", 2304, 4096), ("z5", "zb", 0, 1024), ("z6", "zz", 0, 1792), ("z2", "iw0", 0, 2304), ("z3", "iw1", 0, 2304), ("z4", "iw2", 0, 2304)):
-        dma(sem, T[name][:, c0:c1], T.zer[:, 0:c1 - c0], [view("zer", 0, c1 - c0)], [view(name, c0, c1)])
-    fill(view("ones", 0, 64), 1.0)
-    fill(view("rs", 0, 1), 0.0)
-    act(view("ml", 0, 512), view("zer", 0, 512))
-    act(view("ml", 1152, 1664), view("zer", 0, 512))
-    for al, b, c, w in ((2, 0, 144, 192), (2, 1, 160, 192), (2, 2, 176, 192), (3, 0, 208, 256), (3, 1, 224, 256), (3, 2, 240, 256), (4, 0, 272, 288), (4, 3, 0, 288)):
-        act(view("ml", 1152 * al + 4 * c + b, 1152 * al + 4 * w, 4), view("zer", 0, w - c))
-    tc(view("ul", 0, 72), view("ii", 0, 72))
-    ts(pi[1], pi[0], 15, OP.bitwise_and)
-    ts(pi[2], pi[0], 4, OP.logical_shift_right)
-    ts(pi[3], pi[0], 4, OP.logical_shift_right, 1, OP.bitwise_and)
-    ts(pi[4], pi[0], 5, OP.logical_shift_right)
-    ts(pi[5], pi[0], 15, OP.bitwise_and, 2, OP.logical_shift_right)
-    ts(pi[6], pi[0], 4, OP.bitwise_and, 2, OP.logical_shift_right)
-    tc(view("pf", 0, 7), view("pi", 0, 7))
-    act(pf[7], pf[4], ACT.Identity, 576.0, 144.0)
-    act(pf[8], pf[4], ACT.Identity, 576.0, 432.0)
-    act(pf[9], pf[6], ACT.Copy, 4096.0)
-    act(pf[10], pf[6], ACT.Identity, -4096.0, 4096.0)
-    ts(view("mk16", 0, 288), view("it0", 0, 288), kappa, OP.is_equal)
-    ts(view("kp16", 0, 288), view("it0", 0, 288), 0.0, OP.not_equal)
-    ts(view("gm", 0, 8), view("it1", 144, 152), group, OP.is_equal)
+    for r in range(3):
+        for k in range(3):
+            dma("z%d" % (3 + r), T["iw%d" % r][:, 768 * k:768 * k + 768], T.neg[:, 0:768], [view("neg", 0, 768)], [view("iw%d" % r, 768 * k, 768 * k + 768)])
+    select(view("idx", 0, 256), view("ones", 0, 256), [[0, 2], [-1, 128]], 0)
+    iota(view("cval", 0, 288), [[1, 288]], -144, 0)
+    iota(view("ii", 32, 96), [[16, 8], [128, 4], [0, 2]], f=False)
     for h in range(8):
         for t in range(4):
-            o, i = view("ef", 512 * h + 128 * t + t, 512 * h + 128 * t + 128, 4), view("ones", 0, 32)
-            run("G", lambda: g.affine_select(o[6], i[6], [[0, 2], [-1, 16]], OP.is_equal, 0.0, -16 * h, 1), [i], [o])
-    quant("u", view("ut", 0, 512), 0, 128)
-    pick("up", "u", 0, 128, 128, view("ul", 0, 8))
+            select(view("ef", 512 * h + 128 * t + t, 512 * h + 128 * t + 128, 4), view("ones", 0, 32), [[0, 2], [-1, 16]], -16 * h)
 
-    def constants_0():
-        ts(view("bigm", 0, 288), view("it0", 0, 288), kappa, OP.is_le, BIG, OP.mult)
-        tc(view("clist", 0, 18), view("ii", 72, 90))
+    fill(view("rs", 0, 1), 0.0)
+    fill(view("wn", 0, 48), 0.0)
+    for k, c in enumerate((0.0, -31.0 / 32.0, 32.0)):
+        fill(view("hpat", k, 54, 3), c)
+    tc(view("ul", 0, 16), view("ii", 0, 16))
+    ts(pi[0], pi[3], 15, OP.bitwise_and)
+    ts(pi[1], pi[3], 4, OP.logical_shift_right)
+    ts(pi[2], pi[3], 5, OP.logical_shift_right)
+    tc(view("pf", 0, 3), view("pi", 0, 3))
+    act(view("ml", 0, 1024), zer)
+    for a in range(8, 17):
+        w0, w1 = ML[a // 4], ML[a // 4 + 1]
+        if w0 + 16 * a + 16 < w1:
+            act(view("ml", 4 * (w0 + 16 * a + 16) + a % 4, 4 * w1, 4), view("zer", 0, w1 - w0 - 16 * a - 16))
+    act(view("ml", 4 * ML[4] + 3, 4 * ML[5], 4), view("zer", 0, 288))
+    act(kmid, kappa, ACT.Identity, 2.0 ** 17, 2.0 ** 16)
+    act(view("i16s", 0, 288), view("i16", 0, 288), ACT.Copy, 2.0 ** 17)
+    quant("u", view("ut", 0, 512), 0, 128)
+    pick("up", "u", 0, 256, 128, view("ul", 0, 16))
+    ts(view("pata", 0, 288), view("i16", 0, 288), kappa, OP.not_equal, BIG, OP.mult)
+    ts(view("patb", 0, 288), view("i16s", 0, 288), kmid, OP.subtract, -1.0e22, OP.mult)
+    ts(view("gx", 0, 256), view("gi", 0, 256), group, OP.is_equal)
+    for t in range(4):
+        act(view("ob", t, 512, 4), view("gx", 0, 128))
+    act(rest, group, ACT.Identity, -1.0, 8.0)
+    act(rkc, kappa, ACT.Identity, STEP, -15 * STEP - 1)
+    act(basec, kappa, ACT.Identity, 2 * STEP, -30 * STEP - 1.5)
+    act(ec0, quad, ACT.Identity, 576.0, 144.0)
+    act(ec1, quad, ACT.Identity, 576.0, 432.0)
 
     def constants_1():
-        pick("up", "u", 128, 1152, 128, view("ul", 8, 72))
-        for k in range(8):
-            act(view("ob", 64 * k, 64 * k + 64), view("ones", 0, 64), ACT.Copy, view("gm", k, k + 1))
-        quant("ob", view("ob", 0, 512), 0, 128)
         for z in range(4):
-            for b in range(4):
-                act(view("zb", 512 * (z // 2) + 16 * z + 5 * b, 512 * (z // 2) + 512, 64), view("gm", 0, 8))
+            act(view("mc", 512 * z + 504, 512 * z + 512), view("zer", 0, 8))
+            for t in range(4):
+                act(view("zr", 516 * z + 17 * t, 512 * z + 512, 64), view("gx", 0, 128, 16))
+        quant("ob", view("ob", 0, 512), 0, 128)
 
     def constants_2():
-        for w in range(2):
-            for b in range(4):
-                act(view("zz", 896 * w + 384 + 5 * b, 896 * w + 512, 16), view("ones", 0, 8), ACT.Copy, 16.0 if w else 1.0)
-        act(view("cval", 0, 288), view("cvf", 0, 288))
-        ts(view("neg8", 0, 8), view("it1", 144, 152), group, OP.is_lt, -1.0, OP.mult)
-        ts(view("own8", 0, 8), view("it1", 144, 152), group, OP.is_equal, -BIG, OP.mult)
-        ts(view("offadd", 0, 144), view("it1", 0, 144), group, OP.is_lt, 24.0, OP.mult)
-        ts(view("offt", 0, 144), view("it1", 0, 144), group, OP.is_equal, 48.0, OP.mult)
-        ts(view("kp17", 0, 288), view("it2", 0, 288), 0.0, OP.not_equal)
-        tt(view("offadd", 0, 144), view("offadd", 0, 144), view("offt", 0, 144), OP.add)
-        ts(view("kp4", 0, 144), view("it1", 160, 304), 0.0, OP.not_equal)
-        ts(view("offe", 0, 144), view("offadd", 0, 144), pf[9], OP.subtract)
-        ts(view("offo", 0, 144), view("offadd", 0, 144), pf[10], OP.subtract)
-        ts(view("mk17", 0, 288), view("it2", 0, 288), kappa, OP.is_equal)
-        fill(view("wn", 0, 48), 0.0)
-        fill(view("wn", 48, 72), -BIG)
-        ts(view("msel", 0, 144), view("it1", 160, 304), kap4, OP.is_equal)
-        ts(view("mselt", 0, 144), view("msel", 0, 144), parity, OP.mult)
-        quant("ef", view("ef", 0, 2048), 0, 512)
-        tt(view("mselt", 0, 72), view("msel", 0, 72), view("mselt", 0, 72), OP.subtract)
-        quant("ef", view("ef", 2048, 4096), 512, 1024)
-        quant("zb", view("zb", 0, 1024), 0, 256)
-        quant("zz", view("zz", 0, 1792), 0, 448)
-        fill(view("cval", 144, 145), 0.25)
+        ts(view("patr", 0, 288), view("i16s", 0, 288), kmid, OP.subtract, STEP, OP.min)
+        ts(view("pats", 0, 288), view("i17", 0, 288), kappa, OP.is_equal, -BIG, OP.mult)
+        ts(view("cst", 0, 4), view("sgr", 0, 4), rest, OP.is_ge, -1.0, OP.mult)
+        ts(view("cst", 4, 8), view("sgr", 4, 8), rest, OP.is_lt)
+        ts(view("offadd", 0, 126), view("sgo", 0, 126), rest, OP.is_ge, 24.0, OP.mult)
+        quant("zr", view("zr", 0, 2048), 0, 512)
 
     def constants_3():
-        ts(view("ii", 160, 224), view("ii", 96, 160), kappa, OP.add)
-        tc(view("wl", 0, 64), view("ii", 160, 224))
+        for i in range(8):
+            for name, src in (("cn", "gx"), ("rc", "idx")):
+                o = view(name, 512 * (i // 4) + i % 4, 512 * (i // 4) + 512, 4)
+                act(o, view(src, 112 - 16 * i, 240 - 16 * i) if i < 7 else view("zer", 0, 128))
+        act(view("mf", 1152 + 3, 2304, 4), view("zer", 0, 288))
+
+    def constants_4():
+        quant("cn", view("cn", 0, 1024), 0, 256)
+        quant("rc", view("rc", 0, 1024), 0, 256)
+
+    def constants_5():
+        quant("ef", view("ef", 0, 2048), 0, 512)
+        quant("ef", view("ef", 2048, 4096), 512, 1024)
+
+    def constants_6():
+        ts(view("wl", 0, 64), view("ii", 32, 96), kappa, OP.add)
         pick("wl", "w", 0, 1024, 512, view("wl", 0, 64))
         quant("v", view("vt", 0, 512), 0, 128)
 
+    def unpack(h, bank):
+        mm(bank, C, "ef", 128 * h, "x", 0)
+
+    def keep(h, bank):
+        act(view("fw", 288 * h, 288 * h + 288), ps(bank, 0, 288))
+
     def places(rnd):
+        early = 3 if rnd else 0
         mm(0, C, "up", 0, "x", 0)
-        if rnd == 0:
-            constants_0()
-        tt(view("dm", 0, 288), ps(0, 0, 288), view("mk16", 0, 288), OP.mult)
-        tc(view("ssb", 0, 288), ps(0, 0, 288))
-        sums(view("sc", 0, 288), view("kp16", 0, 288), view("dm", 0, 288))
-        tt(view("sst", 0, 288), ps(0, 0, 288), view("bigm", 0, 288), OP.add)
+        mm(1, C, "up", 0, "x", 0)
+        own_ = ps(0, 0, 288)
+        tt(view("dm", 0, 288), own_, view("pata", 0, 288), OP.add)
+        act(view("ssb", 0, 288), ps(1, 0, 288))
+        scan(view("sc", 0, 288), view("patb", 0, 288), view("dm", 0, 288), OP.max, OP.min)
+        for h in range(early):
+            unpack(h, 5 + h)
+        for i in range(3):
+            mm(SB[i], C, "up", 16 * (i + 1), "x", 0)
         if rnd == 0:
             constants_1()
 
-        def sr_rows(ks):
-            for k in ks:
-                act(view("sr", 288 * k, 288 * k + 288), ps(2 + k % 4, 0, 288))
+        def slot(a, c0, c1):
+            return view("ml", 4 * (ML[a // 4] + c0) + a % 4, 4 * (ML[a // 4] + c1), 4)
 
-        for k in range(4):
-            mm(2 + k % 4, C, "up", 128 + 128 * k, "x", 0)
-        sr_rows(range(4))
-        for k in range(4, 8):
-            mm(2 + k % 4, C, "up", 128 + 128 * k, "x", 0)
-        for al in (4, 3, 2, 1, 0):
-            w = C if al == 4 else max(128, 64 * al + 64)
-            aa = range(4 * al, min(18, 4 * al + 4))
-            for a in aa:
-                ts(view("ml", 1152 * al + a % 4, 1152 * al + 64 * a + 64, 4), view("ssb", 0, 16 * a + 16), view("sc", 16 * a + 15, 16 * a + 16), OP.is_lt)
-            if al == 4:
-                fused(view("ml", 4 * 1152 + 2, 5760, 4), view("sc", 0, 288), view("clist", 0, 18), view("sst", 0, 288), OP.is_equal)
-            quant("ml", view("ml", 1152 * al, 1152 * al + 4 * w), 288 * al, 288 * al + w)
-            mm(1, w, "ob", 0, "ml", 288 * al, al == 4, al == 0)
-            for a in aa:
-                if a:
-                    i, o, acc = view("ml", 1152 * al + a % 4, 1152 * al + 64 * a, 4), view("dump", 288 * (a % 4), 288 * (a % 4) + 16 * a), view("rs", a, a + 1)
-                    run("S", lambda: g.scalar.activation(o[6], i[6], ACT.Identity, bias=1.0, scale=-1.0, accum_out=acc[6]), [i], [o, acc])
-        sr_rows(range(4, 8))
+        def scal(a):
+            return view("sc", 16 * a + 15, 16 * a + 16)
+
+        for k, a in enumerate(BY_SCALAR):
+            d = 288 * k
+            act(view("dump", d, d + 16 * a + 16), view("ssb", 0, 16 * a + 16), ACT.Sign, -1.0, scal(a))
+            act(slot(a, 0, 16 * a), view("dump", d, d + 16 * a), ACT.Relu, acc=view("rs", a, a + 1))
+            act(slot(a, 16 * a, 16 * a + 16), view("dump", d + 16 * a, d + 16 * a + 16), ACT.Relu)
+        tt(view("ml", 4 * ML[4] + 2, 4 * ML[5], 4), own_, view("sc", 0, 288), OP.is_equal)
+        order = (2, 1, 0, 4, 3)
+        for n, al in enumerate(order):
+            for a in range(4 * al, min(18, 4 * al + 4)):
+                if a not in BY_SCALAR:
+                    ts(slot(a, 0, 16 * a + 16), ps(0, 0, 16 * a + 16), scal(a), OP.is_lt)
+            quant("ml", view("ml", 4 * ML[al], 4 * ML[al + 1]), ML[al], ML[al + 1])
+            if n == 0:
+                for a in BY_SCALAR:
+                    act(view("rs", a, a + 1), view("rs", a, a + 1), ACT.Identity, -1.0, 16.0 * a)
+            for a in range(4 * al, min(18, 4 * al + 4)):
+                if a and a not in BY_SCALAR:
+                    act(view("dump", 288 * (a % 3), 288 * (a % 3) + 16 * a), slot(a, 0, 16 * a), ACT.Identity, -1.0, 1.0, acc=view("rs", a, a + 1))
+        for n, al in enumerate((4, 2, 1, 0, 3)):
+            mm(1, ML[al + 1] - ML[al], "ob", 0, "ml", ML[al], n == 0, n == 4)
         if rnd == 0:
             constants_2()
-        for k in range(8):
-            mm(2 + k % 4, C, "ef", 128 * k, "x", 0)
-            act(view("fw", 288 * k, 288 * k + 288), ps(2 + k % 4, 0, 288))
-        for k, gr in enumerate((2, 3, 6, 7)):
-            mm(2 + k, C, "up", 128 + 128 * gr, "x", 0)
-        tt(view("dm", 0, 288), ps(1, 0, 288), view("mk16", 0, 288), OP.mult)
-        sums(view("wm", 0, 288), view("kp16", 0, 288), view("dm", 0, 288))
+        mm(SB[3], C, "up", 64, "x", 0)
+        for h in range(early):
+            keep(h, 5 + h)
+        for i in range(4, 7):
+            mm(SB[i], C, "up", 16 * (i + 1), "x", 0)
+        if rnd == 0:
+            constants_3()
+        act(view("s7", 0, 288), ps(SB[6], 0, 288))
+        scan(view("scn", 0, 288), view("patr", 0, 288), ps(1, 0, 288), OP.add, OP.max)
         rk = view("rk", 0, 18)
-        tt(rk, view("wm", 15, 288, 16), view("rs", 0, 18), OP.add)
-        tc(view("posl", 0, 18), rk)
+        tt(rk, view("scn", 15, 288, 16), view("rs", 0, 18), OP.add)
+        ts(view("posl", 0, 18), rk, rkc, OP.add)
         scatter(view("sort", 0, 288), view("posl", 0, 18), view("ssb", 0, 288))
-        sm = view("spm", 0, 16)
-        tt(sm, view("sort", 16, 288, 17), view("mk16", 0, 16), OP.mult)
-        sp, spa, dec = view("spv", 0, 1), view("spv", 1, 2), view("spv", 2, 3)
-        run("V", lambda: g.vector.tensor_reduce(spa[6], sm[6], AxisListType.X, OP.add, apply_absolute_value=True), [sm], [spa])
-        run("V", lambda: g.vector.tensor_reduce(sp[6], sm[6], AxisListType.X, OP.add), [sm], [sp])
-        ts(dec, spa, EPS, OP.mult, DELTA, OP.add)
-        ts(view("sp8", 0, 8), view("neg8", 0, 8), dec, OP.mult, sp, OP.add)
-        tt(view("sp8", 8, 16), view("sp8", 0, 8), view("own8", 0, 8), OP.add)
-        ts(view("sp8", 16, 24), view("sp8", 8, 16), dec, OP.add)
-        v = view("wr", 15, 288, 17)
-        runs = [lambda: tt(view("wm", 0, 288), view("sort", 0, 288), view("mk17", 0, 288), OP.mult),
-                lambda: sums(view("wr", 0, 288), view("kp17", 0, 288), view("wm", 0, 288)),
-                lambda: [ts(view("wt", 0, 17), v, EPS, OP.mult, -DELTA, OP.add), ts(view("wt", 24, 41), v, -EPS, OP.mult, -DELTA, OP.add)],
-                lambda: tc(view("wn", 0, 17), v),
-                lambda: tt(view("wt", 48, 65), view("wt", 0, 17), view("wt", 24, 41), OP.min),
-                lambda: tt(view("wn", 24, 41), v, view("wt", 48, 65), OP.add)]
-        for gr in range(8):
-            o, i = view("mc", 288 * gr, 288 * gr + 288), view("sr", 288 * gr, 288 * gr + 288)
-            if gr % 4 >= 2:
-                s, b = view("dump", 288 * (gr % 4), 288 * (gr % 4) + 288), view("sp8", 16 + gr, 17 + gr)
-                run("S", lambda: g.scalar.activation(s[6], i[6], ACT.Sign, bias=b[6], scale=-1.0), [i, b], [s])
-                act(o, s, ACT.Relu)
-            else:
-                ts(o, i, view("sp8", 8 + gr, 9 + gr), OP.is_le)
-            if gr < 6:
-                runs[gr]()
-            if gr % 4 == 3:
-                hf = gr // 4
-                quant("mc", view("mc", 1152 * hf, 1152 * hf + 1152), 288 * hf, 288 * hf + 288)
-                for z in range(2):
-                    mm(6 + hf, 286, "zb", 128 * z, "mc", 288 * hf + 2 * z, z == 0, z == 1)
-        for k in range(4):
-            for w in range(2):
-                mm(1, H, "zz", 224 * w + 96 - 32 * k, "mc", 144 * k, k == 0 and w == 0, False)
-        for hf in range(2):
-            c0, c1 = 72 * hf, 72 * hf + 72
-            o, o2 = view("off32", c0, c1), view("off33", c0, c1)
-            tt(o, ps(6 + hf, 0, 286, 4), view("offe", c0, c1), OP.add)
-            tt(o2, ps(6 + hf, 1, 286, 4), view("offo", c0, c1), OP.add)
-            tt(o, o, o2, OP.max)
-            tc(view("off", c0, c1), o)
-            w = view("wn", 0, 72)
-            fetch(view("rt", 576 * hf, 576 * hf + 576), w, view("off", c0 + 36, c1))
-            for k in (2 * hf, 2 * hf + 1):
-                m = view("mf", 576 * k, 576 * k + 576)
-                if k % 2 == 0:
-                    fused(m, w, view("off", 36 * k, 36 * k + 36), view("sr", 576 * k, 576 * k + 576), OP.is_ge)
-                else:
-                    for e in range(2):
-                        c = 576 * hf + 288 * e
-                        tt(view("mf", 576 * k + 288 * e, 576 * k + 288 * e + 288), view("rt", c, c + 288), ps(2 + 2 * hf + e, 0, 288), OP.is_ge)
-                quant("mf", m, 144 * k, 144 * k + 144)
-                mm(1, H, "zz", 96 - 32 * k, "mf", 144 * k, False, k == 3)
-        tt(view("wm", 0, 144), ps(1, 0, 144), view("mselt", 0, 144), OP.mult)
-        sums(view("nc", 0, 144), view("kp4", 0, 144), view("wm", 0, 144))
-        tt(view("pof", 0, 18), view("nc", 3, 72, 4), view("nc", 75, 144, 4), OP.add)
-        tt(view("nt", 0, 18), view("pof", 0, 18), rk, OP.add)
+        scan(view("wr", 289, 305), view("pats", 0, 16), view("sort", 16, 288, 17), OP.add, OP.max)
+        sp, runs = view("wr", 304, 305), view("wr", 15, 288, 17)
+        act(view("dec", 17, 18), sp, ACT.Abs, EPS, DELTA)
+        scan(view("wr", 0, 288), view("pats", 0, 288), view("sort", 0, 288), OP.add, OP.max)
+        ts(view("sp8", 0, 8), view("cst", 0, 8), view("dec", 17, 18), OP.mult, sp, OP.add)
+        for z in range(4):
+            for i in range(4):
+                ts(view("mc", 512 * z + 72 * i, 512 * z + 72 * i + 72), ps(SB[i], z, 288, 4), view("sp8", i, i + 1), OP.is_le)
+            d = 216 * z
+            for i in range(4, 7):
+                act(view("dump", d + 72 * (i - 4), d + 72 * (i - 3)), ps(SB[i], z, 288, 4), ACT.Sign, -1.0, view("sp8", i, i + 1))
+            act(view("mc", 512 * z + 288, 512 * z + 504), view("dump", d, d + 216), ACT.Relu)
+            if z == 3:
+                act(view("dec", 0, 17), runs, ACT.Abs, EPS, DELTA)
+                act(view("wn", 0, 17), runs)
+            for y in ([z - 1] if 0 < z < 3 else [2, 3] if z else []):
+                quant("mc", view("mc", 512 * y, 512 * y + 512), 128 * y, 128 * y + 128)
+                mm(1, 128, "zr", 128 * y, "mc", 128 * y, y == 0, y == 3)
+        tt(view("wn", 24, 41), runs, view("dec", 0, 17), OP.subtract)
+        if rnd == 0:
+            constants_4()
+        tt(view("off32", 0, 126), ps(1, 0, 126), view("offadd", 0, 126), OP.add)
+        tc(view("off", 0, 126), view("off32", 0, 126))
+        wn = view("wn", 0, 48)
+
+        def cmp(i):
+            return view("mf", 1152 * (i // 4) + i % 4, 1152 * (i // 4) + 1152, 4)
+
+        fused(cmp(6), wn, view("off", 108, 126), view("s7", 0, 288), OP.is_ge)
+        for i in range(6):
+            r = view("rt", 288 * i, 288 * i + 288)
+            fetch(r, wn, view("off", 18 * i, 18 * i + 18))
+            if i == 1:
+                for t in range(4):
+                    w = 90 if t < 3 else 18
+                    act(view("rq", t, 4 * w, 4), ps(1, 18 * t, 18 * t + w))
+            tt(cmp(i), r, ps(SB[i], 0, 288), OP.is_ge)
+            if i == 2:
+                quant("rq", view("rq", 0, 800), 0, 200)
+                for k in range(2):
+                    mm(1, 128, "rc", 128 * k, "rq", 72 * k, k == 0, k == 1)
+            if i == 3:
+                quant("mf", view("mf", 0, 1152), 0, 288)
+                mm(2, C, "cn", 0, "mf", 0, True, False)
+                ts(view("base", 0, 18), ps(1, 0, 18), 17.0, OP.mult, basec, OP.add)
+            if i == 4:
+                tt(view("base", 24, 42), view("base", 0, 18), rk, OP.add)
+        quant("mf", view("mf", 1152, 2304), 288, 576)
+        mm(2, C, "cn", 128, "mf", 288, False, True)
+        ts(view("base", 48, 66), view("base", 24, 42), -15.0, OP.add)
+        if rnd == 0:
+            constants_5()
+        for h in range(early, 8):
+            unpack(h, 3 + h % 5)
+            keep(h, 3 + h % 5)
+        scan(view("scn", 0, 288), view("patr", 0, 288), ps(2, 0, 288), OP.add, OP.max)
 
     def seats(rnd):
-        n = view("nt", 0, 18)
-        ph = [view("ph", 18 * k, 18 * k + 18) for k in range(5)]
-        ts(ph[0], n, 1, OP.logical_shift_right)
-        ts(ph[1], n, 1, OP.logical_shift_right, 65520, OP.bitwise_and)
-        ts(ph[2], n, 16, OP.mult)
-        ts(ph[3], ph[0], -31, OP.mult)
-        tt(ph[2], ph[2], ph[1], OP.add)
-        tt(ph[4], ph[2], ph[3], OP.add)
-        tc(view("phl", 0, 18), ph[4])
+        cnt = view("scn", 15, 288, 16)
+        hb = [view("hb", k, 54, 3) for k in range(3)]
+        tt(hb[1], cnt, view("base", 24, 42), OP.add)
+        tt(view("n2", 0, 18), cnt, view("base", 48, 66), OP.add)
+        ts(hb[0], hb[1], 1.5 * 2.0 ** 24, OP.add, -1.5 * 2.0 ** 24, OP.add)
+        ts(hb[2], view("n2", 0, 18), 1.5 * 2.0 ** 28, OP.add, -1.5 * 2.0 ** 28, OP.add)
+        scan(view("hs", 0, 54), view("hpat", 0, 54), view("hb", 0, 54), OP.mult, OP.add)
+        ts(view("phl", 0, 18), view("hs", 2, 54, 3), 0.5, OP.mult, 8.0, OP.add)
         iw = view("iw%d" % rnd, 0, 2304)
         scatter(iw, view("phl", 0, 18), view("cval", 0, 288))
         turn(view("itr", 0, 2304), iw)
         e = [(72 * k, 72 * k + 72) for k in range(7)]
-        i0, i1 = view("itr", 0, 2304, 32), view("itr", 16, 2304, 32)
-        ts(view("en", *e[0]), i0, 0.0, OP.not_equal, pf[7], OP.mult)
-        ts(view("en", *e[1]), i1, 0.0, OP.not_equal, pf[8], OP.mult)
-        tt(view("en", *e[2]), view("en", *e[0]), i0, OP.add)
-        tt(view("en", *e[3]), view("en", *e[1]), i1, OP.add)
-        tt(view("en", *e[4]), view("en", *e[2]), view("en", *e[3]), OP.add)
-        tc(view("en", *e[5], p1=64), view("en", *e[4], p0=64))
-        tt(view("en", *e[6], p1=64), view("en", *e[4], p1=64), view("en", *e[5], p1=64), OP.add)
-        tc(view("en", *e[0], p1=32), view("en", *e[6], p0=32, p1=64))
-        tt(view("en", *e[1], p1=32), view("en", *e[6], p1=32), view("en", *e[0], p1=32), OP.add)
+        ts(view("en", *e[0]), view("itr", 0, 2304, 32), ec0, OP.add)
+        ts(view("en", *e[1]), view("itr", 16, 2304, 32), ec1, OP.add)
+        tt(view("en", *e[2]), view("en", *e[0]), view("en", *e[1]), OP.max)
+        tc(view("en", *e[3], p1=64), view("en", *e[2], p0=64))
+        tt(view("en", *e[4], p1=64), view("en", *e[2], p1=64), view("en", *e[3], p1=64), OP.max)
+        tc(view("en", *e[5], p1=32), view("en", *e[4], p0=32, p1=64))
+        tt(view("en", *e[6], p1=32), view("en", *e[4], p1=32), view("en", *e[5], p1=32), OP.max)
         for t in range(4):
-            tc(view("tl", 0, 72, p0=32 * t, p1=32 * t + 32), view("en", *e[1], p1=32))
+            tc(view("tl", 0, 72, p0=32 * t, p1=32 * t + 32), view("en", *e[6], p1=32))
 
-    def native(dst, dc, src, sc, n, sst, order):
-        for k, (q, t) in enumerate(order):
-            o = view(dst, dc + t, dc + 4 * n, 4, 32 * q, 32 * q + 32)
-            if sst == 1:
-                i = view(src, sc + n * q, sc + n * q + n, 1, 32 * t, 32 * t + 32)
-            else:
-                i = view(src, sc + q, sc + 4 * n, 4, 32 * t, 32 * t + 32)
-            if k % 8 in (2, 5, 6):
-                act(o, i)
-            else:
-                tc(o, i)
+    def move(q, o, i):
+        if q == "S":
+            act(o, i)
+        else:
+            tc(o, i)
 
-    ALL = [(q, t) for q in range(4) for t in range(4)]
+    def half(k):
+        c0, win = 576 * k, view("fw", 0, 2304)
+        vfetch(view("ow", c0, c0 + 288), win, view("tl", 36 * k, 36 * k + 18))
+        fetch(view("ow", c0 + 288, c0 + 576), win, view("tl", 36 * k + 18, 36 * k + 36))
+        for n in range(16):
+            q, t = n // 4, n % 4
+            move("S" if n % 3 == 1 else "V", view("tt", c0 + t, c0 + 576, 4, 32 * q, 32 * q + 32), view("ow", c0 + q, c0 + 576, 4, 32 * t, 32 * t + 32))
 
-    def layer(src, half):
+    def layer(src, hf, between=()):
         for h in range(8):
             a, b = (2 * h) % 8, (2 * h + 1) % 8
             mm(a, H, "wl", 128 * h, src, 0)
             mm(b, H, "ef", 128 * h, src, 0)
-            r = view("rt", 144 * h, 144 * h + 144)
+            r = view("rl", 144 * h, 144 * h + 144)
             act(r, ps(a, 0, 144), ACT.Relu, 0.03125)
-            tt(view("tw", 1152 * half + h, 1152 * half + 1152, 8), ps(b, 0, 144), r, OP.add)
+            tt(view("tw", 1152 * hf + h, 1152 * hf + 1152, 8), ps(b, 0, 144), r, OP.add)
+            if h < len(between):
+                between[h]()
+
+    def home():
+        win = view("tw", 0, 2304)
+        vfetch(view("o2", 0, 288), win, view("hl", 0, 18))
+        for q in range(1, 4):
+            fetch(view("o2", 288 * q, 288 * q + 288), win, view("hl", 18 * q, 18 * q + 18))
+        for n in range(16):
+            q, t = n // 4, n % 4
+            move("S" if n > 12 else "V", view("xt", t, 1152, 4, 32 * q, 32 * q + 32), view("o2", 288 * q, 288 * q + 288, 1, 32 * t, 32 * t + 32))
 
     for rnd in range(3):
         quant("x", view("xt", 0, 1152), 0, 288)
         places(rnd)
         seats(rnd)
         ta, lc = "ta%d" % rnd, "lc%d" % rnd
-        gather2("ow", 0, view("fw", 0, 2304), "tl", 0, 36)
-        native("tt", 0, "ow", 0, 144, 4, ALL)
+        half(0)
         quant(ta, view("tt", 0, 576), 0, 144)
         dst = T.cores[rank ^ MASKS[rnd]]
         rid, pid = topo.addr(dst)[0], topo.addr(dst)[1]
@@ -441,27 +472,23 @@ def rank_program(g, core, T, topo):
         g.remote_dma(T[lc + "_s"][:, 0:144], T[ta + "_s"][:, 0:144], T.sem[arr], T.sem[sent], pid, rid, mask)
         total[arr] = total[sent] = 2 * ne
         note("R", arr, 2 * ne, [], [view(lc + "_q", 0, 144), view(lc + "_s", 0, 144)])
-        gather2("ow", 576, view("fw", 0, 2304), "tl", 36, 36)
-        native("tt", 576, "ow", 576, 144, 4, ALL)
+        half(1)
         quant("tb", view("tt", 576, 1152), 0, 144)
         if rnd == 0:
-            constants_3()
-        for q in range(4):
-            tc(view("hl", 18 * q, 18 * q + 18, p1=32), view("nt", 0, 18, p0=32 * q, p1=32 * q + 32))
-        for t in range(1, 4):
-            tc(view("hl", 0, 72, p0=32 * t, p1=32 * t + 32), view("hl", 0, 72, p1=32))
-        layer("tb", 1)
+            constants_6()
+        lists = [lambda q=q: ts(view("hl", 18 * q, 18 * q + 18, p1=32), view("hb", 1, 54, 3, 32 * q, 32 * q + 32), 0.5, OP.add) for q in range(4)]
+        lists.append(lambda: tc(view("hl", 0, 72, p0=32, p1=64), view("hl", 0, 72, p1=32)))
+        lists.append(lambda: tc(view("hl", 0, 72, p0=64), view("hl", 0, 72, p1=64)))
+        layer("tb", 1, lists)
         if rnd == 2:
             fill(view("ntf", 18, 32), 0.0)
-            tc(view("ntf", 0, 18), view("nt", 0, 18))
+            ts(view("ntf", 0, 18), view("hb", 1, 54, 3), 0.5, OP.add)
             turn(view("ntt", 0, 32), view("ntf", 0, 32))
             for gr in range(8):
                 v = view("ntt", 16 * (gr % 2), 16 * (gr % 2) + 16, 1, 32 * (gr // 2), 32 * (gr // 2) + 18)
                 dma("outd", T.pl[gr:gr + 1, :], v[6], [v], [])
         layer(lc, 0)
-        for k in range(2):
-            gather2("o2", 576 * k, view("tw", 0, 2304), "hl", 36 * k, 36)
-            native("xt", 0, "o2", 0, 288, 1, ALL[8 * k:8 * k + 8])
+        home()
     quant("x", view("xt", 0, 1152), 0, 288)
     mm(0, C, "v", 0, "x", 0)
     v = view("x_q", 0, 288)

@@ -8,19 +8,22 @@ BIG = 1.0e29
 EPS = 2.0 ** -24 + 2.0 ** -32
 DELTA = 2.0 ** -120
 STEP = 4096.0
+LOW = 8192.0
 EMPTY = -32768.0
+CUT = 160
+LATE = 4
 MASKS = [1, 2, 3]
 ML = [0, 128, 256, 448, 704, 992]
-BY_SCALAR = (17, 16, 15)
+BY_SCALAR = (17, 16)
 SB = [2, 3, 4, 0, 5, 6, 7]
 
 SCRATCH = {}
 for _t, _s in (
-        ("float32", "pf 16 i16 288 i16s 288 i17 296 gi 256 sgr 8 sgo 128 pata 288 patb 288 patr 288 pats 288 cst 8 offadd 128 hpat 56 dm 288 sc 288 ssb 288 rs 24 rk 24 scn 288 sort 288 wr 312 dec 24 sp8 8 wn 48 off32 128 s7 288 rt 1728 base 72 hb 56 hs 56 n2 24 en 504 ntf 32 ntt 32 rl 1152"),
+        ("float32", "pf 16 i16 288 i16s 288 i17 296 gi 256 sgr 8 pata 288 patb 288 patr 288 patc 288 pats 288 pat8 288 cst 24 hpat 96 dm 288 sc 288 ssb 288 rs 24 scr 288 scn 288 sort 288 wr 312 dec 24 sp8 8 wn 48 s7 288 rt 1728 base 24 hb 96 hs 96 en 576 es 576 ntf 32 ntt 32 rl 2304"),
         ("int32", "pi 8 ii 96"),
-        ("uint16", "ul 16 wl 64 posl 18 off 128 phl 18 tl 72 hl 72"),
-        ("bfloat16", "dump 864 cval 288 ones 256 zer 1024 neg 768 gx 256 idx 256 ef 4096 ob 512 zr 2048 cn 1024 rc 1024 rq 800 xt 1152 ut 512 vt 512 ml 3968 mc 2048 mf 2304 iw0 2304 iw1 2304 iw2 2304 itr 2304 fw 2304 ow 1152 tt 1152 o2 1152 tw 2304"),
-        ("mx", "ef 1024 ob 128 zr 512 cn 256 rc 256 rq 200 u 128 v 128 up 256 w 512 wl 1024 x 288 ml 992 mc 512 mf 576 tb 144 ta0 144 ta1 144 ta2 144 lc0 144 lc1 144 lc2 144")):
+        ("uint16", "ul 16 wl 64 posl 18 off 128 phl 18 tl 36 hl 72 ls0 36 ls1 36 ls2 36 lp0 36 lp1 36 lp2 36"),
+        ("bfloat16", "dump 1728 cval 288 ones 256 zer 1024 neg 768 gx 256 idx 256 ef 4096 ob 512 zr 2048 cn 1024 rc 1024 rq 800 xt 1152 ut 512 vt 512 ml 3968 mc 2048 mf 2304 iw0 2304 iw1 2304 iw2 2304 itr 2304 fw 2304 fp 2304 ow 1152 tt 1152 o2 1152 tw 2304"),
+        ("mx", "ef 1024 ob 128 zr 512 cn 256 rc 256 rq 200 u 128 v 128 up 256 w 512 wl 1024 x 288 ml 1152 mc 512 mf 576 ta 144 tb 144 xp0 288 xp1 288 xp2 288")):
     _s = _s.split()
     for _n, _w in zip(_s[::2], _s[1::2]):
         if _t == "mx":
@@ -31,7 +34,7 @@ for _t, _s in (
 for _m in range(8):
     SCRATCH["p%d" % _m] = ("psum", [128, 512], "float32")
 
-SEMAPHORES = "sv sa st sg lx lu lw ls lv z0 z1 z2 z3 z4 z5 outd arr0 arr1 arr2 sent0 sent1 sent2".split()
+SEMAPHORES = "sv sa st sg lx ly lu lw ls lv z0 z1 z2 z3 z4 z5 outd arr0 arr1 arr2 sent0 sent1 sent2 larr0 larr1 larr2 lsent0 lsent1 lsent2".split()
 
 
 def rank_program(g, core, T, topo):
@@ -105,6 +108,18 @@ def rank_program(g, core, T, topo):
         g.sync.dma_start(out, in_).then_inc(T.sem[sem], 16)
         note("Y", sem, total[sem], reads, writes)
 
+    def send(rnd, arr, sent, pairs):
+        dst = T.cores[rank ^ MASKS[rnd]]
+        rid, pid = topo.addr(dst)[0], topo.addr(dst)[1]
+        mask, ne = topo.mask(core, dst), len(topo.engines(core, dst))
+        settle("G", [i for o, i in pairs], [])
+        for o, i in pairs:
+            codes = o[0].endswith("_q")
+            g.remote_dma(o[6].bitcast(dt.uint8) if codes else o[6], i[6].bitcast(dt.uint8) if codes else i[6], T.sem[arr], T.sem[sent], pid, rid, mask)
+        total[arr] = total[sent] = len(pairs) * ne
+        note("R", arr, total[arr], [], [o for o, i in pairs])
+        note("R", sent, total[sent], [i for o, i in pairs], [])
+
     def ap(x):
         return x[6] if isinstance(x, tuple) else x
 
@@ -126,8 +141,8 @@ def rank_program(g, core, T, topo):
     def fill(out, c):
         run("V", lambda: g.vector.memset(out[6], c), [], [out])
 
-    def scan(out, pat, a, op0, op1):
-        run("V", lambda: g.vector.tensor_tensor_scan(out[6], pat[6], a[6], 0.0, op0, op1), [pat, a], [out])
+    def scan(out, d0, d1, op0, op1):
+        run("V", lambda: g.vector.tensor_tensor_scan(out[6], d0[6], d1[6], 0.0, op0, op1), [d0, d1], [out])
 
     def fetch(out, win, off):
         run("S", lambda: g.scalar.activation(out[6], win[6].indirect(off[6]), ACT.Copy), [win, off], [out])
@@ -158,6 +173,12 @@ def rank_program(g, core, T, topo):
             kw["accum_out"] = acc[6]
         run("S", lambda: g.scalar.activation(out[6], a[6], f, **kw), rd(a, scale, bias), rd(out, acc))
 
+    def move(q, o, i):
+        if q == "S":
+            act(o, i)
+        else:
+            tc(o, i)
+
     def iota(out, pattern, base=0, cm=0, f=True):
         if f:
             run("G", lambda: g.iota(out[6], pattern, base, cm, allow_small_or_imprecise_dtypes=True), [], [out])
@@ -177,13 +198,13 @@ def rank_program(g, core, T, topo):
 
     def pick(dst, src, n0, n1, w, off):
         o, i, o2, i2 = view(dst + "_q", n0, n1), view(src + "_q", 0, w), view(dst + "_s", n0, n1), view(src + "_s", 0, w)
-        run("V", lambda: g.vector.tensor_copy(o[6].bitcast(dt.uint32), i[6].bitcast(dt.uint32).indirect(off[6])), [i, off], [o])
-        fetch(o2, i2, off)
+        return (lambda: run("V", lambda: g.vector.tensor_copy(o[6].bitcast(dt.uint32), i[6].bitcast(dt.uint32).indirect(off[6])), [i, off], [o]),
+                lambda: fetch(o2, i2, off))
 
-    for sem, name, src, w in (("lx", "xt", T.x, 1152), ("lu", "ut", T.u, 512)):
-        dma(sem, T[name][:, 0:w], src[:], [], [view(name, 0, w)])
+    for sem, name, src, c0, c1 in (("lu", "ut", T.u, 0, 512), ("lx", "xt", T.x, 0, 4 * CUT), ("ly", "xt", T.x, 4 * CUT, 1152)):
+        dma(sem, T[name][:, c0:c1], src[:, c0:c1], [], [view(name, c0, c1)])
     pf = [view("pf", k, k + 1) for k in range(9)]
-    kappa, group, quad, kmid, rest, rkc, basec, ec0, ec1 = pf
+    kappa, group, kmid, klow, rest, rkc, basec, over, base0 = pf
     pi = [view("pi", k, k + 1) for k in range(4)]
     iota(pi[3], [[0, 1]], 0, 1, f=False)
     iota(view("ii", 0, 16), [[0, 2], [16, 8]], f=False)
@@ -191,10 +212,13 @@ def rank_program(g, core, T, topo):
     iota(view("gi", 0, 256), [[0, 2], [1, 8], [0, 16]])
     iota(view("i17", 0, 289), [[0, 17], [1, 17]])
     iota(view("sgr", 0, 8), [[1, 8]], 1)
-    iota(view("sgo", 0, 126), [[1, 7], [0, 18]], 1)
 
     fill(view("zer", 0, 1024), 0.0)
+    ts(pi[0], pi[3], 15, OP.bitwise_and)
+    ts(pi[1], pi[3], 4, OP.logical_shift_right)
     fill(view("ones", 0, 256), 1.0)
+    tc(view("ul", 0, 16), view("ii", 0, 16))
+    tc(view("pf", 0, 2), view("pi", 0, 2))
     fill(view("neg", 0, 768), EMPTY)
     zer = view("zer", 0, 1024)
     for k in range(2):
@@ -208,164 +232,214 @@ def rank_program(g, core, T, topo):
     for r in range(3):
         for k in range(3):
             dma("z%d" % (3 + r), T["iw%d" % r][:, 768 * k:768 * k + 768], T.neg[:, 0:768], [view("neg", 0, 768)], [view("iw%d" % r, 768 * k, 768 * k + 768)])
+
+    def unpackers(hh):
+        for h in hh:
+            for t in range(4):
+                select(view("ef", 512 * h + 128 * t + t, 512 * h + 128 * t + 128, 4), view("ones", 0, 32), [[0, 2], [-1, 16]], -16 * h)
+
+    iota(view("ii", 32, 96), [[16, 8], [128, 4], [0, 2]], f=False)
     select(view("idx", 0, 256), view("ones", 0, 256), [[0, 2], [-1, 128]], 0)
     iota(view("cval", 0, 288), [[1, 288]], -144, 0)
-    iota(view("ii", 32, 96), [[16, 8], [128, 4], [0, 2]], f=False)
-    for h in range(8):
-        for t in range(4):
-            select(view("ef", 512 * h + 128 * t + t, 512 * h + 128 * t + 128, 4), view("ones", 0, 32), [[0, 2], [-1, 16]], -16 * h)
-
+    unpackers([0])
+    act(kmid, kappa, ACT.Identity, 2.0 ** 17, 2.0 ** 16)
+    act(klow, kappa, ACT.Identity, 2.0 ** 17, -2.0 ** 16)
+    act(rest, group, ACT.Identity, -1.0, 8.0)
+    act(view("i16s", 0, 288), view("i16", 0, 288), ACT.Copy, 2.0 ** 17)
+    act(view("ml", 0, 1024), zer)
+    ts(view("pata", 0, 288), view("i16", 0, 288), kappa, OP.not_equal, BIG, OP.mult)
     fill(view("rs", 0, 1), 0.0)
     fill(view("wn", 0, 48), 0.0)
-    for k, c in enumerate((0.0, -31.0 / 32.0, 32.0)):
-        fill(view("hpat", k, 54, 3), c)
-    tc(view("ul", 0, 16), view("ii", 0, 16))
-    ts(pi[0], pi[3], 15, OP.bitwise_and)
-    ts(pi[1], pi[3], 4, OP.logical_shift_right)
-    ts(pi[2], pi[3], 5, OP.logical_shift_right)
-    tc(view("pf", 0, 3), view("pi", 0, 3))
-    act(view("ml", 0, 1024), zer)
+    quant("ml", view("zer", 0, 640), 128, 288)
+    ts(view("patb", 0, 288), view("i16s", 0, 288), kmid, OP.subtract, -1.0e22, OP.mult)
+    ts(view("gx", 0, 256), view("gi", 0, 256), group, OP.is_equal)
+    quant("u", view("ut", 0, 512), 0, 128)
+    ts(view("patr", 0, 288), view("i16s", 0, 288), klow, OP.subtract, STEP, OP.min)
+    for f in pick("up", "u", 0, 256, 128, view("ul", 0, 16)):
+        f()
+    for t in range(4):
+        act(view("ob", t, 512, 4), view("gx", 0, 128))
     for a in range(8, 17):
         w0, w1 = ML[a // 4], ML[a // 4 + 1]
         if w0 + 16 * a + 16 < w1:
             act(view("ml", 4 * (w0 + 16 * a + 16) + a % 4, 4 * w1, 4), view("zer", 0, w1 - w0 - 16 * a - 16))
     act(view("ml", 4 * ML[4] + 3, 4 * ML[5], 4), view("zer", 0, 288))
-    act(kmid, kappa, ACT.Identity, 2.0 ** 17, 2.0 ** 16)
-    act(view("i16s", 0, 288), view("i16", 0, 288), ACT.Copy, 2.0 ** 17)
-    quant("u", view("ut", 0, 512), 0, 128)
-    pick("up", "u", 0, 256, 128, view("ul", 0, 16))
-    ts(view("pata", 0, 288), view("i16", 0, 288), kappa, OP.not_equal, BIG, OP.mult)
-    ts(view("patb", 0, 288), view("i16s", 0, 288), kmid, OP.subtract, -1.0e22, OP.mult)
-    ts(view("gx", 0, 256), view("gi", 0, 256), group, OP.is_equal)
-    for t in range(4):
-        act(view("ob", t, 512, 4), view("gx", 0, 128))
-    act(rest, group, ACT.Identity, -1.0, 8.0)
-    act(rkc, kappa, ACT.Identity, STEP, -15 * STEP - 1)
-    act(basec, kappa, ACT.Identity, 2 * STEP, -30 * STEP - 1.5)
-    act(ec0, quad, ACT.Identity, 576.0, 144.0)
-    act(ec1, quad, ACT.Identity, 576.0, 432.0)
-
-    def constants_1():
-        for z in range(4):
-            act(view("mc", 512 * z + 504, 512 * z + 512), view("zer", 0, 8))
-            for t in range(4):
-                act(view("zr", 516 * z + 17 * t, 512 * z + 512, 64), view("gx", 0, 128, 16))
-        quant("ob", view("ob", 0, 512), 0, 128)
+    act(rkc, kappa, ACT.Identity, STEP, -15 * STEP - 1 - LOW)
+    for z in range(4):
+        for t in range(4):
+            act(view("zr", 516 * z + 17 * t, 512 * z + 512, 64), view("gx", 0, 128, 16))
 
     def constants_2():
-        ts(view("patr", 0, 288), view("i16s", 0, 288), kmid, OP.subtract, STEP, OP.min)
         ts(view("pats", 0, 288), view("i17", 0, 288), kappa, OP.is_equal, -BIG, OP.mult)
-        ts(view("cst", 0, 4), view("sgr", 0, 4), rest, OP.is_ge, -1.0, OP.mult)
-        ts(view("cst", 4, 8), view("sgr", 4, 8), rest, OP.is_lt)
-        ts(view("offadd", 0, 126), view("sgo", 0, 126), rest, OP.is_ge, 24.0, OP.mult)
-        quant("zr", view("zr", 0, 2048), 0, 512)
+        ts(view("cst", 0, 4), view("sgr", 0, 4), rest, OP.is_ge, -DELTA, OP.mult)
+        ts(view("cst", 4, 8), view("sgr", 4, 8), rest, OP.is_ge)
+        ts(view("cst", 16, 20), view("sgr", 0, 4), rest, OP.is_ge, 24.0, OP.mult)
+        ts(view("wl", 0, 64), view("ii", 32, 96), kappa, OP.add)
+        quant("zr", view("zr", 0, 1024), 0, 256)
 
     def constants_3():
-        for i in range(8):
-            for name, src in (("cn", "gx"), ("rc", "idx")):
+        act(view("cst", 8, 12), view("cst", 4, 8), ACT.Identity, -2.0, 1.0)
+        act(view("cst", 12, 16), view("cst", 4, 8), ACT.Identity, 2.0, -1.0)
+        act(view("cst", 20, 24), view("cst", 4, 8), ACT.Identity, 8.0, 16.0)
+        for z in range(4):
+            act(view("mc", 512 * z + 504, 512 * z + 512), view("zer", 0, 8))
+        for name, src in (("rc", "idx"), ("cn", "gx")):
+            for i in range(8):
                 o = view(name, 512 * (i // 4) + i % 4, 512 * (i // 4) + 512, 4)
                 act(o, view(src, 112 - 16 * i, 240 - 16 * i) if i < 7 else view("zer", 0, 128))
-        act(view("mf", 1152 + 3, 2304, 4), view("zer", 0, 288))
 
     def constants_4():
-        quant("cn", view("cn", 0, 1024), 0, 256)
-        quant("rc", view("rc", 0, 1024), 0, 256)
+        act(base0, kappa, ACT.Identity, STEP, -15 * STEP - 0.5)
+        act(over, group, ACT.Relu, 272.0, -4 * 272.0)
+        act(view("mf", 1152 + 3, 2304, 4), view("zer", 0, 288))
+        act(view("patc", 0, 288), view("patr", 0, 288))
+        act(basec, over, ACT.Identity, 1.0, base0)
+        for f in picks[:2]:
+            f[1]()
 
     def constants_5():
-        quant("ef", view("ef", 0, 2048), 0, 512)
-        quant("ef", view("ef", 2048, 4096), 512, 1024)
+        for f in picks[2:]:
+            f[1]()
 
-    def constants_6():
-        ts(view("wl", 0, 64), view("ii", 32, 96), kappa, OP.add)
-        pick("wl", "w", 0, 1024, 512, view("wl", 0, 64))
-        quant("v", view("vt", 0, 512), 0, 128)
+    def patterns():
+        for k, c in enumerate((0.0, 1.0, 1.0 / 32.0, -1.0, -32.0)):
+            fill(view("hpat", k, 90, 5), c)
 
-    def unpack(h, bank):
-        mm(bank, C, "ef", 128 * h, "x", 0)
+    picks = [pick("wl", "w", 128 * h, 128 * h + 128, 512, view("wl", 8 * h, 8 * h + 8)) for h in range(8)]
+    efq = [lambda h=h: quant("ef", view("ef", 512 * h, 512 * h + 512), 128 * h, 128 * h + 128) for h in range(8)]
+    jobs = [lambda: quant("zr", view("zr", 1024, 2048), 256, 512),
+            lambda: [efq[0](), fill(view("hb", 1, 90, 5), -1.5 * 2.0 ** 28)], lambda: [efq[1](), efq[2]()], patterns,
+            lambda: [efq[3](), fill(view("pat8", 0, 288, p1=32), 0.0)],
+            lambda: quant("rc", view("rc", 0, 1024), 0, 256), lambda: quant("cn", view("cn", 0, 1024), 0, 256),
+            lambda: [efq[4](), fill(view("pat8", 0, 288, 8, p1=32), -BIG)], efq[5], efq[6], efq[7]] + [f[0] for f in picks]
 
-    def keep(h, bank):
-        act(view("fw", 288 * h, 288 * h + 288), ps(bank, 0, 288))
+    def spare(n=1):
+        for f in jobs[:n]:
+            f()
+        del jobs[:n]
 
-    def places(rnd):
-        early = 3 if rnd else 0
-        mm(0, C, "up", 0, "x", 0)
-        mm(1, C, "up", 0, "x", 0)
-        own_ = ps(0, 0, 288)
-        tt(view("dm", 0, 288), own_, view("pata", 0, 288), OP.add)
-        act(view("ssb", 0, 288), ps(1, 0, 288))
-        scan(view("sc", 0, 288), view("patb", 0, 288), view("dm", 0, 288), OP.max, OP.min)
-        for h in range(early):
-            unpack(h, 5 + h)
-        for i in range(3):
-            mm(SB[i], C, "up", 16 * (i + 1), "x", 0)
+    def unpack(dst, src, h, bank):
+        mm(bank, C, "ef", 128 * h, src, 0)
+        return lambda: act(view(dst, 288 * h, 288 * h + 288), ps(bank, 0, 288))
+
+    def scalars(bank, c0, c1):
+        tt(view("dm", c0, c1), ps(bank, c0, c1), view("pata", c0, c1), OP.add)
+        return lambda: scan(view("sc", c0, c1), view("patb", c0, c1), view("dm", c0, c1), OP.max, OP.min)
+
+    def slot(a, c0, c1):
+        return view("ml", 4 * (ML[a // 4] + c0) + a % 4, 4 * (ML[a // 4] + c1), 4)
+
+    def scal(a):
+        return view("sc", 16 * a + 15, 16 * a + 16)
+
+    def local(rnd):
+        def compare(aa, bank):
+            for a in aa:
+                ts(slot(a, 0, 16 * a + 16), ps(bank, 0, 16 * a + 16), scal(a), OP.is_lt)
+
+        def rows(aa):
+            for a in aa:
+                d = 864 + 288 * (a % 3)
+                act(view("dump", d, d + 16 * a), slot(a, 0, 16 * a), ACT.Identity, -1.0, 1.0, acc=view("rs", a, a + 1))
+
+        def count(al, first=False, last=False):
+            c0, w = ML[al] + (160 if al else 0), ML[al + 1] - ML[al]
+            quant("ml", view("ml", 4 * ML[al], 4 * ML[al + 1]), c0, c0 + w)
+            mm(1, C if first else w, "ob", 0, "ml", c0, first, last)
+
+        mm(2, CUT, "up", 0, "x", 0)
+        first = scalars(2, 0, CUT)
+        quant("x", view("xt", 4 * CUT, 1152), CUT, C)
+        first()
+        send(rnd, "arr%d" % rnd, "sent%d" % rnd, [(view("xp%d_%s" % (rnd, k), 0, C), view("x_" + k, 0, C)) for k in "qs"])
         if rnd == 0:
-            constants_1()
-
-        def slot(a, c0, c1):
-            return view("ml", 4 * (ML[a // 4] + c0) + a % 4, 4 * (ML[a // 4] + c1), 4)
-
-        def scal(a):
-            return view("sc", 16 * a + 15, 16 * a + 16)
-
+            unpackers(range(1, 8))
+            quant("ob", view("ob", 0, 512), 0, 128)
+        mm(1, C, "up", 0, "x", 0)
+        mm(0, C, "up", 0, "x", 0)
+        act(view("ssb", 0, 288), ps(1, 0, 288))
+        keeps = [unpack("fw", "x", h, 5 + h) for h in range(3 if rnd else 0)]
+        for i in (1, 2):
+            mm(SB[i], C, "up", 16 * (i + 1), "x", 0)
+        compare(range(0, 8), 2)
+        second = scalars(0, CUT, C)
+        compare(range(8, 10), 2)
+        second()
+        rows(range(1, 10))
+        count(0, first=True)
+        count(1)
         for k, a in enumerate(BY_SCALAR):
-            d = 288 * k
-            act(view("dump", d, d + 16 * a + 16), view("ssb", 0, 16 * a + 16), ACT.Sign, -1.0, scal(a))
-            act(slot(a, 0, 16 * a), view("dump", d, d + 16 * a), ACT.Relu, acc=view("rs", a, a + 1))
-            act(slot(a, 16 * a, 16 * a + 16), view("dump", d + 16 * a, d + 16 * a + 16), ACT.Relu)
-        tt(view("ml", 4 * ML[4] + 2, 4 * ML[5], 4), own_, view("sc", 0, 288), OP.is_equal)
-        order = (2, 1, 0, 4, 3)
-        for n, al in enumerate(order):
-            for a in range(4 * al, min(18, 4 * al + 4)):
-                if a not in BY_SCALAR:
-                    ts(slot(a, 0, 16 * a + 16), ps(0, 0, 16 * a + 16), scal(a), OP.is_lt)
-            quant("ml", view("ml", 4 * ML[al], 4 * ML[al + 1]), ML[al], ML[al + 1])
-            if n == 0:
-                for a in BY_SCALAR:
-                    act(view("rs", a, a + 1), view("rs", a, a + 1), ACT.Identity, -1.0, 16.0 * a)
-            for a in range(4 * al, min(18, 4 * al + 4)):
-                if a and a not in BY_SCALAR:
-                    act(view("dump", 288 * (a % 3), 288 * (a % 3) + 16 * a), slot(a, 0, 16 * a), ACT.Identity, -1.0, 1.0, acc=view("rs", a, a + 1))
-        for n, al in enumerate((4, 2, 1, 0, 3)):
-            mm(1, ML[al + 1] - ML[al], "ob", 0, "ml", ML[al], n == 0, n == 4)
+            act(view("dump", 288 * k, 288 * k + 16 * a + 16), view("ssb", 0, 16 * a + 16), ACT.Sign, -1.0, scal(a))
+        for k, a in enumerate(BY_SCALAR):
+            act(slot(a, 0, 16 * a), view("dump", 288 * k, 288 * k + 16 * a), ACT.Relu, acc=view("rs", a, a + 1))
+            act(slot(a, 16 * a, 16 * a + 16), view("dump", 288 * k + 16 * a, 288 * k + 16 * a + 16), ACT.Relu)
+        mm(SB[0], C, "up", 16, "x", 0)
+        compare(range(10, 12), 0)
+        tt(view("ml", 4 * ML[4] + 2, 4 * ML[5], 4), ps(0, 0, 288), view("sc", 0, 288), OP.is_equal)
+        count(2)
+        compare(range(12, 16), 0)
+        rows(range(10, 12))
+        for a in BY_SCALAR:
+            act(view("rs", a, a + 1), view("rs", a, a + 1), ACT.Identity, -1.0, 16.0 * a)
+        rows(range(12, 16))
+        count(4)
+        count(3, last=True)
+        act(view("patr", 15, 288, 16), view("rs", 0, 18), ACT.Identity, 1.0, rkc)
+        mm(SB[3], C, "up", 64, "x", 0)
+        for k in keeps:
+            k()
+        for i in (6, 4, 5):
+            mm(SB[i], C, "up", 16 * (i + 1), "x", 0)
         if rnd == 0:
             constants_2()
-        mm(SB[3], C, "up", 64, "x", 0)
-        for h in range(early):
-            keep(h, 5 + h)
-        for i in range(4, 7):
-            mm(SB[i], C, "up", 16 * (i + 1), "x", 0)
+        act(view("s7", 0, 288), ps(SB[6], 0, 288))
         if rnd == 0:
             constants_3()
-        act(view("s7", 0, 288), ps(SB[6], 0, 288))
-        scan(view("scn", 0, 288), view("patr", 0, 288), ps(1, 0, 288), OP.add, OP.max)
-        rk = view("rk", 0, 18)
-        tt(rk, view("scn", 15, 288, 16), view("rs", 0, 18), OP.add)
-        ts(view("posl", 0, 18), rk, rkc, OP.add)
+
+    def places(rnd):
+        rk = view("scr", 15, 288, 16)
+        scan(view("scr", 0, 288), ps(1, 0, 288), view("patr", 0, 288), OP.max, OP.add)
+        spare()
+        ts(view("posl", 0, 18), rk, LOW, OP.add)
+        spare()
         scatter(view("sort", 0, 288), view("posl", 0, 18), view("ssb", 0, 288))
+        spare()
         scan(view("wr", 289, 305), view("pats", 0, 16), view("sort", 16, 288, 17), OP.add, OP.max)
         sp, runs = view("wr", 304, 305), view("wr", 15, 288, 17)
-        act(view("dec", 17, 18), sp, ACT.Abs, EPS, DELTA)
+        act(view("sp8", 0, 3), view("cst", 12, 15), ACT.Copy, sp)
         scan(view("wr", 0, 288), view("pats", 0, 288), view("sort", 0, 288), OP.add, OP.max)
-        ts(view("sp8", 0, 8), view("cst", 0, 8), view("dec", 17, 18), OP.mult, sp, OP.add)
+
+        def sized(z):
+            for i in range(4, 7):
+                d = 216 * z + 72 * (i - 4)
+                act(view("dump", d, d + 72), ps(SB[i], z, 288, 4), ACT.Relu, view("cst", 4 + i, 5 + i), view("sp8", i - 4, i - 3))
+
+        sized(0)
         for z in range(4):
             for i in range(4):
-                ts(view("mc", 512 * z + 72 * i, 512 * z + 72 * i + 72), ps(SB[i], z, 288, 4), view("sp8", i, i + 1), OP.is_le)
-            d = 216 * z
+                ts(view("mc", 512 * z + 72 * i, 512 * z + 72 * i + 72), ps(SB[i], z, 288, 4), sp, OP.subtract, view("cst", i, i + 1), OP.is_le)
+            if z < 3:
+                sized(z + 1)
             for i in range(4, 7):
-                act(view("dump", d + 72 * (i - 4), d + 72 * (i - 3)), ps(SB[i], z, 288, 4), ACT.Sign, -1.0, view("sp8", i, i + 1))
-            act(view("mc", 512 * z + 288, 512 * z + 504), view("dump", d, d + 216), ACT.Relu)
+                d = 216 * z + 72 * (i - 4)
+                act(view("mc", 512 * z + 72 * i, 512 * z + 72 * i + 72), view("dump", d, d + 72), ACT.Sign, view("cst", 8 + i, 9 + i))
             if z == 3:
                 act(view("dec", 0, 17), runs, ACT.Abs, EPS, DELTA)
                 act(view("wn", 0, 17), runs)
-            for y in ([z - 1] if 0 < z < 3 else [2, 3] if z else []):
+            if z == 2:
+                spare()
+            for y in ([z - 2] if 1 < z < 3 else [1, 2, 3] if z == 3 else []):
                 quant("mc", view("mc", 512 * y, 512 * y + 512), 128 * y, 128 * y + 128)
                 mm(1, 128, "zr", 128 * y, "mc", 128 * y, y == 0, y == 3)
+                if y == 1:
+                    spare()
         tt(view("wn", 24, 41), runs, view("dec", 0, 17), OP.subtract)
+        spare(2)
         if rnd == 0:
             constants_4()
-        tt(view("off32", 0, 126), ps(1, 0, 126), view("offadd", 0, 126), OP.add)
-        tc(view("off", 0, 126), view("off32", 0, 126))
         wn = view("wn", 0, 48)
+        for i in (0, 6, 1, 2, 3, 4, 5):
+            ts(view("off", 18 * i, 18 * i + 18), ps(1, 18 * i, 18 * i + 18), view("cst", 16 + i, 17 + i), OP.add)
 
         def cmp(i):
             return view("mf", 1152 * (i // 4) + i % 4, 1152 * (i // 4) + 1152, 4)
@@ -379,117 +453,133 @@ def rank_program(g, core, T, topo):
                     w = 90 if t < 3 else 18
                     act(view("rq", t, 4 * w, 4), ps(1, 18 * t, 18 * t + w))
             tt(cmp(i), r, ps(SB[i], 0, 288), OP.is_ge)
-            if i == 2:
+            if i in (0, 2):
+                spare()
+            if i == 1:
                 quant("rq", view("rq", 0, 800), 0, 200)
                 for k in range(2):
                     mm(1, 128, "rc", 128 * k, "rq", 72 * k, k == 0, k == 1)
             if i == 3:
+                ts(view("base", 0, 18), ps(1, 0, 18), 17.0, OP.mult, basec, OP.add)
                 quant("mf", view("mf", 0, 1152), 0, 288)
                 mm(2, C, "cn", 0, "mf", 0, True, False)
-                ts(view("base", 0, 18), ps(1, 0, 18), 17.0, OP.mult, basec, OP.add)
             if i == 4:
-                tt(view("base", 24, 42), view("base", 0, 18), rk, OP.add)
+                tt(view("patc", 15, 288, 16), view("base", 0, 18), rk, OP.add)
         quant("mf", view("mf", 1152, 2304), 288, 576)
         mm(2, C, "cn", 128, "mf", 288, False, True)
-        ts(view("base", 48, 66), view("base", 24, 42), -15.0, OP.add)
-        if rnd == 0:
-            constants_5()
-        for h in range(early, 8):
-            unpack(h, 3 + h % 5)
-            keep(h, 3 + h % 5)
-        scan(view("scn", 0, 288), view("patr", 0, 288), ps(2, 0, 288), OP.add, OP.max)
 
     def seats(rnd):
-        cnt = view("scn", 15, 288, 16)
-        hb = [view("hb", k, 54, 3) for k in range(3)]
-        tt(hb[1], cnt, view("base", 24, 42), OP.add)
-        tt(view("n2", 0, 18), cnt, view("base", 48, 66), OP.add)
-        ts(hb[0], hb[1], 1.5 * 2.0 ** 24, OP.add, -1.5 * 2.0 ** 24, OP.add)
-        ts(hb[2], view("n2", 0, 18), 1.5 * 2.0 ** 28, OP.add, -1.5 * 2.0 ** 28, OP.add)
-        scan(view("hs", 0, 54), view("hpat", 0, 54), view("hb", 0, 54), OP.mult, OP.add)
-        ts(view("phl", 0, 18), view("hs", 2, 54, 3), 0.5, OP.mult, 8.0, OP.add)
-        iw = view("iw%d" % rnd, 0, 2304)
-        scatter(iw, view("phl", 0, 18), view("cval", 0, 288))
-        turn(view("itr", 0, 2304), iw)
-        e = [(72 * k, 72 * k + 72) for k in range(7)]
-        ts(view("en", *e[0]), view("itr", 0, 2304, 32), ec0, OP.add)
-        ts(view("en", *e[1]), view("itr", 16, 2304, 32), ec1, OP.add)
-        tt(view("en", *e[2]), view("en", *e[0]), view("en", *e[1]), OP.max)
-        tc(view("en", *e[3], p1=64), view("en", *e[2], p0=64))
-        tt(view("en", *e[4], p1=64), view("en", *e[2], p1=64), view("en", *e[3], p1=64), OP.max)
-        tc(view("en", *e[5], p1=32), view("en", *e[4], p0=32, p1=64))
-        tt(view("en", *e[6], p1=32), view("en", *e[4], p1=32), view("en", *e[5], p1=32), OP.max)
-        for t in range(4):
-            tc(view("tl", 0, 72, p0=32 * t, p1=32 * t + 32), view("en", *e[6], p1=32))
+        spare(3)
+        if rnd == 0:
+            constants_5()
+        todo = [("fw", "x", h) for h in range(3 if rnd else 0, 8)] + [("fp", "xp%d" % rnd, h) for h in range(8)]
+        late = todo[-LATE:]
+        for n, (d, s, h) in enumerate(todo[:-LATE]):
+            unpack(d, s, h, 3 + n % 5)()
+        n = view("scn", 15, 288, 16)
+        scan(view("scn", 0, 288), ps(2, 0, 288), view("patc", 0, 288), OP.max, OP.add)
+        spare()
+        hb = [view("hb", k, 90, 5) for k in range(5)]
+        ts(hb[0], n, LOW - 15.0, OP.add, 1.5 * 2.0 ** 28, OP.add)
+        ts(hb[2], n, LOW, OP.add)
+        for k in (3, 4):
+            ts(hb[k], n, LOW + 1.5 * 2.0 ** 24, OP.add, -1.5 * 2.0 ** 24, OP.add)
+        spare()
+        scan(view("hs", 0, 90), view("hpat", 0, 90), view("hb", 0, 90), OP.mult, OP.add)
+        spare()
+        ts(view("phl", 0, 18), view("hs", 4, 90, 5), 0.5, OP.mult, 8.0, OP.add)
+        spare()
+        iw = "iw%d" % rnd
+        scatter(view(iw, 0, 2304), view("phl", 0, 18), view("cval", 0, 288))
+        spare()
+        for k in (0, 1):
+            turn(view("itr", 1152 * k, 1152 * k + 1152), view(iw, 1152 * k, 1152 * k + 1152))
+        spare()
+        keeps = [unpack(d, s, h, 3 + n % 5) for n, (d, s, h) in enumerate(late)]
+        for k in (0, 1):
+            for gr in range(8):
+                o, i = view("en", 288 * k + gr, 288 * k + 288, 8, p1=32), view("itr", 1152 * k + 16 * (gr % 2), 1152 * k + 1152, 32, 32 * (gr // 2), 32 * (gr // 2) + 32)
+                if gr < 4 * k:
+                    ts(o, i, 288.0 * gr + 144.0, OP.add)
+                else:
+                    act(o, i, ACT.Identity, 1.0, 288.0 * gr + 144.0)
+        for f in keeps:
+            f()
+        for k in (0, 1):
+            scan(view("es", 288 * k, 288 * k + 288, p1=32), view("pat8", 0, 288, p1=32), view("en", 288 * k, 288 * k + 288, p1=32), OP.add, OP.max)
+        for k, name in ((0, "ls%d" % rnd), (1, "tl")):
+            for t in range(4):
+                tc(view(name, 0, 36, p0=32 * t, p1=32 * t + 32), view("es", 288 * k + 7, 288 * k + 288, 8, p1=32))
+            if k == 0:
+                send(rnd, "larr%d" % rnd, "lsent%d" % rnd, [(view("lp%d" % rnd, 0, 36), view("ls%d" % rnd, 0, 36))])
+        spare()
 
-    def move(q, o, i):
-        if q == "S":
-            act(o, i)
-        else:
-            tc(o, i)
-
-    def half(k):
-        c0, win = 576 * k, view("fw", 0, 2304)
-        vfetch(view("ow", c0, c0 + 288), win, view("tl", 36 * k, 36 * k + 18))
-        fetch(view("ow", c0 + 288, c0 + 576), win, view("tl", 36 * k + 18, 36 * k + 36))
+    def half(k, win, lst):
+        c0, win = 576 * k, view(win, 0, 2304)
+        steps = [lambda: [vfetch(view("ow", c0, c0 + 288), win, view(lst, 0, 18)), fetch(view("ow", c0 + 288, c0 + 576), win, view(lst, 18, 36))]]
         for n in range(16):
-            q, t = n // 4, n % 4
-            move("S" if n % 3 == 1 else "V", view("tt", c0 + t, c0 + 576, 4, 32 * q, 32 * q + 32), view("ow", c0 + q, c0 + 576, 4, 32 * t, 32 * t + 32))
+            steps.append(lambda q=n // 4, t=n % 4, n=n: move("S" if n % 3 == 1 else "V", view("tt", c0 + t, c0 + 576, 4, 32 * q, 32 * q + 32), view("ow", c0 + q, c0 + 576, 4, 32 * t, 32 * t + 32)))
+        steps.append(lambda: quant("tb" if k else "ta", view("tt", c0, c0 + 576), 0, 144))
+        return steps
 
-    def layer(src, hf, between=()):
+    def layer(src, hf, between):
         for h in range(8):
             a, b = (2 * h) % 8, (2 * h + 1) % 8
             mm(a, H, "wl", 128 * h, src, 0)
             mm(b, H, "ef", 128 * h, src, 0)
-            r = view("rl", 144 * h, 144 * h + 144)
+            r = view("rl", 1152 * hf + 144 * h, 1152 * hf + 144 * h + 144)
             act(r, ps(a, 0, 144), ACT.Relu, 0.03125)
             tt(view("tw", 1152 * hf + h, 1152 * hf + 1152, 8), ps(b, 0, 144), r, OP.add)
-            if h < len(between):
-                between[h]()
+            for f in between.get(h, ()):
+                f()
 
     def home():
         win = view("tw", 0, 2304)
-        vfetch(view("o2", 0, 288), win, view("hl", 0, 18))
+        w0, w1 = CUT, C - CUT
+        vfetch(view("o2", 0, w0), win, view("hl", 0, 10))
         for q in range(1, 4):
-            fetch(view("o2", 288 * q, 288 * q + 288), win, view("hl", 18 * q, 18 * q + 18))
+            fetch(view("o2", w0 * q, w0 * q + w0), win, view("hl", 10 * q, 10 * q + 10))
+        for q in (0, 2):
+            fetch(view("o2", 4 * w0 + w1 * q, 4 * w0 + w1 * q + 2 * w1), win, view("hl", 40 + 8 * q, 56 + 8 * q))
         for n in range(16):
             q, t = n // 4, n % 4
-            move("S" if n > 12 else "V", view("xt", t, 1152, 4, 32 * q, 32 * q + 32), view("o2", 288 * q, 288 * q + 288, 1, 32 * t, 32 * t + 32))
+            tc(view("xt", t, 4 * w0, 4, 32 * q, 32 * q + 32), view("o2", w0 * q, w0 * q + w0, 1, 32 * t, 32 * t + 32))
+        for n in range(16):
+            q, t = n // 4, n % 4
+            move("S" if n > 11 else "V", view("xt", 4 * w0 + t, 1152, 4, 32 * q, 32 * q + 32), view("o2", 4 * w0 + w1 * q, 4 * w0 + w1 * q + w1, 1, 32 * t, 32 * t + 32))
+            if n == 3:
+                quant("x", view("xt", 0, 4 * CUT), 0, CUT)
 
+    quant("x", view("xt", 0, 4 * CUT), 0, CUT)
     for rnd in range(3):
-        quant("x", view("xt", 0, 1152), 0, 288)
+        local(rnd)
         places(rnd)
         seats(rnd)
-        ta, lc = "ta%d" % rnd, "lc%d" % rnd
-        half(0)
-        quant(ta, view("tt", 0, 576), 0, 144)
-        dst = T.cores[rank ^ MASKS[rnd]]
-        rid, pid = topo.addr(dst)[0], topo.addr(dst)[1]
-        mask, ne = topo.mask(core, dst), len(topo.engines(core, dst))
-        settle("G", [view(ta + "_q", 0, 144), view(ta + "_s", 0, 144)], [])
-        arr, sent = "arr%d" % rnd, "sent%d" % rnd
-        g.remote_dma(T[lc + "_q"][:, 0:144].bitcast(dt.uint8), T[ta + "_q"][:, 0:144].bitcast(dt.uint8), T.sem[arr], T.sem[sent], pid, rid, mask)
-        g.remote_dma(T[lc + "_s"][:, 0:144], T[ta + "_s"][:, 0:144], T.sem[arr], T.sem[sent], pid, rid, mask)
-        total[arr] = total[sent] = 2 * ne
-        note("R", arr, 2 * ne, [], [view(lc + "_q", 0, 144), view(lc + "_s", 0, 144)])
-        half(1)
-        quant("tb", view("tt", 576, 1152), 0, 144)
-        if rnd == 0:
-            constants_6()
-        lists = [lambda q=q: ts(view("hl", 18 * q, 18 * q + 18, p1=32), view("hb", 1, 54, 3, 32 * q, 32 * q + 32), 0.5, OP.add) for q in range(4)]
+        for f in half(1, "fw", "tl"):
+            f()
+        spare(99)
+        lists = [lambda q=q, a0=a0, a1=a1, c=c: ts(view("hl", c + (a1 - a0) * q, c + (a1 - a0) * (q + 1), p1=32), view("scn", 16 * a0 + 15, 16 * a1, 16, 32 * q, 32 * q + 32), LOW + 0.5, OP.add)
+                 for a0, a1, c in ((0, 10, 0), (10, 18, 40)) for q in range(4)]
         lists.append(lambda: tc(view("hl", 0, 72, p0=32, p1=64), view("hl", 0, 72, p1=32)))
         lists.append(lambda: tc(view("hl", 0, 72, p0=64), view("hl", 0, 72, p1=64)))
-        layer("tb", 1, lists)
+        other = half(0, "fp", "lp%d" % rnd)
+        layer("tb", 1, {0: other[:1], 2: other[1:9], 3: other[9:17], 4: other[17:]})
+        last = {0: lists[:3], 1: lists[3:6], 2: lists[6:8], 3: lists[8:9], 4: lists[9:]}
         if rnd == 2:
-            fill(view("ntf", 18, 32), 0.0)
-            ts(view("ntf", 0, 18), view("hb", 1, 54, 3), 0.5, OP.add)
-            turn(view("ntt", 0, 32), view("ntf", 0, 32))
-            for gr in range(8):
-                v = view("ntt", 16 * (gr % 2), 16 * (gr % 2) + 16, 1, 32 * (gr // 2), 32 * (gr // 2) + 18)
-                dma("outd", T.pl[gr:gr + 1, :], v[6], [v], [])
-        layer(lc, 0)
+            def places_out():
+                fill(view("ntf", 18, 32), 0.0)
+                ts(view("ntf", 0, 18), view("scn", 15, 288, 16), LOW + 0.5, OP.add)
+                quant("v", view("vt", 0, 512), 0, 128)
+
+            def places_out2():
+                turn(view("ntt", 0, 32), view("ntf", 0, 32))
+                for gr in range(8):
+                    v = view("ntt", 16 * (gr % 2), 16 * (gr % 2) + 16, 1, 32 * (gr // 2), 32 * (gr // 2) + 18)
+                    dma("outd", T.pl[gr:gr + 1, :], v[6], [v], [])
+            last[5], last[6] = [places_out], [places_out2]
+        layer("ta", 0, last)
         home()
-    quant("x", view("xt", 0, 1152), 0, 288)
+    quant("x", view("xt", 4 * CUT, 1152), CUT, C)
     mm(0, C, "v", 0, "x", 0)
     v = view("x_q", 0, 288)
     dma("outd", T.oc[:], v[6].bitcast(dt.uint8), [v], [])

@@ -12,6 +12,8 @@ LOW = 8192.0
 EMPTY = -32768.0
 CUT = 160
 LATE = 4
+PARTS = ((2, 0, CUT), (3, CUT, C))
+FREE = (4, 5, 7, 0, 1, 6)
 MASKS = [1, 2, 3]
 ML = [0, 128, 256, 448, 704, 992]
 BY_SCALAR = (17, 16)
@@ -19,10 +21,10 @@ SB = [2, 3, 4, 0, 5, 6, 7]
 
 SCRATCH = {}
 for _t, _s in (
-        ("float32", "pf 16 i16 288 i16s 288 i17 296 gi 256 sgr 8 pata 288 patb 288 patr 288 patc 288 pats 288 pat8 288 cst 24 hpat 96 dm 288 sc 288 ssb 288 rs 24 scr 288 scn 288 sort 288 wr 312 dec 24 sp8 8 wn 48 s7 288 rt 1728 base 24 hb 96 hs 96 en 576 es 576 ntf 32 ntt 32 rl 2304"),
+        ("float32", "pf 16 i16 288 i16s 288 i17 296 gi 256 sgr 8 pata 288 patb 288 patr 288 patc 288 pats 288 pat8 288 cst 24 hpat 96 dm 288 sc 288 ssb 288 rs 24 scr 288 scn 288 sort 288 wr 312 dec 24 sp8 8 wn 48 s7 288 rt 1728 base 24 hb 96 hs 96 es 576 ntf 32 ntt 32 rl 2304"),
         ("int32", "pi 8 ii 96"),
         ("uint16", "ul 16 wl 64 posl 18 off 128 phl 18 tl 36 hl 72 ls0 36 ls1 36 ls2 36 lp0 36 lp1 36 lp2 36"),
-        ("bfloat16", "dump 1728 cval 288 ones 256 zer 1024 neg 768 gx 256 idx 256 ef 4096 ob 512 zr 2048 cn 1024 rc 1024 rq 800 xt 1152 ut 512 vt 512 ml 3968 mc 2048 mf 2304 iw0 2304 iw1 2304 iw2 2304 itr 2304 fw 2304 fp 2304 ow 1152 tt 1152 o2 1152 tw 2304"),
+        ("bfloat16", "dump 1728 cval 288 ones 256 zer 1024 neg 768 gx 256 idx 256 ef 4096 ob 512 zr 2048 cn 1024 rc 1024 rq 800 xt 1152 ut 512 vt 512 ml 3968 mc 2048 mf 2304 iw0 2304 iw1 2304 iw2 2304 itr 2304 fw 2304 fp 2304 ow 1152 tt 1152 o2 1152 en 576 tw 2304"),
         ("mx", "ef 1024 ob 128 zr 512 cn 256 rc 256 rq 200 u 128 v 128 up 256 w 512 wl 1024 x 288 ml 1152 mc 512 mf 576 ta 144 tb 144 xp0 288 xp1 288 xp2 288")):
     _s = _s.split()
     for _n, _w in zip(_s[::2], _s[1::2]):
@@ -102,10 +104,10 @@ def rank_program(g, core, T, topo):
         call().then_inc(T.sem[sem], 1)
         note(q, sem, total[sem], reads, writes)
 
-    def dma(sem, out, in_, reads, writes):
-        settle("Y", reads, writes)
+    def dma(sem, out, in_, reads, writes, q="Y"):
+        settle(q, reads, writes)
         total[sem] = total.get(sem, 0) + 16
-        g.sync.dma_start(out, in_).then_inc(T.sem[sem], 16)
+        (g.sync if q == "Y" else g.scalar).dma_start(out, in_).then_inc(T.sem[sem], 16)
         note("Y", sem, total[sem], reads, writes)
 
     def send(rnd, arr, sent, pairs):
@@ -278,7 +280,6 @@ def rank_program(g, core, T, topo):
         quant("zr", view("zr", 0, 1024), 0, 256)
 
     def constants_3():
-        act(view("cst", 8, 12), view("cst", 4, 8), ACT.Identity, -2.0, 1.0)
         act(view("cst", 12, 16), view("cst", 4, 8), ACT.Identity, 2.0, -1.0)
         act(view("cst", 20, 24), view("cst", 4, 8), ACT.Identity, 8.0, 16.0)
         for z in range(4):
@@ -286,7 +287,7 @@ def rank_program(g, core, T, topo):
         for name, src in (("rc", "idx"), ("cn", "gx")):
             for i in range(8):
                 o = view(name, 512 * (i // 4) + i % 4, 512 * (i // 4) + 512, 4)
-                act(o, view(src, 112 - 16 * i, 240 - 16 * i) if i < 7 else view("zer", 0, 128))
+                act(o, view(src, 112 - 16 * i, 240 - 16 * i) if i < 7 else view("zer", 0, 128), ACT.Copy, view("cst", 8 + i, 9 + i) if name == "rc" and i > 3 else 1.0)
 
     def constants_4():
         act(base0, kappa, ACT.Identity, STEP, -15 * STEP - 0.5)
@@ -309,9 +310,9 @@ def rank_program(g, core, T, topo):
     efq = [lambda h=h: quant("ef", view("ef", 512 * h, 512 * h + 512), 128 * h, 128 * h + 128) for h in range(8)]
     jobs = [lambda: quant("zr", view("zr", 1024, 2048), 256, 512),
             lambda: [efq[0](), fill(view("hb", 1, 90, 5), -1.5 * 2.0 ** 28)], lambda: [efq[1](), efq[2]()], patterns,
-            lambda: [efq[3](), fill(view("pat8", 0, 288, p1=32), 0.0)],
+            lambda: [efq[3](), fill(view("pat8", 0, 288, p1=32), -576.0)],
             lambda: quant("rc", view("rc", 0, 1024), 0, 256), lambda: quant("cn", view("cn", 0, 1024), 0, 256),
-            lambda: [efq[4](), fill(view("pat8", 0, 288, 8, p1=32), -BIG)], efq[5], efq[6], efq[7]] + [f[0] for f in picks]
+            lambda: [efq[4](), fill(view("pat8", 0, 288, 8, p1=32), -BIG), fill(view("pat8", 4, 288, 8, p1=32), 1440.0)], efq[5], efq[6], efq[7]] + [f[0] for f in picks]
 
     def spare(n=1):
         for f in jobs[:n]:
@@ -374,16 +375,16 @@ def rank_program(g, core, T, topo):
             act(slot(a, 0, 16 * a), view("dump", 288 * k, 288 * k + 16 * a), ACT.Relu, acc=view("rs", a, a + 1))
             act(slot(a, 16 * a, 16 * a + 16), view("dump", 288 * k + 16 * a, 288 * k + 16 * a + 16), ACT.Relu)
         mm(SB[0], C, "up", 16, "x", 0)
-        compare(range(10, 12), 0)
-        tt(view("ml", 4 * ML[4] + 2, 4 * ML[5], 4), ps(0, 0, 288), view("sc", 0, 288), OP.is_equal)
-        count(2)
         compare(range(12, 16), 0)
-        rows(range(10, 12))
+        tt(view("ml", 4 * ML[4] + 2, 4 * ML[5], 4), ps(0, 0, 288), view("sc", 0, 288), OP.is_equal)
+        count(3)
+        compare(range(10, 12), 0)
+        rows(range(12, 14))
         for a in BY_SCALAR:
             act(view("rs", a, a + 1), view("rs", a, a + 1), ACT.Identity, -1.0, 16.0 * a)
-        rows(range(12, 16))
+        rows((14, 15, 10, 11))
         count(4)
-        count(3, last=True)
+        count(2, last=True)
         act(view("patr", 15, 288, 16), view("rs", 0, 18), ACT.Identity, 1.0, rkc)
         mm(SB[3], C, "up", 64, "x", 0)
         for k in keeps:
@@ -406,13 +407,12 @@ def rank_program(g, core, T, topo):
         spare()
         scan(view("wr", 289, 305), view("pats", 0, 16), view("sort", 16, 288, 17), OP.add, OP.max)
         sp, runs = view("wr", 304, 305), view("wr", 15, 288, 17)
-        act(view("sp8", 0, 3), view("cst", 12, 15), ACT.Copy, sp)
         scan(view("wr", 0, 288), view("pats", 0, 288), view("sort", 0, 288), OP.add, OP.max)
 
         def sized(z):
             for i in range(4, 7):
                 d = 216 * z + 72 * (i - 4)
-                act(view("dump", d, d + 72), ps(SB[i], z, 288, 4), ACT.Relu, view("cst", 4 + i, 5 + i), view("sp8", i - 4, i - 3))
+                act(view("dump", d, d + 72), ps(SB[i], z, 288, 4), ACT.Sign, -1.0, sp)
 
         sized(0)
         for z in range(4):
@@ -422,7 +422,7 @@ def rank_program(g, core, T, topo):
                 sized(z + 1)
             for i in range(4, 7):
                 d = 216 * z + 72 * (i - 4)
-                act(view("mc", 512 * z + 72 * i, 512 * z + 72 * i + 72), view("dump", d, d + 72), ACT.Sign, view("cst", 8 + i, 9 + i))
+                act(view("mc", 512 * z + 72 * i, 512 * z + 72 * i + 72), view("dump", d, d + 72), ACT.Relu, view("cst", 8 + i, 9 + i))
             if z == 3:
                 act(view("dec", 0, 17), runs, ACT.Abs, EPS, DELTA)
                 act(view("wn", 0, 17), runs)
@@ -439,19 +439,19 @@ def rank_program(g, core, T, topo):
             constants_4()
         wn = view("wn", 0, 48)
         for i in (0, 6, 1, 2, 3, 4, 5):
-            ts(view("off", 18 * i, 18 * i + 18), ps(1, 18 * i, 18 * i + 18), view("cst", 16 + i, 17 + i), OP.add)
+            ts(view("off", 18 * i, 18 * i + 18), ps(1, 18 * i, 18 * i + 18), view("cst", 8 + i, 9 + i) if i > 3 else 1.0, OP.mult, view("cst", 16 + i, 17 + i), OP.add)
 
         def cmp(i):
             return view("mf", 1152 * (i // 4) + i % 4, 1152 * (i // 4) + 1152, 4)
 
         fused(cmp(6), wn, view("off", 108, 126), view("s7", 0, 288), OP.is_ge)
-        for i in range(6):
+        for i in range(5):
             r = view("rt", 288 * i, 288 * i + 288)
             fetch(r, wn, view("off", 18 * i, 18 * i + 18))
             if i == 1:
                 for t in range(4):
                     w = 90 if t < 3 else 18
-                    act(view("rq", t, 4 * w, 4), ps(1, 18 * t, 18 * t + w))
+                    tc(view("rq", t, 4 * w, 4), ps(1, 18 * t, 18 * t + w))
             tt(cmp(i), r, ps(SB[i], 0, 288), OP.is_ge)
             if i in (0, 2):
                 spare()
@@ -461,12 +461,18 @@ def rank_program(g, core, T, topo):
                     mm(1, 128, "rc", 128 * k, "rq", 72 * k, k == 0, k == 1)
             if i == 3:
                 ts(view("base", 0, 18), ps(1, 0, 18), 17.0, OP.mult, basec, OP.add)
-                quant("mf", view("mf", 0, 1152), 0, 288)
-                mm(2, C, "cn", 0, "mf", 0, True, False)
             if i == 4:
                 tt(view("patc", 15, 288, 16), view("base", 0, 18), rk, OP.add)
-        quant("mf", view("mf", 1152, 2304), 288, 576)
-        mm(2, C, "cn", 128, "mf", 288, False, True)
+        quant("mf", view("mf", 0, 1152), 0, 288)
+        for b, c0, c1 in PARTS:
+            mm(b, c1 - c0, "cn", 0, "mf", c0, True, False)
+        for b, c0, c1 in PARTS:
+            fetch(view("rt", 1440 + c0, 1440 + c1), wn, view("off", 90 + c0 // 16, 90 + c1 // 16))
+        for b, c0, c1 in PARTS:
+            tt(view("mf", 1153 + 4 * c0, 1152 + 4 * c1, 4), view("rt", 1440 + c0, 1440 + c1), ps(SB[5], c0, c1), OP.is_ge)
+        for b, c0, c1 in PARTS:
+            quant("mf", view("mf", 1152 + 4 * c0, 1152 + 4 * c1), 288 + c0, 288 + c1)
+            mm(b, c1 - c0, "cn", 128, "mf", 288 + c0, False, True)
 
     def seats(rnd):
         spare(3)
@@ -475,9 +481,10 @@ def rank_program(g, core, T, topo):
         todo = [("fw", "x", h) for h in range(3 if rnd else 0, 8)] + [("fp", "xp%d" % rnd, h) for h in range(8)]
         late = todo[-LATE:]
         for n, (d, s, h) in enumerate(todo[:-LATE]):
-            unpack(d, s, h, 3 + n % 5)()
+            unpack(d, s, h, FREE[n % 6])()
         n = view("scn", 15, 288, 16)
-        scan(view("scn", 0, 288), ps(2, 0, 288), view("patc", 0, 288), OP.max, OP.add)
+        for b, c0, c1 in PARTS:
+            scan(view("scn", c0, c1), ps(b, 0, c1 - c0), view("patc", c0, c1), OP.max, OP.add)
         spare()
         hb = [view("hb", k, 90, 5) for k in range(5)]
         ts(hb[0], n, LOW - 15.0, OP.add, 1.5 * 2.0 ** 28, OP.add)
@@ -495,21 +502,17 @@ def rank_program(g, core, T, topo):
         for k in (0, 1):
             turn(view("itr", 1152 * k, 1152 * k + 1152), view(iw, 1152 * k, 1152 * k + 1152))
         spare()
-        keeps = [unpack(d, s, h, 3 + n % 5) for n, (d, s, h) in enumerate(late)]
+        keeps = [unpack(d, s, h, FREE[(n + 2) % 6]) for n, (d, s, h) in enumerate(late)]
         for k in (0, 1):
-            for gr in range(8):
-                o, i = view("en", 288 * k + gr, 288 * k + 288, 8, p1=32), view("itr", 1152 * k + 16 * (gr % 2), 1152 * k + 1152, 32, 32 * (gr // 2), 32 * (gr // 2) + 32)
-                if gr < 4 * k:
-                    ts(o, i, 288.0 * gr + 144.0, OP.add)
-                else:
-                    act(o, i, ACT.Identity, 1.0, 288.0 * gr + 144.0)
+            for q in range(4):
+                move("V" if q < 2 * k else "S", view("en", 288 * k + q, 288 * k + 288, 4, p1=32), view("itr", 1152 * k, 1152 * k + 1152, 16, 32 * q, 32 * q + 32))
         for f in keeps:
             f()
         for k in (0, 1):
             scan(view("es", 288 * k, 288 * k + 288, p1=32), view("pat8", 0, 288, p1=32), view("en", 288 * k, 288 * k + 288, p1=32), OP.add, OP.max)
         for k, name in ((0, "ls%d" % rnd), (1, "tl")):
             for t in range(4):
-                tc(view(name, 0, 36, p0=32 * t, p1=32 * t + 32), view("es", 288 * k + 7, 288 * k + 288, 8, p1=32))
+                ts(view(name, 0, 36, p0=32 * t, p1=32 * t + 32), view("es", 288 * k + 7, 288 * k + 288, 8, p1=32), 7 * 288.0 + 144.0, OP.add)
             if k == 0:
                 send(rnd, "larr%d" % rnd, "lsent%d" % rnd, [(view("lp%d" % rnd, 0, 36), view("ls%d" % rnd, 0, 36))])
         spare()
@@ -563,7 +566,8 @@ def rank_program(g, core, T, topo):
         lists.append(lambda: tc(view("hl", 0, 72, p0=32, p1=64), view("hl", 0, 72, p1=32)))
         lists.append(lambda: tc(view("hl", 0, 72, p0=64), view("hl", 0, 72, p1=64)))
         other = half(0, "fp", "lp%d" % rnd)
-        layer("tb", 1, {0: other[:1], 2: other[1:9], 3: other[9:17], 4: other[17:]})
+        other[0]()
+        layer("tb", 1, {1: other[1:9], 2: other[9:17], 3: other[17:]})
         last = {0: lists[:3], 1: lists[3:6], 2: lists[6:8], 3: lists[8:9], 4: lists[9:]}
         if rnd == 2:
             def places_out():
@@ -579,16 +583,18 @@ def rank_program(g, core, T, topo):
             last[5], last[6] = [places_out], [places_out2]
         layer("ta", 0, last)
         home()
+    mm(0, CUT, "v", 0, "x", 0)
+    dma("outd", T.oc[:, 0:4 * CUT], T.x_q[:, 0:CUT].bitcast(dt.uint8), [view("x_q", 0, CUT)], [])
     quant("x", view("xt", 4 * CUT, 1152), CUT, C)
-    mm(0, C, "v", 0, "x", 0)
-    v = view("x_q", 0, 288)
-    dma("outd", T.oc[:], v[6].bitcast(dt.uint8), [v], [])
+    mm(1, C - CUT, "v", 0, "x", CUT)
+    act(view("dm", 0, CUT), ps(0, 0, CUT))
+    dma("outd", T.y[:, 0:CUT], T.dm[:, 0:CUT], [view("dm", 0, CUT)], [])
+    dma("outd", T.oc[:, 4 * CUT:4 * C], T.x_q[:, CUT:C].bitcast(dt.uint8), [view("x_q", CUT, C)], [])
     for k in range(4):
         v = view("x_s", 0, 288, 1, 32 * k, 32 * k + 4)
-        dma("outd", T.osc[4 * k:4 * k + 4, :], v[6], [v], [])
-    tc(view("dm", 0, 288), ps(0, 0, 288))
-    v = view("dm", 0, 288)
-    dma("outd", T.y[:], v[6], [v], [])
+        dma("outd", T.osc[4 * k:4 * k + 4, :], v[6], [v], [], "S")
+    tc(view("dm", CUT, C), ps(1, 0, C - CUT))
+    dma("outd", T.y[:, CUT:C], T.dm[:, CUT:C], [view("dm", CUT, C)], [])
     for sem in SEMAPHORES:
         if known["G"].get(sem, 0) < total[sem]:
             g.wait_ge(T.sem[sem], total[sem])

@@ -11,6 +11,7 @@ STEP = 4096.0
 LOW = 8192.0
 EMPTY = -32768.0
 CUT = 160
+AC = CUT // 16
 LATE = 4
 PARTS = ((2, 0, CUT), (3, CUT, C))
 FREE = (4, 5, 7, 0, 1, 6)
@@ -18,14 +19,15 @@ MASKS = [1, 2, 3]
 ML = [0, 128, 256, 448, 704, 992]
 BY_SCALAR = (17, 16)
 SB = [2, 3, 4, 0, 5, 6, 7]
+M2, M4, M8, M32 = [1.5 * 2.0 ** (23 + k) for k in (1, 2, 3, 5)]
 
 SCRATCH = {}
 for _t, _s in (
-        ("float32", "pf 16 i16 288 i16s 288 i17 296 gi 256 sgr 8 pata 288 patb 288 patr 288 patc 288 pats 288 pat8 288 cst 24 hpat 96 dm 288 sc 288 ssb 288 rs 24 scr 288 scn 288 sort 288 wr 312 dec 24 sp8 8 wn 48 s7 288 rt 1728 base 24 hb 96 hs 96 es 576 ntf 32 ntt 32 rl 2304"),
+        ("float32", "pf 16 i16 288 i16s 288 i17 296 gi 256 pata 288 patb 288 patr 288 patc 288 pats 288 pat8 288 cst 32 hpat 192 dm 288 sc 288 ssb 288 rs 24 scr 288 scn 288 sort 288 wr 312 dec 24 wn 48 s7 288 rt 1728 hb 96 hs 96 es 576 ntf 64 rl 1152 hx 256"),
         ("int32", "pi 8 ii 96"),
-        ("uint16", "ul 16 wl 64 posl 18 off 128 phl 18 tl 36 hl 72 ls0 36 ls1 36 ls2 36 lp0 36 lp1 36 lp2 36"),
-        ("bfloat16", "dump 1728 cval 288 ones 256 zer 1024 neg 768 gx 256 idx 256 ef 4096 ob 512 zr 2048 cn 1024 rc 1024 rq 800 xt 1152 ut 512 vt 512 ml 3968 mc 2048 mf 2304 iw0 2304 iw1 2304 iw2 2304 itr 2304 fw 2304 fp 2304 ow 1152 tt 1152 o2 1152 en 576 tw 2304"),
-        ("mx", "ef 1024 ob 128 zr 512 cn 256 rc 256 rq 200 u 128 v 128 up 256 w 512 wl 1024 x 288 ml 1152 mc 512 mf 576 ta 144 tb 144 xp0 288 xp1 288 xp2 288")):
+        ("uint16", "ul 16 wl 32 posl 18 off 128 phl 18 tl 36 hl 72 ls0 36 ls1 36 ls2 36 lp0 36 lp1 36 lp2 36"),
+        ("bfloat16", "dump 1728 cval 288 ones 512 zer 1024 neg 768 gx 256 idx 256 ef 4096 ob 512 zr 2048 cn 1024 rc 1024 rq 800 xt 1152 ut 512 vt 512 ml 3968 mc 2048 mf 2304 iw0 2304 iw1 2304 iw2 2304 itr 2304 fw 2304 fp 2304 ow 1152 tt 1152 o2 1152 en 576 tw 2336 tz 1184 eu 2048"),
+        ("mx", "ef 1024 ob 128 zr 512 cn 256 rc 256 rq 200 u 128 v 128 up 256 w 512 wl 512 eu 512 x 288 ml 1152 mc 512 mf 576 ta 144 tb 144 xp0 288 xp1 288 xp2 288")):
     _s = _s.split()
     for _n, _w in zip(_s[::2], _s[1::2]):
         if _t == "mx":
@@ -36,7 +38,7 @@ for _t, _s in (
 for _m in range(8):
     SCRATCH["p%d" % _m] = ("psum", [128, 512], "float32")
 
-SEMAPHORES = "sv sa st sg lx ly lu lw ls lv z0 z1 z2 z3 z4 z5 outd arr0 arr1 arr2 sent0 sent1 sent2 larr0 larr1 larr2 lsent0 lsent1 lsent2".split()
+SEMAPHORES = "sv sa st sg lx ly lu lw ls lv y0 y1 y2 y3 y4 y5 y6 y7 z0 z1 z2 outd arr0 arr1 arr2 sent0 sent1 sent2 larr0 larr1 larr2 lsent0 lsent1 lsent2".split()
 
 
 def rank_program(g, core, T, topo):
@@ -110,6 +112,10 @@ def rank_program(g, core, T, topo):
         (g.sync if q == "Y" else g.scalar).dma_start(out, in_).then_inc(T.sem[sem], 16)
         note("Y", sem, total[sem], reads, writes)
 
+    def spread(sem, name, c0, c1, src):
+        o, i = view(name, c0, c1), view(src, 0, c1 - c0)
+        dma(sem, o[6], i[6], [i], [o])
+
     def send(rnd, arr, sent, pairs):
         dst = T.cores[rank ^ MASKS[rnd]]
         rid, pid = topo.addr(dst)[0], topo.addr(dst)[1]
@@ -178,6 +184,9 @@ def rank_program(g, core, T, topo):
     def move(q, o, i):
         if q == "S":
             act(o, i)
+        elif q == "G":
+            n = len(range(o[3], o[4], o[5]))
+            run("G", lambda: g.affine_select(o[6], i[6], [[0, n]], OP.is_equal, 0.0, 0, 0), [i], [o])
         else:
             tc(o, i)
 
@@ -205,42 +214,39 @@ def rank_program(g, core, T, topo):
 
     for sem, name, src, c0, c1 in (("lu", "ut", T.u, 0, 512), ("lx", "xt", T.x, 0, 4 * CUT), ("ly", "xt", T.x, 4 * CUT, 1152)):
         dma(sem, T[name][:, c0:c1], src[:, c0:c1], [], [view(name, c0, c1)])
-    pf = [view("pf", k, k + 1) for k in range(9)]
-    kappa, group, kmid, klow, rest, rkc, basec, over, base0 = pf
+    pf = [view("pf", k, k + 1) for k in range(13)]
+    kappa, group, odd, kmid, klow, rest, rkc, basec, over, base0, hc0, hc1, hc2 = pf
     pi = [view("pi", k, k + 1) for k in range(4)]
     iota(pi[3], [[0, 1]], 0, 1, f=False)
     iota(view("ii", 0, 16), [[0, 2], [16, 8]], f=False)
     iota(view("i16", 0, 288), [[0, 18], [1, 16]])
     iota(view("gi", 0, 256), [[0, 2], [1, 8], [0, 16]])
     iota(view("i17", 0, 289), [[0, 17], [1, 17]])
-    iota(view("sgr", 0, 8), [[1, 8]], 1)
+    iota(view("cst", 24, 32), [[1, 8]], 1)
 
     fill(view("zer", 0, 1024), 0.0)
     ts(pi[0], pi[3], 15, OP.bitwise_and)
     ts(pi[1], pi[3], 4, OP.logical_shift_right)
-    fill(view("ones", 0, 256), 1.0)
+    ts(pi[2], pi[3], 4, OP.logical_shift_right, 1, OP.bitwise_and)
+    fill(view("ones", 0, 512), 1.0)
     tc(view("ul", 0, 16), view("ii", 0, 16))
-    tc(view("pf", 0, 2), view("pi", 0, 2))
+    tc(view("pf", 0, 3), view("pi", 0, 3))
     fill(view("neg", 0, 768), EMPTY)
-    zer = view("zer", 0, 1024)
-    for k in range(2):
-        dma("z0", T.zr[:, 1024 * k:1024 * k + 1024], zer[6], [zer], [view("zr", 1024 * k, 1024 * k + 1024)])
-    for k in range(4):
-        dma("z1", T.ef[:, 1024 * k:1024 * k + 1024], zer[6], [zer], [view("ef", 1024 * k, 1024 * k + 1024)])
-    dma("z2", T.rq[:, 0:800], T.zer[:, 0:800], [zer], [view("rq", 0, 800)])
+    for k, (name, c0, c1) in enumerate((("ml", 0, 1024), ("zr", 0, 1024), ("zr", 1024, 2048), ("ef", 0, 1024), ("ef", 1024, 2048), ("ef", 2048, 3072), ("ef", 3072, 4096), ("rq", 0, 800))):
+        spread("y%d" % k, name, c0, c1, "zer")
     dma("lw", T.w_q[:, 0:512].bitcast(dt.uint8), T.wc[:], [], [view("w_q", 0, 512)])
     dma("ls", T.w_s[:, 0:512], T.ws[:], [], [view("w_s", 0, 512)])
-    dma("lv", T.vt[:, 0:512], T.v[:], [], [view("vt", 0, 512)])
-    for r in range(3):
+
+    def empty(r):
         for k in range(3):
-            dma("z%d" % (3 + r), T["iw%d" % r][:, 768 * k:768 * k + 768], T.neg[:, 0:768], [view("neg", 0, 768)], [view("iw%d" % r, 768 * k, 768 * k + 768)])
+            spread("z%d" % r, "iw%d" % r, 768 * k, 768 * k + 768, "neg")
 
     def unpackers(hh):
         for h in hh:
             for t in range(4):
                 select(view("ef", 512 * h + 128 * t + t, 512 * h + 128 * t + 128, 4), view("ones", 0, 32), [[0, 2], [-1, 16]], -16 * h)
 
-    iota(view("ii", 32, 96), [[16, 8], [128, 4], [0, 2]], f=False)
+    iota(view("ii", 32, 64), [[32, 4], [128, 4], [16, 2]], f=False)
     select(view("idx", 0, 256), view("ones", 0, 256), [[0, 2], [-1, 128]], 0)
     iota(view("cval", 0, 288), [[1, 288]], -144, 0)
     unpackers([0])
@@ -248,45 +254,48 @@ def rank_program(g, core, T, topo):
     act(klow, kappa, ACT.Identity, 2.0 ** 17, -2.0 ** 16)
     act(rest, group, ACT.Identity, -1.0, 8.0)
     act(view("i16s", 0, 288), view("i16", 0, 288), ACT.Copy, 2.0 ** 17)
-    act(view("ml", 0, 1024), zer)
-    ts(view("pata", 0, 288), view("i16", 0, 288), kappa, OP.not_equal, BIG, OP.mult)
-    fill(view("rs", 0, 1), 0.0)
-    fill(view("wn", 0, 48), 0.0)
-    quant("ml", view("zer", 0, 640), 128, 288)
-    ts(view("patb", 0, 288), view("i16s", 0, 288), kmid, OP.subtract, -1.0e22, OP.mult)
-    ts(view("gx", 0, 256), view("gi", 0, 256), group, OP.is_equal)
-    quant("u", view("ut", 0, 512), 0, 128)
-    ts(view("patr", 0, 288), view("i16s", 0, 288), klow, OP.subtract, STEP, OP.min)
-    for f in pick("up", "u", 0, 256, 128, view("ul", 0, 16)):
-        f()
-    for t in range(4):
-        act(view("ob", t, 512, 4), view("gx", 0, 128))
     for a in range(8, 17):
         w0, w1 = ML[a // 4], ML[a // 4 + 1]
         if w0 + 16 * a + 16 < w1:
             act(view("ml", 4 * (w0 + 16 * a + 16) + a % 4, 4 * w1, 4), view("zer", 0, w1 - w0 - 16 * a - 16))
     act(view("ml", 4 * ML[4] + 3, 4 * ML[5], 4), view("zer", 0, 288))
     act(rkc, kappa, ACT.Identity, STEP, -15 * STEP - 1 - LOW)
+    ts(view("pata", 0, 288), view("i16", 0, 288), kappa, OP.not_equal, BIG, OP.mult)
+    fill(view("rs", 0, 1), 0.0)
+    fill(view("wn", 0, 48), 0.0)
+    quant("ml", view("zer", 0, 640), 128, 288)
+    ts(view("patb", 0, 288), view("i16s", 0, 288), kmid, OP.subtract, -1.0e22, OP.mult)
+    ts(view("gx", 0, 256), view("gi", 0, 256), group, OP.is_equal)
+    for t in range(4):
+        act(view("ob", t, 512, 4), view("gx", 0, 128))
+    ts(view("patr", 0, 288), view("i16s", 0, 288), klow, OP.subtract, STEP, OP.min)
+    quant("u", view("ut", 0, 512), 0, 128)
+    quant("x", view("xt", 0, 4 * CUT), 0, CUT)
+    for k in range(2):
+        for f in pick("up", "u", 128 * k, 128 * k + 128, 128, view("ul", 8 * k, 8 * k + 8)):
+            f()
     for z in range(4):
         for t in range(4):
             act(view("zr", 516 * z + 17 * t, 512 * z + 512, 64), view("gx", 0, 128, 16))
 
     def constants_2():
         ts(view("pats", 0, 288), view("i17", 0, 288), kappa, OP.is_equal, -BIG, OP.mult)
-        ts(view("cst", 0, 4), view("sgr", 0, 4), rest, OP.is_ge, -DELTA, OP.mult)
-        ts(view("cst", 4, 8), view("sgr", 4, 8), rest, OP.is_ge)
-        ts(view("cst", 16, 20), view("sgr", 0, 4), rest, OP.is_ge, 24.0, OP.mult)
-        ts(view("wl", 0, 64), view("ii", 32, 96), kappa, OP.add)
+        ts(view("cst", 0, 4), view("cst", 24, 28), rest, OP.is_ge, -DELTA, OP.mult)
+        ts(view("cst", 4, 8), view("cst", 28, 32), rest, OP.is_ge)
+        ts(view("cst", 16, 20), view("cst", 24, 28), rest, OP.is_ge, 24.0, OP.mult)
+        ts(view("wl", 0, 32), view("ii", 32, 64), kappa, OP.add)
         quant("zr", view("zr", 0, 1024), 0, 256)
 
     def constants_3():
+        act(view("cst", 8, 12), view("cst", 4, 8), ACT.Identity, -2.0, 1.0)
         act(view("cst", 12, 16), view("cst", 4, 8), ACT.Identity, 2.0, -1.0)
         act(view("cst", 20, 24), view("cst", 4, 8), ACT.Identity, 8.0, 16.0)
         for z in range(4):
             act(view("mc", 512 * z + 504, 512 * z + 512), view("zer", 0, 8))
         for name, src in (("rc", "idx"), ("cn", "gx")):
             for i in range(8):
-                o = view(name, 512 * (i // 4) + i % 4, 512 * (i // 4) + 512, 4)
+                j = (i + 1) % 7 if name == "cn" and i < 7 else i
+                o = view(name, 512 * (j // 4) + j % 4, 512 * (j // 4) + 512, 4)
                 act(o, view(src, 112 - 16 * i, 240 - 16 * i) if i < 7 else view("zer", 0, 128), ACT.Copy, view("cst", 8 + i, 9 + i) if name == "rc" and i > 3 else 1.0)
 
     def constants_4():
@@ -295,24 +304,30 @@ def rank_program(g, core, T, topo):
         act(view("mf", 1152 + 3, 2304, 4), view("zer", 0, 288))
         act(view("patc", 0, 288), view("patr", 0, 288))
         act(basec, over, ACT.Identity, 1.0, base0)
+        act(hc0, odd, ACT.Identity, -16.0, 592.0)
+        act(hc1, odd, ACT.Identity, -2336.0, 1184.0)
+        act(hc2, odd, ACT.Identity, 2336.0, -1183.5)
         for f in picks[:2]:
             f[1]()
 
     def constants_5():
+        for k, c in enumerate((0.0, 1.0, 1.0 / 32.0, -1.0, -32.0)):
+            act(view("hpat", k, 90, 5), view("zer", 0, 18), ACT.Identity, 1.0, c)
+        act(view("hb", 1, 90, 5), view("zer", 0, 18), ACT.Identity, 1.0, -M32)
+        for k, c in enumerate((-BIG, -576.0, -576.0, -576.0, 1440.0, -576.0, -576.0, -576.0)):
+            act(view("pat8", k, 288, 8, p1=32), view("zer", 0, 36, p1=32), ACT.Identity, 1.0, c)
+        act(view("hpat", 96, 186), view("ones", 0, 90))
+        for c in (0, 1168):
+            act(view("tz", c, c + 16), view("zer", 0, 16))
+        act(view("hpat", 96, 186, 5), view("zer", 0, 18))
         for f in picks[2:]:
             f[1]()
 
-    def patterns():
-        for k, c in enumerate((0.0, 1.0, 1.0 / 32.0, -1.0, -32.0)):
-            fill(view("hpat", k, 90, 5), c)
-
-    picks = [pick("wl", "w", 128 * h, 128 * h + 128, 512, view("wl", 8 * h, 8 * h + 8)) for h in range(8)]
+    picks = [pick("wl", "w", 128 * h, 128 * h + 128, 512, view("wl", 8 * h, 8 * h + 8)) for h in range(4)]
     efq = [lambda h=h: quant("ef", view("ef", 512 * h, 512 * h + 512), 128 * h, 128 * h + 128) for h in range(8)]
-    jobs = [lambda: quant("zr", view("zr", 1024, 2048), 256, 512),
-            lambda: [efq[0](), fill(view("hb", 1, 90, 5), -1.5 * 2.0 ** 28)], lambda: [efq[1](), efq[2]()], patterns,
-            lambda: [efq[3](), fill(view("pat8", 0, 288, p1=32), -576.0)],
-            lambda: quant("rc", view("rc", 0, 1024), 0, 256), lambda: quant("cn", view("cn", 0, 1024), 0, 256),
-            lambda: [efq[4](), fill(view("pat8", 0, 288, 8, p1=32), -BIG), fill(view("pat8", 4, 288, 8, p1=32), 1440.0)], efq[5], efq[6], efq[7]] + [f[0] for f in picks]
+    jobs = [lambda: quant("zr", view("zr", 1024, 2048), 256, 512), efq[0], lambda: [efq[1](), efq[2]()], efq[3], efq[4],
+            lambda: quant("rc", view("rc", 0, 1024), 0, 256), lambda: quant("cn", view("cn", 0, 1024), 0, 256), efq[5], efq[6], efq[7]]
+    jobs += [f[0] for f in picks] + [lambda k=k: quant("eu", view("eu", 1024 * k, 1024 * k + 1024), 256 * k, 256 * k + 256) for k in range(2)]
 
     def spare(n=1):
         for f in jobs[:n]:
@@ -349,53 +364,55 @@ def rank_program(g, core, T, topo):
             mm(1, C if first else w, "ob", 0, "ml", c0, first, last)
 
         mm(2, CUT, "up", 0, "x", 0)
-        first = scalars(2, 0, CUT)
+        first = [scalars(2, 0, 64), scalars(2, 64, CUT)]
         quant("x", view("xt", 4 * CUT, 1152), CUT, C)
-        first()
+        for f in first:
+            f()
         send(rnd, "arr%d" % rnd, "sent%d" % rnd, [(view("xp%d_%s" % (rnd, k), 0, C), view("x_" + k, 0, C)) for k in "qs"])
         if rnd == 0:
             unpackers(range(1, 8))
+            for q in range(4):
+                select(view("eu", 512 * q, 512 * q + 512), view("ones", 0, 512), [[-1000, 4], [-1, 32], [1000, 4]], -32 * q)
             quant("ob", view("ob", 0, 512), 0, 128)
         mm(1, C, "up", 0, "x", 0)
         mm(0, C, "up", 0, "x", 0)
-        act(view("ssb", 0, 288), ps(1, 0, 288))
         keeps = [unpack("fw", "x", h, 5 + h) for h in range(3 if rnd else 0)]
         for i in (1, 2):
             mm(SB[i], C, "up", 16 * (i + 1), "x", 0)
-        compare(range(0, 8), 2)
+        compare(range(0, AC - 2), 2)
         second = scalars(0, CUT, C)
-        compare(range(8, 10), 2)
+        compare(range(AC - 2, AC), 2)
         second()
-        rows(range(1, 10))
+        rows(range(1, AC))
+        for k, a in enumerate(BY_SCALAR):
+            act(view("dump", 288 * k, 288 * k + 16 * a), ps(1, 0, 16 * a), ACT.Sign, -1.0, scal(a))
         count(0, first=True)
         count(1)
         for k, a in enumerate(BY_SCALAR):
-            act(view("dump", 288 * k, 288 * k + 16 * a + 16), view("ssb", 0, 16 * a + 16), ACT.Sign, -1.0, scal(a))
-        for k, a in enumerate(BY_SCALAR):
             act(slot(a, 0, 16 * a), view("dump", 288 * k, 288 * k + 16 * a), ACT.Relu, acc=view("rs", a, a + 1))
-            act(slot(a, 16 * a, 16 * a + 16), view("dump", 288 * k + 16 * a, 288 * k + 16 * a + 16), ACT.Relu)
         mm(SB[0], C, "up", 16, "x", 0)
         compare(range(12, 16), 0)
         tt(view("ml", 4 * ML[4] + 2, 4 * ML[5], 4), ps(0, 0, 288), view("sc", 0, 288), OP.is_equal)
+        for a in BY_SCALAR:
+            ts(slot(a, 16 * a, 16 * a + 16), ps(0, 16 * a, 16 * a + 16), scal(a), OP.is_lt)
         count(3)
-        compare(range(10, 12), 0)
+        compare(range(AC, 12), 0)
         rows(range(12, 14))
         for a in BY_SCALAR:
             act(view("rs", a, a + 1), view("rs", a, a + 1), ACT.Identity, -1.0, 16.0 * a)
-        rows((14, 15, 10, 11))
+        rows([14, 15] + list(range(AC, 12)))
         count(4)
         count(2, last=True)
         act(view("patr", 15, 288, 16), view("rs", 0, 18), ACT.Identity, 1.0, rkc)
-        mm(SB[3], C, "up", 64, "x", 0)
+        act(view("ssb", 0, 288), ps(0, 0, 288))
         for k in keeps:
             k()
-        for i in (6, 4, 5):
+        for i in (6, 4, 5, 3):
             mm(SB[i], C, "up", 16 * (i + 1), "x", 0)
         if rnd == 0:
             constants_2()
-        act(view("s7", 0, 288), ps(SB[6], 0, 288))
-        if rnd == 0:
             constants_3()
+        act(view("s7", 0, 288), ps(SB[6], 0, 288))
 
     def places(rnd):
         rk = view("scr", 15, 288, 16)
@@ -405,23 +422,32 @@ def rank_program(g, core, T, topo):
         spare()
         scatter(view("sort", 0, 288), view("posl", 0, 18), view("ssb", 0, 288))
         spare()
+        settle("Y", [view("posl", 0, 18)], [])
+        empty(rnd)
+        if rnd == 1:
+            dma("lv", T.vt[:, 0:512], T.v[:], [], [view("vt", 0, 512)])
         scan(view("wr", 289, 305), view("pats", 0, 16), view("sort", 16, 288, 17), OP.add, OP.max)
         sp, runs = view("wr", 304, 305), view("wr", 15, 288, 17)
         scan(view("wr", 0, 288), view("pats", 0, 288), view("sort", 0, 288), OP.add, OP.max)
 
-        def sized(z):
+        def signs(z):
             for i in range(4, 7):
                 d = 216 * z + 72 * (i - 4)
                 act(view("dump", d, d + 72), ps(SB[i], z, 288, 4), ACT.Sign, -1.0, sp)
 
-        sized(0)
+        signs(0)
         for z in range(4):
             for i in range(4):
                 ts(view("mc", 512 * z + 72 * i, 512 * z + 72 * i + 72), ps(SB[i], z, 288, 4), sp, OP.subtract, view("cst", i, i + 1), OP.is_le)
-            if z < 3:
-                sized(z + 1)
+            if z < 2:
+                signs(z + 1)
+            if z == 0:
+                ts(view("dec", 20, 23), view("cst", 8, 11), sp, OP.mult)
             for i in range(4, 7):
                 d = 216 * z + 72 * (i - 4)
+                if z == 3:
+                    ts(view("mc", 512 * z + 72 * i, 512 * z + 72 * i + 72), ps(SB[i], z, 288, 4), view("cst", 4 + i, 5 + i), OP.mult, view("dec", 16 + i, 17 + i), OP.is_gt)
+                    continue
                 act(view("mc", 512 * z + 72 * i, 512 * z + 72 * i + 72), view("dump", d, d + 72), ACT.Relu, view("cst", 8 + i, 9 + i))
             if z == 3:
                 act(view("dec", 0, 17), runs, ACT.Abs, EPS, DELTA)
@@ -442,16 +468,16 @@ def rank_program(g, core, T, topo):
             ts(view("off", 18 * i, 18 * i + 18), ps(1, 18 * i, 18 * i + 18), view("cst", 8 + i, 9 + i) if i > 3 else 1.0, OP.mult, view("cst", 16 + i, 17 + i), OP.add)
 
         def cmp(i):
+            i = (i + 1) % 7
             return view("mf", 1152 * (i // 4) + i % 4, 1152 * (i // 4) + 1152, 4)
 
         fused(cmp(6), wn, view("off", 108, 126), view("s7", 0, 288), OP.is_ge)
+        for t in range(4):
+            w = 90 if t < 3 else 18
+            tc(view("rq", t, 4 * w, 4), ps(1, 18 * t, 18 * t + w))
         for i in range(5):
             r = view("rt", 288 * i, 288 * i + 288)
             fetch(r, wn, view("off", 18 * i, 18 * i + 18))
-            if i == 1:
-                for t in range(4):
-                    w = 90 if t < 3 else 18
-                    tc(view("rq", t, 4 * w, 4), ps(1, 18 * t, 18 * t + w))
             tt(cmp(i), r, ps(SB[i], 0, 288), OP.is_ge)
             if i in (0, 2):
                 spare()
@@ -460,19 +486,37 @@ def rank_program(g, core, T, topo):
                 for k in range(2):
                     mm(1, 128, "rc", 128 * k, "rq", 72 * k, k == 0, k == 1)
             if i == 3:
-                ts(view("base", 0, 18), ps(1, 0, 18), 17.0, OP.mult, basec, OP.add)
+                quant("mf", view("mf", 0, 1152), 0, 288)
+                for b, c0, c1 in PARTS:
+                    mm(b, c1 - c0, "cn", 0, "mf", c0, True, False)
+                ts(view("hx", 236, 254), ps(1, 0, 18), 17.0, OP.mult, basec, OP.add)
             if i == 4:
-                tt(view("patc", 15, 288, 16), view("base", 0, 18), rk, OP.add)
-        quant("mf", view("mf", 0, 1152), 0, 288)
-        for b, c0, c1 in PARTS:
-            mm(b, c1 - c0, "cn", 0, "mf", c0, True, False)
+                tt(view("patc", 15, 288, 16), view("hx", 236, 254), rk, OP.add)
         for b, c0, c1 in PARTS:
             fetch(view("rt", 1440 + c0, 1440 + c1), wn, view("off", 90 + c0 // 16, 90 + c1 // 16))
         for b, c0, c1 in PARTS:
-            tt(view("mf", 1153 + 4 * c0, 1152 + 4 * c1, 4), view("rt", 1440 + c0, 1440 + c1), ps(SB[5], c0, c1), OP.is_ge)
+            tt(view("mf", 1154 + 4 * c0, 1152 + 4 * c1, 4), view("rt", 1440 + c0, 1440 + c1), ps(SB[5], c0, c1), OP.is_ge)
         for b, c0, c1 in PARTS:
             quant("mf", view("mf", 1152 + 4 * c0, 1152 + 4 * c1), 288 + c0, 288 + c1)
             mm(b, c1 - c0, "cn", 128, "mf", 288 + c0, False, True)
+
+    def way_home(n, hb):
+        hx = [view("hx", k, 90, 5) for k in range(5)]
+        n4, n8 = view("hx", 96, 114), view("hx", 120, 138)
+
+        def cut(qq):
+            for a0, a1, c in ((0, AC, 0), (AC, 18, 4 * AC)):
+                for q in qq:
+                    tc(view("hl", c + (a1 - a0) * q, c + (a1 - a0) * (q + 1), p1=32), view("hx", 148 + 5 * a0, 144 + 5 * a1, 5, 32 * q, 32 * q + 32))
+
+        return [lambda: [ts(n4, n, LOW - 1.0, OP.add, M4, OP.add), ts(n8, n, LOW - 3.0, OP.add, M8, OP.add), ts(hx[4], n, 1151.25 - LOW, OP.is_ge, 288.0, OP.mult)],
+                lambda: [ts(hx[0], hb[2], hc1, OP.mult, hc0, OP.add), ts(hx[1], hb[3], hc2, OP.mult),
+                         ts(hx[2], n4, -M4, OP.add, 71.5, OP.mult), ts(hx[3], n8, -M8, OP.add, -71.75, OP.mult)],
+                lambda: None,
+                lambda: scan(view("hx", 144, 234), view("hpat", 96, 186), view("hx", 0, 90), OP.mult, OP.add),
+                lambda: cut((0, 1)), lambda: cut((2, 3)),
+                lambda: tc(view("hl", 0, 72, p0=32, p1=64), view("hl", 0, 72, p1=32)),
+                lambda: tc(view("hl", 0, 72, p0=64), view("hl", 0, 72, p1=64))]
 
     def seats(rnd):
         spare(3)
@@ -487,10 +531,11 @@ def rank_program(g, core, T, topo):
             scan(view("scn", c0, c1), ps(b, 0, c1 - c0), view("patc", c0, c1), OP.max, OP.add)
         spare()
         hb = [view("hb", k, 90, 5) for k in range(5)]
-        ts(hb[0], n, LOW - 15.0, OP.add, 1.5 * 2.0 ** 28, OP.add)
+        ts(hb[0], n, LOW - 15.0, OP.add, M32, OP.add)
         ts(hb[2], n, LOW, OP.add)
         for k in (3, 4):
-            ts(hb[k], n, LOW + 1.5 * 2.0 ** 24, OP.add, -1.5 * 2.0 ** 24, OP.add)
+            ts(hb[k], n, LOW + M2, OP.add, -M2, OP.add)
+        jobs.extend(way_home(n, hb))
         spare()
         scan(view("hs", 0, 90), view("hpat", 0, 90), view("hb", 0, 90), OP.mult, OP.add)
         spare()
@@ -519,69 +564,67 @@ def rank_program(g, core, T, topo):
 
     def half(k, win, lst):
         c0, win = 576 * k, view(win, 0, 2304)
-        steps = [lambda: [vfetch(view("ow", c0, c0 + 288), win, view(lst, 0, 18)), fetch(view("ow", c0 + 288, c0 + 576), win, view(lst, 18, 36))]]
+        steps = [lambda: [vfetch(view("ow", c0, c0 + 288), win, view(lst, 0, 18)), fetch(view("ow", c0 + 288, c0 + 576), win, view(lst, 18, 36)), spare()]]
         for n in range(16):
-            steps.append(lambda q=n // 4, t=n % 4, n=n: move("S" if n % 3 == 1 else "V", view("tt", c0 + t, c0 + 576, 4, 32 * q, 32 * q + 32), view("ow", c0 + q, c0 + 576, 4, 32 * t, 32 * t + 32)))
-        steps.append(lambda: quant("tb" if k else "ta", view("tt", c0, c0 + 576), 0, 144))
+            steps.append(lambda q=n // 4, t=n % 4, n=n: move("G" if n == 0 else "S" if n % 3 == 1 else "V", view("tt", c0 + t, c0 + 576, 4, 32 * q, 32 * q + 32), view("ow", c0 + q, c0 + 576, 4, 32 * t, 32 * t + 32)))
+        steps.append(lambda: [spare(k), quant("tb" if k else "ta", view("tt", c0, c0 + 576), 0, 144)])
         return steps
 
-    def layer(src, hf, between):
-        for h in range(8):
-            a, b = (2 * h) % 8, (2 * h + 1) % 8
-            mm(a, H, "wl", 128 * h, src, 0)
-            mm(b, H, "ef", 128 * h, src, 0)
-            r = view("rl", 1152 * hf + 144 * h, 1152 * hf + 144 * h + 144)
-            act(r, ps(a, 0, 144), ACT.Relu, 0.03125)
-            tt(view("tw", 1152 * hf + h, 1152 * hf + 1152, 8), ps(b, 0, 144), r, OP.add)
-            for f in between.get(h, ()):
-                f()
+    def layer(src, hf):
+        def product(q):
+            mm(2 * q, H, "wl", 128 * q, src, 0)
+            mm(2 * q + 1, H, "eu", 128 * q, src, 0)
+
+        r = [view("rl", 576 * hf + 144 * q, 576 * hf + 144 * q + 144) for q in range(4)]
+        o = [view("tw", 576 * hf + 288 * (q // 2) + q % 2, 576 * hf + 288 * (q // 2) + 288, 2) for q in range(4)]
+        return ([lambda q=q: product(q) for q in range(4)], [lambda q=q: act(r[q], ps(2 * q, 0, 144), ACT.Relu, 0.03125) for q in range(4)],
+                [lambda q=q: tt(o[q], ps(2 * q + 1, 0, 144), r[q], OP.add) for q in range(4)])
+
+    def swap(c0, c1, d0, d1):
+        return [lambda: turn(view("tz", 16 + c0, 16 + c1), view("tw", c0, c1)), lambda: turn(view("tw", 1152 + d0, 1152 + d1), view("tz", d0, d1))]
 
     def home():
-        win = view("tw", 0, 2304)
+        win = view("tw", 0, 2336)
         w0, w1 = CUT, C - CUT
-        vfetch(view("o2", 0, w0), win, view("hl", 0, 10))
+        vfetch(view("o2", 0, w0), win, view("hl", 0, AC))
         for q in range(1, 4):
-            fetch(view("o2", w0 * q, w0 * q + w0), win, view("hl", 10 * q, 10 * q + 10))
+            fetch(view("o2", w0 * q, w0 * q + w0), win, view("hl", AC * q, AC * q + AC))
         for q in (0, 2):
-            fetch(view("o2", 4 * w0 + w1 * q, 4 * w0 + w1 * q + 2 * w1), win, view("hl", 40 + 8 * q, 56 + 8 * q))
+            fetch(view("o2", 4 * w0 + w1 * q, 4 * w0 + w1 * q + 2 * w1), win, view("hl", 4 * AC + (18 - AC) * q, 4 * AC + (18 - AC) * (q + 2)))
         for n in range(16):
             q, t = n // 4, n % 4
-            tc(view("xt", t, 4 * w0, 4, 32 * q, 32 * q + 32), view("o2", w0 * q, w0 * q + w0, 1, 32 * t, 32 * t + 32))
+            move("G" if n in (3, 7) else "V", view("xt", t, 4 * w0, 4, 32 * q, 32 * q + 32), view("o2", w0 * q, w0 * q + w0, 1, 32 * t, 32 * t + 32))
         for n in range(16):
             q, t = n // 4, n % 4
-            move("S" if n > 11 else "V", view("xt", 4 * w0 + t, 1152, 4, 32 * q, 32 * q + 32), view("o2", 4 * w0 + w1 * q, 4 * w0 + w1 * q + w1, 1, 32 * t, 32 * t + 32))
+            move("G" if n == 3 else "S" if n > 11 else "V", view("xt", 4 * w0 + t, 1152, 4, 32 * q, 32 * q + 32), view("o2", 4 * w0 + w1 * q, 4 * w0 + w1 * q + w1, 1, 32 * t, 32 * t + 32))
             if n == 3:
                 quant("x", view("xt", 0, 4 * CUT), 0, CUT)
 
-    quant("x", view("xt", 0, 4 * CUT), 0, CUT)
+    def places_out():
+        fill(view("ntf", 18, 32), 0.0)
+        ts(view("ntf", 0, 18), view("scn", 15, 288, 16), LOW + 0.5, OP.add)
+        quant("v", view("vt", 0, 512), 0, 128)
+
+    def places_out2():
+        turn(view("ntf", 32, 64), view("ntf", 0, 32))
+        for gr in range(8):
+            v = view("ntf", 32 + 16 * (gr % 2), 48 + 16 * (gr % 2), 1, 32 * (gr // 2), 32 * (gr // 2) + 18)
+            dma("outd", T.pl[gr:gr + 1, :], v[6], [v], [])
+
     for rnd in range(3):
         local(rnd)
         places(rnd)
         seats(rnd)
+        if rnd == 2:
+            jobs.extend([places_out, places_out2])
         for f in half(1, "fw", "tl"):
             f()
-        spare(99)
-        lists = [lambda q=q, a0=a0, a1=a1, c=c: ts(view("hl", c + (a1 - a0) * q, c + (a1 - a0) * (q + 1), p1=32), view("scn", 16 * a0 + 15, 16 * a1, 16, 32 * q, 32 * q + 32), LOW + 0.5, OP.add)
-                 for a0, a1, c in ((0, 10, 0), (10, 18, 40)) for q in range(4)]
-        lists.append(lambda: tc(view("hl", 0, 72, p0=32, p1=64), view("hl", 0, 72, p1=32)))
-        lists.append(lambda: tc(view("hl", 0, 72, p0=64), view("hl", 0, 72, p1=64)))
         other = half(0, "fp", "lp%d" % rnd)
-        other[0]()
-        layer("tb", 1, {1: other[1:9], 2: other[9:17], 3: other[17:]})
-        last = {0: lists[:3], 1: lists[3:6], 2: lists[6:8], 3: lists[8:9], 4: lists[9:]}
-        if rnd == 2:
-            def places_out():
-                fill(view("ntf", 18, 32), 0.0)
-                ts(view("ntf", 0, 18), view("scn", 15, 288, 16), LOW + 0.5, OP.add)
-                quant("v", view("vt", 0, 512), 0, 128)
-
-            def places_out2():
-                turn(view("ntt", 0, 32), view("ntf", 0, 32))
-                for gr in range(8):
-                    v = view("ntt", 16 * (gr % 2), 16 * (gr % 2) + 16, 1, 32 * (gr // 2), 32 * (gr // 2) + 18)
-                    dma("outd", T.pl[gr:gr + 1, :], v[6], [v], [])
-            last[5], last[6] = [places_out], [places_out2]
-        layer("ta", 0, last)
+        (pb, rb, sb), (pa, ra, sa) = layer("tb", 1), layer("ta", 0)
+        one, end, mid, two = swap(576, 1152, 608, 896), swap(0, 0, 896, 1184), swap(0, 288, 0, 288), swap(288, 576, 288, 608)
+        for f in (pb + other[:1] + rb[:1] + other[1:17] + rb[1:] + sb[:1] + other[17:] + sb[1:] + [lambda: spare(99)] + pa + ra
+                  + one[:1] + sa + mid[:1] + one[1:] + two[:1] + mid[1:] + end[1:] + two[1:]):
+            f()
         home()
     mm(0, CUT, "v", 0, "x", 0)
     dma("outd", T.oc[:, 0:4 * CUT], T.x_q[:, 0:CUT].bitcast(dt.uint8), [view("x_q", 0, CUT)], [])

@@ -12,22 +12,24 @@ LOW = 8192.0
 EMPTY = -32768.0
 CUT = 160
 AC = CUT // 16
-LATE = 4
-PARTS = ((2, 0, CUT), (3, CUT, C))
-FREE = (4, 5, 7, 0, 1, 6)
+LATE = (6, 4, 4)
+PARTS = ((2, 0, CUT), (4, CUT, C))
+FREE = (5, 0, 3, 1, 6, 7)
 MASKS = [1, 2, 3]
-ML = [0, 128, 256, 448, 704, 992]
+ML = [128, 0, 192, 384, 640]
+MW = [64, 128, 192, 256, 288]
 BY_SCALAR = (17, 16)
 SB = [2, 3, 4, 0, 5, 6, 7]
+RB = (1, 3, 1)
 M2, M4, M8, M32 = [1.5 * 2.0 ** (23 + k) for k in (1, 2, 3, 5)]
 
 SCRATCH = {}
 for _t, _s in (
-        ("float32", "pf 16 i16 288 i16s 288 i17 296 gi 256 pata 288 patb 288 patr 288 patc 288 pats 288 pat8 288 cst 32 hpat 192 dm 288 sc 288 ssb 288 rs 24 scr 288 scn 288 sort 288 wr 312 dec 24 wn 48 s7 288 rt 1728 hb 96 hs 96 es 576 ntf 64 rl 1152 hx 256"),
+        ("float32", "pf 16 i16 288 i16s 288 i17 296 gi 256 pata 288 patb 288 patr 288 patc 288 pats 288 pat8 288 cst 32 hpat 192 dm 288 sc 288 ssb 288 rs 72 scr 288 scn 288 sort 288 wr 312 dec 24 wn 48 s7 288 rt 1728 hb 96 hs 96 es 576 ntf 64 rl 1152 hx 256"),
         ("int32", "pi 8 ii 96"),
         ("uint16", "ul 16 wl 32 posl 18 off 128 phl 18 tl 36 hl 72 ls0 36 ls1 36 ls2 36 lp0 36 lp1 36 lp2 36"),
-        ("bfloat16", "dump 1728 cval 288 ones 512 zer 1024 neg 768 gx 256 idx 256 ef 4096 ob 512 zr 2048 cn 1024 rc 1024 rq 800 xt 1152 ut 512 vt 512 ml 3968 mc 2048 mf 2304 iw0 2304 iw1 2304 iw2 2304 itr 2304 fw 2304 fp 2304 ow 1152 tt 1152 o2 1152 en 576 tw 2336 tz 1184 eu 2048"),
-        ("mx", "ef 1024 ob 128 zr 512 cn 256 rc 256 rq 200 u 128 v 128 up 256 w 512 wl 512 eu 512 x 288 ml 1152 mc 512 mf 576 ta 144 tb 144 xp0 288 xp1 288 xp2 288")):
+        ("bfloat16", "dump 2016 cval 576 ones 512 zer 1024 neg 768 gx 256 idx 256 ef 4096 ob 512 zr 2048 cn 1024 rc 1024 rq 584 xt 1152 ut 512 vt 512 ml 3968 mc 2016 mf 2304 iw0 2304 iw1 2304 iw2 2304 itr 2304 fw 2304 fp 2304 ow 1152 tt 1152 o2 1152 en 576 tw 2336 tz 1184 eu 2048"),
+        ("mx", "ef 1024 ob 128 zr 512 cn 256 rc 256 rq 146 u 128 v 128 up 256 w 512 wl 512 eu 512 x 288 ml 1152 mc 632 mf 576 ta 144 tb 144 xp0 288 xp1 288 xp2 288")):
     _s = _s.split()
     for _n, _w in zip(_s[::2], _s[1::2]):
         if _t == "mx":
@@ -213,7 +215,7 @@ def rank_program(g, core, T, topo):
                 lambda: fetch(o2, i2, off))
 
     for sem, name, src, c0, c1 in (("lu", "ut", T.u, 0, 512), ("lx", "xt", T.x, 0, 4 * CUT), ("ly", "xt", T.x, 4 * CUT, 1152)):
-        dma(sem, T[name][:, c0:c1], src[:, c0:c1], [], [view(name, c0, c1)])
+        dma(sem, T[name][:, c0:c1], src[:, c0:c1], [], [view(name, c0, c1)], "S" if name == "ut" else "Y")
     pf = [view("pf", k, k + 1) for k in range(13)]
     kappa, group, odd, kmid, klow, rest, rkc, basec, over, base0, hc0, hc1, hc2 = pf
     pi = [view("pi", k, k + 1) for k in range(4)]
@@ -228,11 +230,13 @@ def rank_program(g, core, T, topo):
     ts(pi[0], pi[3], 15, OP.bitwise_and)
     ts(pi[1], pi[3], 4, OP.logical_shift_right)
     ts(pi[2], pi[3], 4, OP.logical_shift_right, 1, OP.bitwise_and)
-    fill(view("ones", 0, 512), 1.0)
     tc(view("ul", 0, 16), view("ii", 0, 16))
+    fill(view("cval", 288, 576), 1.0)
+    fill(view("rs", 0, 1), 0.0)
+    fill(view("wn", 0, 48), 0.0)
     tc(view("pf", 0, 3), view("pi", 0, 3))
-    fill(view("neg", 0, 768), EMPTY)
-    for k, (name, c0, c1) in enumerate((("ml", 0, 1024), ("zr", 0, 1024), ("zr", 1024, 2048), ("ef", 0, 1024), ("ef", 1024, 2048), ("ef", 2048, 3072), ("ef", 3072, 4096), ("rq", 0, 800))):
+    act(view("ones", 0, 512), view("zer", 0, 512), ACT.Identity, 1.0, 1.0)
+    for k, (name, c0, c1) in enumerate((("zr", 0, 1024), ("zr", 1024, 2048), ("ml", 0, 768), ("ef", 0, 1024), ("ef", 1024, 2048), ("ef", 2048, 3072), ("ef", 3072, 4096), ("rq", 0, 584))):
         spread("y%d" % k, name, c0, c1, "zer")
     dma("lw", T.w_q[:, 0:512].bitcast(dt.uint8), T.wc[:], [], [view("w_q", 0, 512)])
     dma("ls", T.w_s[:, 0:512], T.ws[:], [], [view("w_s", 0, 512)])
@@ -241,74 +245,71 @@ def rank_program(g, core, T, topo):
         for k in range(3):
             spread("z%d" % r, "iw%d" % r, 768 * k, 768 * k + 768, "neg")
 
-    def unpackers(hh):
-        for h in hh:
-            for t in range(4):
-                select(view("ef", 512 * h + 128 * t + t, 512 * h + 128 * t + 128, 4), view("ones", 0, 32), [[0, 2], [-1, 16]], -16 * h)
-
     iota(view("ii", 32, 64), [[32, 4], [128, 4], [16, 2]], f=False)
     select(view("idx", 0, 256), view("ones", 0, 256), [[0, 2], [-1, 128]], 0)
     iota(view("cval", 0, 288), [[1, 288]], -144, 0)
-    unpackers([0])
-    act(kmid, kappa, ACT.Identity, 2.0 ** 17, 2.0 ** 16)
+    iota(view("mf", 1152 + 3, 2304, 4), [[0, 288]], 0, 0)
+    for h in range(8):
+        for t in range(4):
+            select(view("ef", 512 * h + 128 * t + t, 512 * h + 128 * t + 128, 4), view("ones", 0, 32), [[0, 2], [-1, 16]], -16 * h)
+    fill(view("cval", 288, 576, 16), 0.0)
+    quant("ml", view("zer", 0, 896), 192, 416)
+    ts(kmid, kappa, 0.5, OP.add)
+    ts(view("pata", 0, 288), view("i16", 0, 288), kappa, OP.not_equal, -BIG, OP.mult)
+    ts(view("patb", 0, 288), view("i16", 0, 288), kmid, OP.subtract, 1.0e27, OP.mult)
     act(klow, kappa, ACT.Identity, 2.0 ** 17, -2.0 ** 16)
     act(rest, group, ACT.Identity, -1.0, 8.0)
+    act(rkc, kappa, ACT.Identity, STEP - 1, 15 - 15 * STEP - LOW)
     act(view("i16s", 0, 288), view("i16", 0, 288), ACT.Copy, 2.0 ** 17)
-    for a in range(8, 17):
-        w0, w1 = ML[a // 4], ML[a // 4 + 1]
-        if w0 + 16 * a + 16 < w1:
-            act(view("ml", 4 * (w0 + 16 * a + 16) + a % 4, 4 * w1, 4), view("zer", 0, w1 - w0 - 16 * a - 16))
-    act(view("ml", 4 * ML[4] + 3, 4 * ML[5], 4), view("zer", 0, 288))
-    act(rkc, kappa, ACT.Identity, STEP, -15 * STEP - 1 - LOW)
-    ts(view("pata", 0, 288), view("i16", 0, 288), kappa, OP.not_equal, BIG, OP.mult)
-    fill(view("rs", 0, 1), 0.0)
-    fill(view("wn", 0, 48), 0.0)
-    quant("ml", view("zer", 0, 640), 128, 288)
-    ts(view("patb", 0, 288), view("i16s", 0, 288), kmid, OP.subtract, -1.0e22, OP.mult)
-    ts(view("gx", 0, 256), view("gi", 0, 256), group, OP.is_equal)
-    for t in range(4):
-        act(view("ob", t, 512, 4), view("gx", 0, 128))
-    ts(view("patr", 0, 288), view("i16s", 0, 288), klow, OP.subtract, STEP, OP.min)
+    for a in range(8, 18):
+        w0, w1 = ML[a // 4], ML[a // 4] + MW[a // 4]
+        act(view("ml", 4 * (w0 + 16 * a) + a % 4, 4 * w1, 4), view("zer", 0, w1 - w0 - 16 * a))
+    act(view("ml", 4 * ML[4] + 3, 4 * ML[4] + 1152, 4), view("zer", 0, 288))
     quant("u", view("ut", 0, 512), 0, 128)
     quant("x", view("xt", 0, 4 * CUT), 0, CUT)
     for k in range(2):
         for f in pick("up", "u", 128 * k, 128 * k + 128, 128, view("ul", 8 * k, 8 * k + 8)):
             f()
-    for z in range(4):
-        for t in range(4):
-            act(view("zr", 516 * z + 17 * t, 512 * z + 512, 64), view("gx", 0, 128, 16))
+        if k == 0:
+            ts(view("gx", 0, 256), view("gi", 0, 256), group, OP.is_equal)
+    ts(view("patr", 0, 288), view("i16s", 0, 288), klow, OP.subtract, STEP, OP.min)
+    act(view("rs", 48, 64), view("zer", 0, 16), ACT.Identity, 1.0, rkc)
+    for a in BY_SCALAR:
+        act(view("rs", 48 + a, 49 + a), rkc, ACT.Identity, 1.0, 16.0 * a)
+    for t in range(4):
+        act(view("ob", t, 512, 4), view("gx", 0, 128))
+
+    def shifted(name, src, ii):
+        for i in ii:
+            j = i if name == "cn" or i < 3 else i + 1 if i < 7 else 3
+            o = view(name, 512 * (j // 4) + j % 4, 512 * (j // 4) + 512, 4)
+            act(o, view(src, 112 - 16 * i, 240 - 16 * i) if i < 7 else view("zer", 0, 128), ACT.Copy, view("cst", 8 + i, 9 + i) if name == "rc" and i > 3 else 1.0)
+
+    def constants_1():
+        for z in range(4):
+            for t in range(4):
+                act(view("zr", 516 * z + 17 * t, 512 * z + 512, 64), view("gx", 0, 128, 16))
 
     def constants_2():
-        ts(view("pats", 0, 288), view("i17", 0, 288), kappa, OP.is_equal, -BIG, OP.mult)
         ts(view("cst", 0, 4), view("cst", 24, 28), rest, OP.is_ge, -DELTA, OP.mult)
         ts(view("cst", 4, 8), view("cst", 28, 32), rest, OP.is_ge)
         ts(view("cst", 16, 20), view("cst", 24, 28), rest, OP.is_ge, 24.0, OP.mult)
         ts(view("wl", 0, 32), view("ii", 32, 64), kappa, OP.add)
-        quant("zr", view("zr", 0, 1024), 0, 256)
 
     def constants_3():
-        act(view("cst", 8, 12), view("cst", 4, 8), ACT.Identity, -2.0, 1.0)
         act(view("cst", 12, 16), view("cst", 4, 8), ACT.Identity, 2.0, -1.0)
         act(view("cst", 20, 24), view("cst", 4, 8), ACT.Identity, 8.0, 16.0)
-        for z in range(4):
-            act(view("mc", 512 * z + 504, 512 * z + 512), view("zer", 0, 8))
-        for name, src in (("rc", "idx"), ("cn", "gx")):
-            for i in range(8):
-                j = (i + 1) % 7 if name == "cn" and i < 7 else i
-                o = view(name, 512 * (j // 4) + j % 4, 512 * (j // 4) + 512, 4)
-                act(o, view(src, 112 - 16 * i, 240 - 16 * i) if i < 7 else view("zer", 0, 128), ACT.Copy, view("cst", 8 + i, 9 + i) if name == "rc" and i > 3 else 1.0)
+        shifted("cn", "gx", range(8))
+        shifted("rc", "idx", range(8))
 
     def constants_4():
         act(base0, kappa, ACT.Identity, STEP, -15 * STEP - 0.5)
         act(over, group, ACT.Relu, 272.0, -4 * 272.0)
-        act(view("mf", 1152 + 3, 2304, 4), view("zer", 0, 288))
         act(view("patc", 0, 288), view("patr", 0, 288))
         act(basec, over, ACT.Identity, 1.0, base0)
         act(hc0, odd, ACT.Identity, -16.0, 592.0)
         act(hc1, odd, ACT.Identity, -2336.0, 1184.0)
         act(hc2, odd, ACT.Identity, 2336.0, -1183.5)
-        for f in picks[:2]:
-            f[1]()
 
     def constants_5():
         for k, c in enumerate((0.0, 1.0, 1.0 / 32.0, -1.0, -32.0)):
@@ -320,14 +321,15 @@ def rank_program(g, core, T, topo):
         for c in (0, 1168):
             act(view("tz", c, c + 16), view("zer", 0, 16))
         act(view("hpat", 96, 186, 5), view("zer", 0, 18))
-        for f in picks[2:]:
+        for f in picks:
             f[1]()
 
     picks = [pick("wl", "w", 128 * h, 128 * h + 128, 512, view("wl", 8 * h, 8 * h + 8)) for h in range(4)]
     efq = [lambda h=h: quant("ef", view("ef", 512 * h, 512 * h + 512), 128 * h, 128 * h + 128) for h in range(8)]
-    jobs = [lambda: quant("zr", view("zr", 1024, 2048), 256, 512), efq[0], lambda: [efq[1](), efq[2]()], efq[3], efq[4],
-            lambda: quant("rc", view("rc", 0, 1024), 0, 256), lambda: quant("cn", view("cn", 0, 1024), 0, 256), efq[5], efq[6], efq[7]]
-    jobs += [f[0] for f in picks] + [lambda k=k: quant("eu", view("eu", 1024 * k, 1024 * k + 1024), 256 * k, 256 * k + 256) for k in range(2)]
+    jobs = [lambda: quant("zr", view("zr", 0, 1024), 0, 256), lambda: quant("zr", view("zr", 1024, 2048), 256, 512), lambda: [efq[0](), quant("mc", view("zer", 0, 512), 0, 128)],
+            lambda: quant("rc", view("rc", 0, 1024), 0, 256), lambda: quant("cn", view("cn", 0, 1024), 0, 256)] + efq[1:]
+    jobs += [f[0] for f in picks]
+    euq = [lambda k=k: quant("eu", view("eu", 1024 * k, 1024 * k + 1024), 256 * k, 256 * k + 256) for k in range(2)]
 
     def spare(n=1):
         for f in jobs[:n]:
@@ -340,7 +342,7 @@ def rank_program(g, core, T, topo):
 
     def scalars(bank, c0, c1):
         tt(view("dm", c0, c1), ps(bank, c0, c1), view("pata", c0, c1), OP.add)
-        return lambda: scan(view("sc", c0, c1), view("patb", c0, c1), view("dm", c0, c1), OP.max, OP.min)
+        return lambda: scan(view("sc", c0, c1), view("patb", c0, c1), view("dm", c0, c1), OP.min, OP.max)
 
     def slot(a, c0, c1):
         return view("ml", 4 * (ML[a // 4] + c0) + a % 4, 4 * (ML[a // 4] + c1), 4)
@@ -349,18 +351,24 @@ def rank_program(g, core, T, topo):
         return view("sc", 16 * a + 15, 16 * a + 16)
 
     def local(rnd):
+        ring = [864]
+
         def compare(aa, bank):
             for a in aa:
-                ts(slot(a, 0, 16 * a + 16), ps(bank, 0, 16 * a + 16), scal(a), OP.is_lt)
+                ts(slot(a, 0, 16 * a), ps(bank, 0, 16 * a), scal(a), OP.is_lt)
 
         def rows(aa):
             for a in aa:
-                d = 864 + 288 * (a % 3)
+                d = ring[0] if ring[0] + 16 * a <= 1728 else 864
+                ring[0] = d + 16 * a
                 act(view("dump", d, d + 16 * a), slot(a, 0, 16 * a), ACT.Identity, -1.0, 1.0, acc=view("rs", a, a + 1))
 
         def count(al, first=False, last=False):
-            c0, w = ML[al] + (160 if al else 0), ML[al + 1] - ML[al]
-            quant("ml", view("ml", 4 * ML[al], 4 * ML[al + 1]), c0, c0 + w)
+            c0, w = ML[al] + (224 if al > 1 else 0), MW[al]
+            if al == 0:
+                quant("ml", view("ml", 0, 768), 0, 192)
+            if al > 1:
+                quant("ml", view("ml", 4 * ML[al], 4 * ML[al] + 4 * w), c0, c0 + w)
             mm(1, C if first else w, "ob", 0, "ml", c0, first, last)
 
         mm(2, CUT, "up", 0, "x", 0)
@@ -370,49 +378,55 @@ def rank_program(g, core, T, topo):
             f()
         send(rnd, "arr%d" % rnd, "sent%d" % rnd, [(view("xp%d_%s" % (rnd, k), 0, C), view("x_" + k, 0, C)) for k in "qs"])
         if rnd == 0:
-            unpackers(range(1, 8))
+            iota(view("neg", 0, 768), [[0, 768]], int(EMPTY), 0)
+            constants_1()
             for q in range(4):
                 select(view("eu", 512 * q, 512 * q + 512), view("ones", 0, 512), [[-1000, 4], [-1, 32], [1000, 4]], -32 * q)
-            quant("ob", view("ob", 0, 512), 0, 128)
         mm(1, C, "up", 0, "x", 0)
         mm(0, C, "up", 0, "x", 0)
         keeps = [unpack("fw", "x", h, 5 + h) for h in range(3 if rnd else 0)]
         for i in (1, 2):
             mm(SB[i], C, "up", 16 * (i + 1), "x", 0)
-        compare(range(0, AC - 2), 2)
+        compare((3, 2, 1, 7, 6, 5, 4), 2)
         second = scalars(0, CUT, C)
-        compare(range(AC - 2, AC), 2)
+        compare((9, 8), 2)
         second()
-        rows(range(1, AC))
+        rows((3, 2, 1, 7, 6, 5, 4, 9, 8))
         for k, a in enumerate(BY_SCALAR):
             act(view("dump", 288 * k, 288 * k + 16 * a), ps(1, 0, 16 * a), ACT.Sign, -1.0, scal(a))
+        if rnd == 0:
+            quant("ob", view("ob", 0, 512), 0, 128)
         count(0, first=True)
         count(1)
         for k, a in enumerate(BY_SCALAR):
             act(slot(a, 0, 16 * a), view("dump", 288 * k, 288 * k + 16 * a), ACT.Relu, acc=view("rs", a, a + 1))
         mm(SB[0], C, "up", 16, "x", 0)
         compare(range(12, 16), 0)
-        tt(view("ml", 4 * ML[4] + 2, 4 * ML[5], 4), ps(0, 0, 288), view("sc", 0, 288), OP.is_equal)
-        for a in BY_SCALAR:
-            ts(slot(a, 16 * a, 16 * a + 16), ps(0, 16 * a, 16 * a + 16), scal(a), OP.is_lt)
+        inside = view("ml", 4 * ML[4] + 2, 4 * ML[4] + 1152, 4)
+        tt(inside, ps(0, 0, 288), view("sc", 0, 288), OP.is_le)
         count(3)
-        compare(range(AC, 12), 0)
-        rows(range(12, 14))
-        for a in BY_SCALAR:
-            act(view("rs", a, a + 1), view("rs", a, a + 1), ACT.Identity, -1.0, 16.0 * a)
-        rows([14, 15] + list(range(AC, 12)))
+        scan(view("dump", 1728, 2016), view("cval", 288, 576), inside, OP.mult, OP.add)
+        compare((10, 11), 0)
+        rows((12, 13, 14, 15, 10, 11))
+        tt(view("rs", 24, 42), view("rs", 48, 66), view("dump", 1743, 2016, 16), OP.subtract)
         count(4)
         count(2, last=True)
-        act(view("patr", 15, 288, 16), view("rs", 0, 18), ACT.Identity, 1.0, rkc)
+        tt(view("patr", 271, 288, 16), view("rs", 40, 42), view("rs", 16, 18), OP.subtract)
+        if rnd == 0:
+            constants_2()
+        tt(view("patr", 15, 256, 16), view("rs", 0, 16), view("rs", 24, 40), OP.add)
+        if rnd == 0:
+            ts(view("pats", 0, 288), view("i17", 0, 288), kappa, OP.is_equal, -BIG, OP.mult)
         act(view("ssb", 0, 288), ps(0, 0, 288))
         for k in keeps:
             k()
-        for i in (6, 4, 5, 3):
+        for i in (4, 5, 6, 3):
             mm(SB[i], C, "up", 16 * (i + 1), "x", 0)
         if rnd == 0:
-            constants_2()
             constants_3()
-        act(view("s7", 0, 288), ps(SB[6], 0, 288))
+        act(view("s7", 0, 288), ps(SB[1], 0, 288))
+        if rnd == 0:
+            constants_4()
 
     def places(rnd):
         rk = view("scr", 15, 288, 16)
@@ -427,75 +441,101 @@ def rank_program(g, core, T, topo):
         if rnd == 1:
             dma("lv", T.vt[:, 0:512], T.v[:], [], [view("vt", 0, 512)])
         scan(view("wr", 289, 305), view("pats", 0, 16), view("sort", 16, 288, 17), OP.add, OP.max)
-        sp, runs = view("wr", 304, 305), view("wr", 15, 288, 17)
+        sp, runs, wn = view("wr", 304, 305), view("wr", 15, 288, 17), view("wn", 0, 48)
         scan(view("wr", 0, 288), view("pats", 0, 288), view("sort", 0, 288), OP.add, OP.max)
 
-        def signs(z):
-            for i in range(4, 7):
-                d = 216 * z + 72 * (i - 4)
-                act(view("dump", d, d + 72), ps(SB[i], z, 288, 4), ACT.Sign, -1.0, sp)
+        def cell(i, z):
+            k = min(i // 2, 2)
+            c = 576 * k + (216 if k == 2 else 144) * z + 72 * (i - 2 * k)
+            return view("mc", c, c + 72)
 
-        signs(0)
-        for z in range(4):
-            for i in range(4):
-                ts(view("mc", 512 * z + 72 * i, 512 * z + 72 * i + 72), ps(SB[i], z, 288, 4), sp, OP.subtract, view("cst", i, i + 1), OP.is_le)
-            if z < 2:
-                signs(z + 1)
-            if z == 0:
-                ts(view("dec", 20, 23), view("cst", 8, 11), sp, OP.mult)
-            for i in range(4, 7):
-                d = 216 * z + 72 * (i - 4)
-                if z == 3:
-                    ts(view("mc", 512 * z + 72 * i, 512 * z + 72 * i + 72), ps(SB[i], z, 288, 4), view("cst", 4 + i, 5 + i), OP.mult, view("dec", 16 + i, 17 + i), OP.is_gt)
-                    continue
-                act(view("mc", 512 * z + 72 * i, 512 * z + 72 * i + 72), view("dump", d, d + 72), ACT.Relu, view("cst", 8 + i, 9 + i))
-            if z == 3:
-                act(view("dec", 0, 17), runs, ACT.Abs, EPS, DELTA)
-                act(view("wn", 0, 17), runs)
-            if z == 2:
-                spare()
-            for y in ([z - 2] if 1 < z < 3 else [1, 2, 3] if z == 3 else []):
-                quant("mc", view("mc", 512 * y, 512 * y + 512), 128 * y, 128 * y + 128)
-                mm(1, 128, "zr", 128 * y, "mc", 128 * y, y == 0, y == 3)
-                if y == 1:
-                    spare()
-        tt(view("wn", 24, 41), runs, view("dec", 0, 17), OP.subtract)
-        spare(2)
-        if rnd == 0:
-            constants_4()
-        wn = view("wn", 0, 48)
-        for i in (0, 6, 1, 2, 3, 4, 5):
-            ts(view("off", 18 * i, 18 * i + 18), ps(1, 18 * i, 18 * i + 18), view("cst", 8 + i, 9 + i) if i > 3 else 1.0, OP.mult, view("cst", 16 + i, 17 + i), OP.add)
+        def scores(i, z):
+            return view("s7", z, 288, 4) if i == 1 else ps(SB[i], z, 288, 4)
+
+        def below(i):
+            for z in range(4):
+                ts(cell(i, z), scores(i, z), sp, OP.subtract, view("cst", i, i + 1), OP.is_le)
+
+        def signs(i):
+            for z in range(4):
+                act(view("dump", 288 * (i - 4) + 72 * z, 288 * (i - 4) + 72 * z + 72), scores(i, z), ACT.Sign, -1.0, sp)
+
+        def ones(i):
+            for z in range(4):
+                act(cell(i, z), view("dump", 288 * (i - 4) + 72 * z, 288 * (i - 4) + 72 * z + 72), ACT.Relu, view("cst", 8 + i, 9 + i))
+
+        def count(k):
+            w, c0 = 54 if k == 2 else 36, 144 * k
+            quant("mc", view("mc", 4 * c0, 4 * c0 + 16 * w), 128 + c0, 128 + c0 + 4 * w)
+            for z in range(4):
+                mm(RB[k], 128, "zr", 128 * z, "mc", c0 + w * (z + 1), z == 0, z == 3)
+
+        def number(i):
+            k = min(i // 2, 2)
+            c = 18 * (i - 2 * k) + (74 if k == 2 else 92)
+            return ps(RB[k], c, c + 18)
+
+        def offsets(ii):
+            for i in ii:
+                ts(view("off", 18 * i, 18 * i + 18), number(i), view("cst", 8 + i, 9 + i) if i > 3 else 1.0, OP.mult, view("cst", 16 + i, 17 + i), OP.add)
+
+        def numbers(ii):
+            for i in ii:
+                j = i if i < 3 else 69 + i
+                tc(view("rq", j, j + 72, 4), number(i))
 
         def cmp(i):
-            i = (i + 1) % 7
             return view("mf", 1152 * (i // 4) + i % 4, 1152 * (i // 4) + 1152, 4)
 
-        fused(cmp(6), wn, view("off", 108, 126), view("s7", 0, 288), OP.is_ge)
-        for t in range(4):
-            w = 90 if t < 3 else 18
-            tc(view("rq", t, 4 * w, 4), ps(1, 18 * t, 18 * t + w))
-        for i in range(5):
+        def against(i):
             r = view("rt", 288 * i, 288 * i + 288)
             fetch(r, wn, view("off", 18 * i, 18 * i + 18))
             tt(cmp(i), r, ps(SB[i], 0, 288), OP.is_ge)
-            if i in (0, 2):
-                spare()
-            if i == 1:
-                quant("rq", view("rq", 0, 800), 0, 200)
-                for k in range(2):
-                    mm(1, 128, "rc", 128 * k, "rq", 72 * k, k == 0, k == 1)
-            if i == 3:
-                quant("mf", view("mf", 0, 1152), 0, 288)
-                for b, c0, c1 in PARTS:
-                    mm(b, c1 - c0, "cn", 0, "mf", c0, True, False)
-                ts(view("hx", 236, 254), ps(1, 0, 18), 17.0, OP.mult, basec, OP.add)
-            if i == 4:
-                tt(view("patc", 15, 288, 16), view("hx", 236, 254), rk, OP.add)
+
+        signs(4)
+        act(view("dec", 0, 17), runs, ACT.Abs, EPS, DELTA)
+        signs(5)
+        act(view("wn", 0, 17), runs)
+        ones(4)
+        signs(6)
+        ones(5)
+        ones(6)
+        below(0)
+        below(1)
+        below(2)
+        count(0)
+        below(3)
+        tt(view("wn", 24, 41), runs, view("dec", 0, 17), OP.subtract)
+        spare()
+        count(1)
+        spare()
+        offsets((0, 1))
+        numbers((0, 1))
+        count(2)
+        spare()
+        offsets((2, 3))
+        fused(cmp(1), wn, view("off", 18, 36), view("s7", 0, 288), OP.is_ge)
+        numbers((2, 3))
+        against(0)
+        offsets((4, 5, 6))
+        numbers((4, 5, 6))
+        against(2)
+        quant("rq", view("rq", 0, 584), 0, 146)
+        for k in range(2):
+            mm(RB[1], 128, "rc", 128 * k, "rq", 18 * k, k == 0, k == 1)
+        against(3)
+        against(4)
+        quant("mf", view("mf", 0, 1152), 0, 288)
         for b, c0, c1 in PARTS:
-            fetch(view("rt", 1440 + c0, 1440 + c1), wn, view("off", 90 + c0 // 16, 90 + c1 // 16))
+            mm(b, c1 - c0, "cn", 0, "mf", c0, True, False)
+        ts(view("hx", 236, 254), ps(RB[1], 0, 18), 17.0, OP.mult, basec, OP.add)
+        against(5)
         for b, c0, c1 in PARTS:
-            tt(view("mf", 1154 + 4 * c0, 1152 + 4 * c1, 4), view("rt", 1440 + c0, 1440 + c1), ps(SB[5], c0, c1), OP.is_ge)
+            fetch(view("rt", 288 + c0, 288 + c1), wn, view("off", 108 + c0 // 16, 108 + c1 // 16))
+        for b, c0, c1 in PARTS:
+            tt(view("mf", 1154 + 4 * c0, 1152 + 4 * c1, 4), view("rt", 288 + c0, 288 + c1), ps(SB[6], c0, c1), OP.is_ge)
+        tt(view("patc", 15, 288, 16), view("hx", 236, 254), rk, OP.add)
+        spare()
         for b, c0, c1 in PARTS:
             quant("mf", view("mf", 1152 + 4 * c0, 1152 + 4 * c1), 288 + c0, 288 + c1)
             mm(b, c1 - c0, "cn", 128, "mf", 288 + c0, False, True)
@@ -519,12 +559,12 @@ def rank_program(g, core, T, topo):
                 lambda: tc(view("hl", 0, 72, p0=64), view("hl", 0, 72, p1=64))]
 
     def seats(rnd):
-        spare(3)
+        spare(5)
         if rnd == 0:
             constants_5()
         todo = [("fw", "x", h) for h in range(3 if rnd else 0, 8)] + [("fp", "xp%d" % rnd, h) for h in range(8)]
-        late = todo[-LATE:]
-        for n, (d, s, h) in enumerate(todo[:-LATE]):
+        late = todo[-LATE[rnd]:]
+        for n, (d, s, h) in enumerate(todo[:-LATE[rnd]]):
             unpack(d, s, h, FREE[n % 6])()
         n = view("scn", 15, 288, 16)
         for b, c0, c1 in PARTS:
@@ -535,7 +575,8 @@ def rank_program(g, core, T, topo):
         ts(hb[2], n, LOW, OP.add)
         for k in (3, 4):
             ts(hb[k], n, LOW + M2, OP.add, -M2, OP.add)
-        jobs.extend(way_home(n, hb))
+        way = way_home(n, hb)
+        jobs.extend(way if rnd else way[:2] + [lambda: [way[3](), euq[0]()], euq[1], way[4], way[2]] + way[5:])
         spare()
         scan(view("hs", 0, 90), view("hpat", 0, 90), view("hb", 0, 90), OP.mult, OP.add)
         spare()
@@ -544,22 +585,37 @@ def rank_program(g, core, T, topo):
         iw = "iw%d" % rnd
         scatter(view(iw, 0, 2304), view("phl", 0, 18), view("cval", 0, 288))
         spare()
-        for k in (0, 1):
-            turn(view("itr", 1152 * k, 1152 * k + 1152), view(iw, 1152 * k, 1152 * k + 1152))
-        spare()
         keeps = [unpack(d, s, h, FREE[(n + 2) % 6]) for n, (d, s, h) in enumerate(late)]
-        for k in (0, 1):
+
+        def turned(c0, c1):
+            turn(view("itr", c0, c1), view(iw, c0, c1))
+
+        def entries(k, v=0):
             for q in range(4):
-                move("V" if q < 2 * k else "S", view("en", 288 * k + q, 288 * k + 288, 4, p1=32), view("itr", 1152 * k, 1152 * k + 1152, 16, 32 * q, 32 * q + 32))
-        for f in keeps:
-            f()
-        for k in (0, 1):
-            scan(view("es", 288 * k, 288 * k + 288, p1=32), view("pat8", 0, 288, p1=32), view("en", 288 * k, 288 * k + 288, p1=32), OP.add, OP.max)
-        for k, name in ((0, "ls%d" % rnd), (1, "tl")):
+                move("V" if q < v else "S", view("en", 144 * k + q, 144 * k + 144, 4, p1=32), view("itr", 576 * k, 576 * k + 576, 16, 32 * q, 32 * q + 32))
+
+        def largest(k):
+            scan(view("es", 144 * k, 144 * k + 144, p1=32), view("pat8", 0, 144, p1=32), view("en", 144 * k, 144 * k + 144, p1=32), OP.add, OP.max)
+
+        def lists(k, name):
             for t in range(4):
                 ts(view(name, 0, 36, p0=32 * t, p1=32 * t + 32), view("es", 288 * k + 7, 288 * k + 288, 8, p1=32), 7 * 288.0 + 144.0, OP.add)
-            if k == 0:
-                send(rnd, "larr%d" % rnd, "lsent%d" % rnd, [(view("lp%d" % rnd, 0, 36), view("ls%d" % rnd, 0, 36))])
+
+        for k in range(4):
+            turned(576 * k, 576 * k + 576)
+        for k in range(3):
+            entries(k)
+        largest(0)
+        largest(1)
+        entries(3, 2)
+        for f in keeps:
+            f()
+        largest(2)
+        lists(0, "ls%d" % rnd)
+        send(rnd, "larr%d" % rnd, "lsent%d" % rnd, [(view("lp%d" % rnd, 0, 36), view("ls%d" % rnd, 0, 36))])
+        largest(3)
+        spare()
+        lists(1, "tl")
         spare()
 
     def half(k, win, lst):
@@ -572,8 +628,8 @@ def rank_program(g, core, T, topo):
 
     def layer(src, hf):
         def product(q):
-            mm(2 * q, H, "wl", 128 * q, src, 0)
-            mm(2 * q + 1, H, "eu", 128 * q, src, 0)
+            for k in (2 * q, 2 * q + 1):
+                mm(2 * (k % 4) + k // 4, H, "eu" if k // 4 else "wl", 128 * (k % 4), src, 0)
 
         r = [view("rl", 576 * hf + 144 * q, 576 * hf + 144 * q + 144) for q in range(4)]
         o = [view("tw", 576 * hf + 288 * (q // 2) + q % 2, 576 * hf + 288 * (q // 2) + 288, 2) for q in range(4)]
@@ -583,10 +639,11 @@ def rank_program(g, core, T, topo):
     def swap(c0, c1, d0, d1):
         return [lambda: turn(view("tz", 16 + c0, 16 + c1), view("tw", c0, c1)), lambda: turn(view("tw", 1152 + d0, 1152 + d1), view("tz", d0, d1))]
 
-    def home():
+    def home(last):
         win = view("tw", 0, 2336)
         w0, w1 = CUT, C - CUT
         vfetch(view("o2", 0, w0), win, view("hl", 0, AC))
+        spare()
         for q in range(1, 4):
             fetch(view("o2", w0 * q, w0 * q + w0), win, view("hl", AC * q, AC * q + AC))
         for q in (0, 2):
@@ -596,8 +653,9 @@ def rank_program(g, core, T, topo):
             move("G" if n in (3, 7) else "V", view("xt", t, 4 * w0, 4, 32 * q, 32 * q + 32), view("o2", w0 * q, w0 * q + w0, 1, 32 * t, 32 * t + 32))
         for n in range(16):
             q, t = n // 4, n % 4
-            move("G" if n == 3 else "S" if n > 11 else "V", view("xt", 4 * w0 + t, 1152, 4, 32 * q, 32 * q + 32), view("o2", 4 * w0 + w1 * q, 4 * w0 + w1 * q + w1, 1, 32 * t, 32 * t + 32))
+            move("G" if n == 3 or (last and n == 7) else "S" if n > 11 else "V", view("xt", 4 * w0 + t, 1152, 4, 32 * q, 32 * q + 32), view("o2", 4 * w0 + w1 * q, 4 * w0 + w1 * q + w1, 1, 32 * t, 32 * t + 32))
             if n == 3:
+                spare()
                 quant("x", view("xt", 0, 4 * CUT), 0, CUT)
 
     def places_out():
@@ -615,17 +673,15 @@ def rank_program(g, core, T, topo):
         local(rnd)
         places(rnd)
         seats(rnd)
-        if rnd == 2:
-            jobs.extend([places_out, places_out2])
-        for f in half(1, "fw", "tl"):
-            f()
-        other = half(0, "fp", "lp%d" % rnd)
+        mine, other = half(1, "fw", "tl"), half(0, "fp", "lp%d" % rnd)
         (pb, rb, sb), (pa, ra, sa) = layer("tb", 1), layer("ta", 0)
         one, end, mid, two = swap(576, 1152, 608, 896), swap(0, 0, 896, 1184), swap(0, 288, 0, 288), swap(288, 576, 288, 608)
-        for f in (pb + other[:1] + rb[:1] + other[1:17] + rb[1:] + sb[:1] + other[17:] + sb[1:] + [lambda: spare(99)] + pa + ra
-                  + one[:1] + sa + mid[:1] + one[1:] + two[:1] + mid[1:] + end[1:] + two[1:]):
+        for f in (mine[:17] + other[:1] + mine[17:] + pb + other[1:17] + rb + other[17:] + sb + [spare] + pa + ra + one[:1] + [spare]
+                  + sa + [spare] + mid[:1] + one[1:] + two[:1] + [lambda: spare(99)] + mid[1:] + end[1:] + two[1:]):
             f()
-        home()
+        if rnd == 2:
+            jobs.extend([places_out, places_out2])
+        home(rnd == 2)
     mm(0, CUT, "v", 0, "x", 0)
     dma("outd", T.oc[:, 0:4 * CUT], T.x_q[:, 0:CUT].bitcast(dt.uint8), [view("x_q", 0, CUT)], [])
     quant("x", view("xt", 4 * CUT, 1152), CUT, C)

from concourse.mybir import dt, AluOpType, AxisListType, ActivationFunctionType

OP = AluOpType
ACT = ActivationFunctionType
C = 288
H = 144
BIG = 1.0e29
EPS = 2.0 ** -24 + 2.0 ** -32
DELTA = 2.0 ** -120
STEP = 4096.0
LOW = 8192.0
EMPTY = -32768.0
CUT = 160
AC = CUT // 16
LATE = (6, 4, 4)
PARTS = ((2, 0, CUT), (4, CUT, C))
FREE = (5, 0, 3, 1, 6, 7)
MASKS = [1, 2, 3]
ML = [128, 0, 192, 384, 640]
MW = [64, 128, 192, 256, 288]
BY_SCALAR = (17, 16)
SB = [2, 3, 4, 0, 5, 6, 7]
RB = (1, 3, 1)
M2, M4, M8, M32 = [1.5 * 2.0 ** (23 + k) for k in (1, 2, 3, 5)]

SCRATCH = {}
for _t, _s in (
        ("float32", "pf 16 i16 288 i16s 288 i17 296 gi 256 pata 288 patb 288 patr 288 patc 288 pats 288 pat8 288 cst 32 hpat 192 dm 288 sc 288 ssb 288 rs 72 scr 288 scn 288 sort 288 wr 312 dec 24 wn 48 s7 288 rt 1728 hb 96 hs 96 es 576 ntf 64 rl 1152 hx 256"),
        ("int32", "pi 8 ii 96"),
        ("uint16", "ul 16 wl 32 posl 18 off 128 phl 18 tl 36 hl 72 ls0 36 ls1 36 ls2 36 lp0 36 lp1 36 lp2 36"),
        ("bfloat16", "dump 2016 cval 576 ones 512 zer 1024 neg 768 gx 256 idx 256 ef 4096 ob 512 zr 2048 cn 1024 rc 1024 rq 584 xt 1152 ut 512 vt 512 ml 3968 mc 2016 mf 2304 iw0 2304 iw1 2304 iw2 2304 itr 2304 fw 2304 fp 2304 ow 1152 tt 1152 o2 1152 en 576 tw 2336 tz 1184 eu 2048"),
        ("mx", "ef 1024 ob 128 zr 512 cn 256 rc 256 rq 146 u 128 v 128 up 256 w 512 wl 512 eu 512 x 288 ml 1152 mc 632 mf 576 ta 144 tb 144 xp0 288 xp1 288 xp2 288")):
    _s = _s.split()
    for _n, _w in zip(_s[::2], _s[1::2]):
        if _t == "mx":
            SCRATCH[_n + "_q"] = ("sbuf", [128, int(_w)], "float8_e4m3fn_x4")
            SCRATCH[_n + "_s"] = ("sbuf", [128, int(_w)], "uint8")
        else:
            SCRATCH[_n] = ("sbuf", [128, int(_w)], _t)
for _m in range(8):
    SCRATCH["p%d" % _m] = ("psum", [128, 512], "float32")

SEMAPHORES = "sv sa st sg lx ly lu lw ls lv y0 y1 y2 y3 y4 y5 y6 y7 z0 z1 z2 outd arr0 arr1 arr2 sent0 sent1 sent2 larr0 larr1 larr2 lsent0 lsent1 lsent2".split()


def rank_program(g, core, T, topo):
    rank = T.rank_of(core)
    if rank is None:
        return
    wait = {"V": g.vector.wait_ge, "S": g.scalar.wait_ge, "T": g.tensor.wait_ge, "G": g.wait_ge, "Y": g.sync.wait_ge}
    own = {"V": "sv", "S": "sa", "T": "st", "G": "sg"}
    total, snaps, hist = {}, {}, {}
    known = {q: {} for q in "VSTGYR"}

    def view(name, c0, c1, st=1, p0=0, p1=128):
        if p0 == 0 and p1 == 128:
            ap = T[name][:, c0:c1] if st == 1 else T[name][:, c0:c1:st]
        else:
            ap = T[name][p0:p1, c0:c1] if st == 1 else T[name][p0:p1, c0:c1:st]
        return (name, p0, p1, c0, c1, st, ap)

    def clash(a, b):
        if a[1] >= b[2] or b[1] >= a[2] or a[3] >= b[4] or b[3] >= a[4]:
            return False
        return not (a[5] == b[5] and a[5] > 1 and (a[3] - b[3]) % a[5])

    def covers(a, b):
        return a[1] <= b[1] and a[2] >= b[2] and a[3] <= b[3] and a[4] >= b[4] and (a[5] == 1 or (a[5] == b[5] and (a[3] - b[3]) % a[5] == 0))

    def settle(q, reads, writes, group=False):
        need = {}
        for kind, vs in (("r", reads), ("w", writes)):
            for v in vs:
                bank = SCRATCH[v[0]][0] == "psum"
                for (k2, q2, v2, sem, val) in hist.get(v[0], []):
                    if q2 == q and q in "VSTG":
                        if (kind == "r" and k2 == "r") or (group and bank) or not clash(v, v2):
                            continue
                    elif not bank and ((kind == "r" and k2 == "r") or not clash(v, v2)):
                        continue
                    if sem[0] == "z":
                        val = total[sem]
                    need[sem] = max(need.get(sem, 0), val)
        kn = known[q]
        for sem, val in sorted(need.items(), key=lambda e: -e[1]):
            if kn.get(sem, 0) >= val:
                continue
            wait[q](T.sem[sem], val)
            kn[sem] = val
            for s2, v2 in snaps.get((sem, val), {}).items():
                kn[s2] = max(kn.get(s2, 0), v2)

    def note(q, sem, val, reads, writes):
        snaps[(sem, val)] = dict(known[q])
        for k, vs in (("w", writes), ("r", reads)):
            for v in vs:
                h = hist.setdefault(v[0], [])
                if k == "w":
                    h[:] = [e for e in h if not covers(v, e[2])]
                else:
                    h[:] = [e for e in h if not (e[0] == "r" and e[1] == q and q in "VSTG" and covers(v, e[2]))]
                h.append((k, q, v, sem, val))

    def run(q, call, reads, writes, group=False):
        settle(q, reads, writes, group)
        sem = own[q]
        total[sem] = total.get(sem, 0) + 1
        call().then_inc(T.sem[sem], 1)
        note(q, sem, total[sem], reads, writes)

    def dma(sem, out, in_, reads, writes, q="Y"):
        settle(q, reads, writes)
        total[sem] = total.get(sem, 0) + 16
        (g.sync if q == "Y" else g.scalar).dma_start(out, in_).then_inc(T.sem[sem], 16)
        note("Y", sem, total[sem], reads, writes)

    def spread(sem, name, c0, c1, src):
        o, i = view(name, c0, c1), view(src, 0, c1 - c0)
        dma(sem, o[6], i[6], [i], [o])

    def send(rnd, arr, sent, pairs):
        dst = T.cores[rank ^ MASKS[rnd]]
        rid, pid = topo.addr(dst)[0], topo.addr(dst)[1]
        mask, ne = topo.mask(core, dst), len(topo.engines(core, dst))
        settle("G", [i for o, i in pairs], [])
        for o, i in pairs:
            codes = o[0].endswith("_q")
            g.remote_dma(o[6].bitcast(dt.uint8) if codes else o[6], i[6].bitcast(dt.uint8) if codes else i[6], T.sem[arr], T.sem[sent], pid, rid, mask)
        total[arr] = total[sent] = len(pairs) * ne
        note("R", arr, total[arr], [], [o for o, i in pairs])
        note("R", sent, total[sent], [i for o, i in pairs], [])

    def ap(x):
        return x[6] if isinstance(x, tuple) else x

    def rd(*xs):
        return [x for x in xs if isinstance(x, tuple)]

    def ts(out, a, s1, op0, s2=None, op1=None):
        if op1 is None:
            run("V", lambda: g.vector.tensor_scalar(out[6], a[6], ap(s1), None, op0), rd(a, s1), [out])
        else:
            run("V", lambda: g.vector.tensor_scalar(out[6], a[6], ap(s1), ap(s2), op0, op1), rd(a, s1, s2), [out])

    def tt(out, a, b, op):
        run("V", lambda: g.vector.tensor_tensor(out[6], a[6], b[6], op), [a, b], [out])

    def tc(out, a):
        run("V", lambda: g.vector.tensor_copy(out[6], a[6]), [a], [out])

    def fill(out, c):
        run("V", lambda: g.vector.memset(out[6], c), [], [out])

    def scan(out, d0, d1, op0, op1):
        run("V", lambda: g.vector.tensor_tensor_scan(out[6], d0[6], d1[6], 0.0, op0, op1), [d0, d1], [out])

    def fetch(out, win, off):
        run("S", lambda: g.scalar.activation(out[6], win[6].indirect(off[6]), ACT.Copy), [win, off], [out])

    def vfetch(out, win, off):
        run("V", lambda: g.vector.tensor_copy(out[6], win[6].indirect(off[6])), [win, off], [out])

    def fused(out, win, off, b, op):
        run("V", lambda: g.vector.tensor_tensor(out[6], win[6].indirect(off[6]), b[6], op), [win, off, b], [out])

    def scatter(win, off, a):
        run("V", lambda: g.vector.tensor_copy(win[6].indirect(off[6]), a[6]), [a, off], [win])

    def turn(out, a):
        run("V", lambda: g.vector.transpose(out[6], a[6]), [a], [out])

    def quant(n, a, c0, c1):
        o, p = view(n + "_q", c0, c1), view(n + "_s", c0, c1)
        run("V", lambda: g.vector.quantize_mx(o[6], p[6], a[6]), [a], [o, p])

    def act(out, a, f=ACT.Copy, scale=1.0, bias=0.0, acc=None):
        kw = {}
        if isinstance(scale, tuple) or scale != 1.0:
            kw["scale"] = ap(scale)
        if isinstance(bias, tuple) or bias != 0.0:
            kw["bias"] = ap(bias)
        if acc is not None:
            kw["accum_out"] = acc[6]
        run("S", lambda: g.scalar.activation(out[6], a[6], f, **kw), rd(a, scale, bias), rd(out, acc))

    def move(q, o, i):
        if q == "S":
            act(o, i)
        elif q == "G":
            n = len(range(o[3], o[4], o[5]))
            run("G", lambda: g.affine_select(o[6], i[6], [[0, n]], OP.is_equal, 0.0, 0, 0), [i], [o])
        else:
            tc(o, i)

    def iota(out, pattern, base=0, cm=0, f=True):
        if f:
            run("G", lambda: g.iota(out[6], pattern, base, cm, allow_small_or_imprecise_dtypes=True), [], [out])
        else:
            run("G", lambda: g.iota(out[6], pattern, base, cm), [], [out])

    def select(out, a, pattern, base):
        run("G", lambda: g.affine_select(out[6], a[6], pattern, OP.is_equal, 0.0, base, 1), [a], [out])

    def mm(bank, n, l, l0, r, r0, start=True, stop=True):
        o = view("p%d" % bank, 0, n)
        lq, ls, rq, rs = view(l + "_q", l0, l0 + 128), view(l + "_s", l0, l0 + 128), view(r + "_q", r0, r0 + n), view(r + "_s", r0, r0 + n)
        run("T", lambda: g.tensor.matmul_mx(o[6], lq[6], ls[6], rq[6], rs[6], start, stop), [lq, ls, rq, rs], [o], group=not start)

    def ps(bank, c0, c1, st=1):
        return view("p%d" % bank, c0, c1, st)

    def pick(dst, src, n0, n1, w, off):
        o, i, o2, i2 = view(dst + "_q", n0, n1), view(src + "_q", 0, w), view(dst + "_s", n0, n1), view(src + "_s", 0, w)
        return (lambda: run("V", lambda: g.vector.tensor_copy(o[6].bitcast(dt.uint32), i[6].bitcast(dt.uint32).indirect(off[6])), [i, off], [o]),
                lambda: fetch(o2, i2, off))

    for sem, name, src, c0, c1 in (("lu", "ut", T.u, 0, 512), ("lx", "xt", T.x, 0, 4 * CUT), ("ly", "xt", T.x, 4 * CUT, 1152)):
        dma(sem, T[name][:, c0:c1], src[:, c0:c1], [], [view(name, c0, c1)], "S" if name == "ut" else "Y")
    pf = [view("pf", k, k + 1) for k in range(13)]
    kappa, group, odd, kmid, klow, rest, rkc, basec, over, base0, hc0, hc1, hc2 = pf
    pi = [view("pi", k, k + 1) for k in range(4)]
    iota(pi[3], [[0, 1]], 0, 1, f=False)
    iota(view("ii", 0, 16), [[0, 2], [16, 8]], f=False)
    iota(view("i16", 0, 288), [[0, 18], [1, 16]])
    iota(view("gi", 0, 256), [[0, 2], [1, 8], [0, 16]])
    iota(view("i17", 0, 289), [[0, 17], [1, 17]])
    iota(view("cst", 24, 32), [[1, 8]], 1)

    fill(view("zer", 0, 1024), 0.0)
    ts(pi[0], pi[3], 15, OP.bitwise_and)
    ts(pi[1], pi[3], 4, OP.logical_shift_right)
    ts(pi[2], pi[3], 4, OP.logical_shift_right, 1, OP.bitwise_and)
    tc(view("ul", 0, 16), view("ii", 0, 16))
    fill(view("cval", 288, 576), 1.0)
    fill(view("rs", 0, 1), 0.0)
    fill(view("wn", 0, 48), 0.0)
    tc(view("pf", 0, 3), view("pi", 0, 3))
    act(view("ones", 0, 512), view("zer", 0, 512), ACT.Identity, 1.0, 1.0)
    for k, (name, c0, c1) in enumerate((("zr", 0, 1024), ("zr", 1024, 2048), ("ml", 0, 768), ("ef", 0, 1024), ("ef", 1024, 2048), ("ef", 2048, 3072), ("ef", 3072, 4096), ("rq", 0, 584))):
        spread("y%d" % k, name, c0, c1, "zer")
    dma("lw", T.w_q[:, 0:512].bitcast(dt.uint8), T.wc[:], [], [view("w_q", 0, 512)])
    dma("ls", T.w_s[:, 0:512], T.ws[:], [], [view("w_s", 0, 512)])

    def empty(r):
        for k in range(3):
            spread("z%d" % r, "iw%d" % r, 768 * k, 768 * k + 768, "neg")

    iota(view("ii", 32, 64), [[32, 4], [128, 4], [16, 2]], f=False)
    select(view("idx", 0, 256), view("ones", 0, 256), [[0, 2], [-1, 128]], 0)
    iota(view("cval", 0, 288), [[1, 288]], -144, 0)
    iota(view("mf", 1152 + 3, 2304, 4), [[0, 288]], 0, 0)
    for h in range(8):
        for t in range(4):
            select(view("ef", 512 * h + 128 * t + t, 512 * h + 128 * t + 128, 4), view("ones", 0, 32), [[0, 2], [-1, 16]], -16 * h)
    fill(view("cval", 288, 576, 16), 0.0)
    quant("ml", view("zer", 0, 896), 192, 416)
    ts(kmid, kappa, 0.5, OP.add)
    ts(view("pata", 0, 288), view("i16", 0, 288), kappa, OP.not_equal, -BIG, OP.mult)
    ts(view("patb", 0, 288), view("i16", 0, 288), kmid, OP.subtract, 1.0e27, OP.mult)
    act(klow, kappa, ACT.Identity, 2.0 ** 17, -2.0 ** 16)
    act(rest, group, ACT.Identity, -1.0, 8.0)
    act(rkc, kappa, ACT.Identity, STEP - 1, 15 - 15 * STEP - LOW)
    act(view("i16s", 0, 288), view("i16", 0, 288), ACT.Copy, 2.0 ** 17)
    for a in range(8, 18):
        w0, w1 = ML[a // 4], ML[a // 4] + MW[a // 4]
        act(view("ml", 4 * (w0 + 16 * a) + a % 4, 4 * w1, 4), view("zer", 0, w1 - w0 - 16 * a))
    act(view("ml", 4 * ML[4] + 3, 4 * ML[4] + 1152, 4), view("zer", 0, 288))
    quant("u", view("ut", 0, 512), 0, 128)
    quant("x", view("xt", 0, 4 * CUT), 0, CUT)
    for k in range(2):
        for f in pick("up", "u", 128 * k, 128 * k + 128, 128, view("ul", 8 * k, 8 * k + 8)):
            f()
        if k == 0:
            ts(view("gx", 0, 256), view("gi", 0, 256), group, OP.is_equal)
    ts(view("patr", 0, 288), view("i16s", 0, 288), klow, OP.subtract, STEP, OP.min)
    act(view("rs", 48, 64), view("zer", 0, 16), ACT.Identity, 1.0, rkc)
    for a in BY_SCALAR:
        act(view("rs", 48 + a, 49 + a), rkc, ACT.Identity, 1.0, 16.0 * a)
    for t in range(4):
        act(view("ob", t, 512, 4), view("gx", 0, 128))

    def shifted(name, src, ii):
        for i in ii:
            j = i if name == "cn" or i < 3 else i + 1 if i < 7 else 3
            o = view(name, 512 * (j // 4) + j % 4, 512 * (j // 4) + 512, 4)
            act(o, view(src, 112 - 16 * i, 240 - 16 * i) if i < 7 else view("zer", 0, 128), ACT.Copy, view("cst", 8 + i, 9 + i) if name == "rc" and i > 3 else 1.0)

    def constants_1():
        for z in range(4):
            for t in range(4):
                act(view("zr", 516 * z + 17 * t, 512 * z + 512, 64), view("gx", 0, 128, 16))

    def constants_2():
        ts(view("cst", 0, 4), view("cst", 24, 28), rest, OP.is_ge, -DELTA, OP.mult)
        ts(view("cst", 4, 8), view("cst", 28, 32), rest, OP.is_ge)
        ts(view("cst", 16, 20), view("cst", 24, 28), rest, OP.is_ge, 24.0, OP.mult)
        ts(view("wl", 0, 32), view("ii", 32, 64), kappa, OP.add)

    def constants_3():
        act(view("cst", 12, 16), view("cst", 4, 8), ACT.Identity, 2.0, -1.0)
        act(view("cst", 20, 24), view("cst", 4, 8), ACT.Identity, 8.0, 16.0)
        shifted("cn", "gx", range(8))
        shifted("rc", "idx", range(8))

    def constants_4():
        act(base0, kappa, ACT.Identity, STEP, -15 * STEP - 0.5)
        act(over, group, ACT.Relu, 272.0, -4 * 272.0)
        act(view("patc", 0, 288), view("patr", 0, 288))
        act(basec, over, ACT.Identity, 1.0, base0)
        act(hc0, odd, ACT.Identity, -16.0, 592.0)
        act(hc1, odd, ACT.Identity, -2336.0, 1184.0)
        act(hc2, odd, ACT.Identity, 2336.0, -1183.5)

    def constants_5():
        for k, c in enumerate((0.0, 1.0, 1.0 / 32.0, -1.0, -32.0)):
            act(view("hpat", k, 90, 5), view("zer", 0, 18), ACT.Identity, 1.0, c)
        act(view("hb", 1, 90, 5), view("zer", 0, 18), ACT.Identity, 1.0, -M32)
        for k, c in enumerate((-BIG, -576.0, -576.0, -576.0, 1440.0, -576.0, -576.0, -576.0)):
            act(view("pat8", k, 288, 8, p1=32), view("zer", 0, 36, p1=32), ACT.Identity, 1.0, c)
        act(view("hpat", 96, 186), view("ones", 0, 90))
        for c in (0, 1168):
            act(view("tz", c, c + 16), view("zer", 0, 16))
        act(view("hpat", 96, 186, 5), view("zer", 0, 18))
        for f in picks:
            f[1]()

    picks = [pick("wl", "w", 128 * h, 128 * h + 128, 512, view("wl", 8 * h, 8 * h + 8)) for h in range(4)]
    efq = [lambda h=h: quant("ef", view("ef", 512 * h, 512 * h + 512), 128 * h, 128 * h + 128) for h in range(8)]
    jobs = [lambda: quant("zr", view("zr", 0, 1024), 0, 256), lambda: quant("zr", view("zr", 1024, 2048), 256, 512), lambda: [efq[0](), quant("mc", view("zer", 0, 512), 0, 128)],
            lambda: quant("rc", view("rc", 0, 1024), 0, 256), lambda: quant("cn", view("cn", 0, 1024), 0, 256)] + efq[1:]
    jobs += [f[0] for f in picks]
    euq = [lambda k=k: quant("eu", view("eu", 1024 * k, 1024 * k + 1024), 256 * k, 256 * k + 256) for k in range(2)]

    def spare(n=1):
        for f in jobs[:n]:
            f()
        del jobs[:n]

    def unpack(dst, src, h, bank):
        mm(bank, C, "ef", 128 * h, src, 0)
        return lambda: act(view(dst, 288 * h, 288 * h + 288), ps(bank, 0, 288))

    def scalars(bank, c0, c1):
        tt(view("dm", c0, c1), ps(bank, c0, c1), view("pata", c0, c1), OP.add)
        return lambda: scan(view("sc", c0, c1), view("patb", c0, c1), view("dm", c0, c1), OP.min, OP.max)

    def slot(a, c0, c1):
        return view("ml", 4 * (ML[a // 4] + c0) + a % 4, 4 * (ML[a // 4] + c1), 4)

    def scal(a):
        return view("sc", 16 * a + 15, 16 * a + 16)

    def local(rnd):
        ring = [864]

        def compare(aa, bank):
            for a in aa:
                ts(slot(a, 0, 16 * a), ps(bank, 0, 16 * a), scal(a), OP.is_lt)

        def rows(aa):
            for a in aa:
                d = ring[0] if ring[0] + 16 * a <= 1728 else 864
                ring[0] = d + 16 * a
                act(view("dump", d, d + 16 * a), slot(a, 0, 16 * a), ACT.Identity, -1.0, 1.0, acc=view("rs", a, a + 1))

        def count(al, first=False, last=False):
            c0, w = ML[al] + (224 if al > 1 else 0), MW[al]
            if al == 0:
                quant("ml", view("ml", 0, 768), 0, 192)
            if al > 1:
                quant("ml", view("ml", 4 * ML[al], 4 * ML[al] + 4 * w), c0, c0 + w)
            mm(1, C if first else w, "ob", 0, "ml", c0, first, last)

        mm(2, CUT, "up", 0, "x", 0)
        first = [scalars(2, 0, 64), scalars(2, 64, CUT)]
        quant("x", view("xt", 4 * CUT, 1152), CUT, C)
        for f in first:
            f()
        send(rnd, "arr%d" % rnd, "sent%d" % rnd, [(view("xp%d_%s" % (rnd, k), 0, C), view("x_" + k, 0, C)) for k in "qs"])
        if rnd == 0:
            iota(view("neg", 0, 768), [[0, 768]], int(EMPTY), 0)
            constants_1()
            for q in range(4):
                select(view("eu", 512 * q, 512 * q + 512), view("ones", 0, 512), [[-1000, 4], [-1, 32], [1000, 4]], -32 * q)
        mm(1, C, "up", 0, "x", 0)
        mm(0, C, "up", 0, "x", 0)
        keeps = [unpack("fw", "x", h, 5 + h) for h in range(3 if rnd else 0)]
        for i in (1, 2):
            mm(SB[i], C, "up", 16 * (i + 1), "x", 0)
        compare((3, 2, 1, 7, 6, 5, 4), 2)
        second = scalars(0, CUT, C)
        compare((9, 8), 2)
        second()
        rows((3, 2, 1, 7, 6, 5, 4, 9, 8))
        for k, a in enumerate(BY_SCALAR):
            act(view("dump", 288 * k, 288 * k + 16 * a), ps(1, 0, 16 * a), ACT.Sign, -1.0, scal(a))
        if rnd == 0:
            quant("ob", view("ob", 0, 512), 0, 128)
        count(0, first=True)
        count(1)
        for k, a in enumerate(BY_SCALAR):
            act(slot(a, 0, 16 * a), view("dump", 288 * k, 288 * k + 16 * a), ACT.Relu, acc=view("rs", a, a + 1))
        mm(SB[0], C, "up", 16, "x", 0)
        compare(range(12, 16), 0)
        inside = view("ml", 4 * ML[4] + 2, 4 * ML[4] + 1152, 4)
        tt(inside, ps(0, 0, 288), view("sc", 0, 288), OP.is_le)
        count(3)
        scan(view("dump", 1728, 2016), view("cval", 288, 576), inside, OP.mult, OP.add)
        compare((10, 11), 0)
        rows((12, 13, 14, 15, 10, 11))
        tt(view("rs", 24, 42), view("rs", 48, 66), view("dump", 1743, 2016, 16), OP.subtract)
        count(4)
        count(2, last=True)
        tt(view("patr", 271, 288, 16), view("rs", 40, 42), view("rs", 16, 18), OP.subtract)
        if rnd == 0:
            constants_2()
        tt(view("patr", 15, 256, 16), view("rs", 0, 16), view("rs", 24, 40), OP.add)
        if rnd == 0:
            ts(view("pats", 0, 288), view("i17", 0, 288), kappa, OP.is_equal, -BIG, OP.mult)
        act(view("ssb", 0, 288), ps(0, 0, 288))
        for k in keeps:
            k()
        for i in (4, 5, 6, 3):
            mm(SB[i], C, "up", 16 * (i + 1), "x", 0)
        if rnd == 0:
            constants_3()
        act(view("s7", 0, 288), ps(SB[1], 0, 288))
        if rnd == 0:
            constants_4()

    def places(rnd):
        rk = view("scr", 15, 288, 16)
        scan(view("scr", 0, 288), ps(1, 0, 288), view("patr", 0, 288), OP.max, OP.add)
        spare()
        ts(view("posl", 0, 18), rk, LOW, OP.add)
        spare()
        scatter(view("sort", 0, 288), view("posl", 0, 18), view("ssb", 0, 288))
        spare()
        settle("Y", [view("posl", 0, 18)], [])
        empty(rnd)
        if rnd == 1:
            dma("lv", T.vt[:, 0:512], T.v[:], [], [view("vt", 0, 512)])
        scan(view("wr", 289, 305), view("pats", 0, 16), view("sort", 16, 288, 17), OP.add, OP.max)
        sp, runs, wn = view("wr", 304, 305), view("wr", 15, 288, 17), view("wn", 0, 48)
        scan(view("wr", 0, 288), view("pats", 0, 288), view("sort", 0, 288), OP.add, OP.max)

        def cell(i, z):
            k = min(i // 2, 2)
            c = 576 * k + (216 if k == 2 else 144) * z + 72 * (i - 2 * k)
            return view("mc", c, c + 72)

        def scores(i, z):
            return view("s7", z, 288, 4) if i == 1 else ps(SB[i], z, 288, 4)

        def below(i):
            for z in range(4):
                ts(cell(i, z), scores(i, z), sp, OP.subtract, view("cst", i, i + 1), OP.is_le)

        def signs(i):
            for z in range(4):
                act(view("dump", 288 * (i - 4) + 72 * z, 288 * (i - 4) + 72 * z + 72), scores(i, z), ACT.Sign, -1.0, sp)

        def ones(i):
            for z in range(4):
                act(cell(i, z), view("dump", 288 * (i - 4) + 72 * z, 288 * (i - 4) + 72 * z + 72), ACT.Relu, view("cst", 8 + i, 9 + i))

        def count(k):
            w, c0 = 54 if k == 2 else 36, 144 * k
            quant("mc", view("mc", 4 * c0, 4 * c0 + 16 * w), 128 + c0, 128 + c0 + 4 * w)
            for z in range(4):
                mm(RB[k], 128, "zr", 128 * z, "mc", c0 + w * (z + 1), z == 0, z == 3)

        def number(i):
            k = min(i // 2, 2)
            c = 18 * (i - 2 * k) + (74 if k == 2 else 92)
            return ps(RB[k], c, c + 18)

        def offsets(ii):
            for i in ii:
                ts(view("off", 18 * i, 18 * i + 18), number(i), view("cst", 8 + i, 9 + i) if i > 3 else 1.0, OP.mult, view("cst", 16 + i, 17 + i), OP.add)

        def numbers(ii):
            for i in ii:
                j = i if i < 3 else 69 + i
                tc(view("rq", j, j + 72, 4), number(i))

        def cmp(i):
            return view("mf", 1152 * (i // 4) + i % 4, 1152 * (i // 4) + 1152, 4)

        def against(i):
            r = view("rt", 288 * i, 288 * i + 288)
            fetch(r, wn, view("off", 18 * i, 18 * i + 18))
            tt(cmp(i), r, ps(SB[i], 0, 288), OP.is_ge)

        signs(4)
        act(view("dec", 0, 17), runs, ACT.Abs, EPS, DELTA)
        signs(5)
        act(view("wn", 0, 17), runs)
        ones(4)
        signs(6)
        ones(5)
        ones(6)
        below(0)
        below(1)
        below(2)
        count(0)
        below(3)
        tt(view("wn", 24, 41), runs, view("dec", 0, 17), OP.subtract)
        spare()
        count(1)
        spare()
        offsets((0, 1))
        numbers((0, 1))
        count(2)
        spare()
        offsets((2, 3))
        fused(cmp(1), wn, view("off", 18, 36), view("s7", 0, 288), OP.is_ge)
        numbers((2, 3))
        against(0)
        offsets((4, 5, 6))
        numbers((4, 5, 6))
        against(2)
        quant("rq", view("rq", 0, 584), 0, 146)
        for k in range(2):
            mm(RB[1], 128, "rc", 128 * k, "rq", 18 * k, k == 0, k == 1)
        against(3)
        against(4)
        quant("mf", view("mf", 0, 1152), 0, 288)
        for b, c0, c1 in PARTS:
            mm(b, c1 - c0, "cn", 0, "mf", c0, True, False)
        ts(view("hx", 236, 254), ps(RB[1], 0, 18), 17.0, OP.mult, basec, OP.add)
        against(5)
        for b, c0, c1 in PARTS:
            fetch(view("rt", 288 + c0, 288 + c1), wn, view("off", 108 + c0 // 16, 108 + c1 // 16))
        for b, c0, c1 in PARTS:
            tt(view("mf", 1154 + 4 * c0, 1152 + 4 * c1, 4), view("rt", 288 + c0, 288 + c1), ps(SB[6], c0, c1), OP.is_ge)
        tt(view("patc", 15, 288, 16), view("hx", 236, 254), rk, OP.add)
        spare()
        for b, c0, c1 in PARTS:
            quant("mf", view("mf", 1152 + 4 * c0, 1152 + 4 * c1), 288 + c0, 288 + c1)
            mm(b, c1 - c0, "cn", 128, "mf", 288 + c0, False, True)

    def way_home(n, hb):
        hx = [view("hx", k, 90, 5) for k in range(5)]
        n4, n8 = view("hx", 96, 114), view("hx", 120, 138)

        def cut(qq):
            for a0, a1, c in ((0, AC, 0), (AC, 18, 4 * AC)):
                for q in qq:
                    tc(view("hl", c + (a1 - a0) * q, c + (a1 - a0) * (q + 1), p1=32), view("hx", 148 + 5 * a0, 144 + 5 * a1, 5, 32 * q, 32 * q + 32))

        return [lambda: [ts(n4, n, LOW - 1.0, OP.add, M4, OP.add), ts(n8, n, LOW - 3.0, OP.add, M8, OP.add), ts(hx[4], n, 1151.25 - LOW, OP.is_ge, 288.0, OP.mult)],
                lambda: [ts(hx[0], hb[2], hc1, OP.mult, hc0, OP.add), ts(hx[1], hb[3], hc2, OP.mult),
                         ts(hx[2], n4, -M4, OP.add, 71.5, OP.mult), ts(hx[3], n8, -M8, OP.add, -71.75, OP.mult)],
                lambda: None,
                lambda: scan(view("hx", 144, 234), view("hpat", 96, 186), view("hx", 0, 90), OP.mult, OP.add),
                lambda: cut((0, 1)), lambda: cut((2, 3)),
                lambda: tc(view("hl", 0, 72, p0=32, p1=64), view("hl", 0, 72, p1=32)),
                lambda: tc(view("hl", 0, 72, p0=64), view("hl", 0, 72, p1=64))]

    def seats(rnd):
        spare(5)
        if rnd == 0:
            constants_5()
        todo = [("fw", "x", h) for h in range(3 if rnd else 0, 8)] + [("fp", "xp%d" % rnd, h) for h in range(8)]
        late = todo[-LATE[rnd]:]
        for n, (d, s, h) in enumerate(todo[:-LATE[rnd]]):
            unpack(d, s, h, FREE[n % 6])()
        n = view("scn", 15, 288, 16)
        for b, c0, c1 in PARTS:
            scan(view("scn", c0, c1), ps(b, 0, c1 - c0), view("patc", c0, c1), OP.max, OP.add)
        spare()
        hb = [view("hb", k, 90, 5) for k in range(5)]
        ts(hb[0], n, LOW - 15.0, OP.add, M32, OP.add)
        ts(hb[2], n, LOW, OP.add)
        for k in (3, 4):
            ts(hb[k], n, LOW + M2, OP.add, -M2, OP.add)
        way = way_home(n, hb)
        jobs.extend(way if rnd else way[:2] + [lambda: [way[3](), euq[0]()], euq[1], way[4], way[2]] + way[5:])
        spare()
        scan(view("hs", 0, 90), view("hpat", 0, 90), view("hb", 0, 90), OP.mult, OP.add)
        spare()
        ts(view("phl", 0, 18), view("hs", 4, 90, 5), 0.5, OP.mult, 8.0, OP.add)
        spare()
        iw = "iw%d" % rnd
        scatter(view(iw, 0, 2304), view("phl", 0, 18), view("cval", 0, 288))
        spare()
        keeps = [unpack(d, s, h, FREE[(n + 2) % 6]) for n, (d, s, h) in enumerate(late)]

        def turned(c0, c1):
            turn(view("itr", c0, c1), view(iw, c0, c1))

        def entries(k, v=0):
            for q in range(4):
                move("V" if q < v else "S", view("en", 144 * k + q, 144 * k + 144, 4, p1=32), view("itr", 576 * k, 576 * k + 576, 16, 32 * q, 32 * q + 32))

        def largest(k):
            scan(view("es", 144 * k, 144 * k + 144, p1=32), view("pat8", 0, 144, p1=32), view("en", 144 * k, 144 * k + 144, p1=32), OP.add, OP.max)

        def lists(k, name):
            for t in range(4):
                ts(view(name, 0, 36, p0=32 * t, p1=32 * t + 32), view("es", 288 * k + 7, 288 * k + 288, 8, p1=32), 7 * 288.0 + 144.0, OP.add)

        for k in range(4):
            turned(576 * k, 576 * k + 576)
        for k in range(3):
            entries(k)
        largest(0)
        largest(1)
        entries(3, 2)
        for f in keeps:
            f()
        largest(2)
        lists(0, "ls%d" % rnd)
        send(rnd, "larr%d" % rnd, "lsent%d" % rnd, [(view("lp%d" % rnd, 0, 36), view("ls%d" % rnd, 0, 36))])
        largest(3)
        spare()
        lists(1, "tl")
        spare()

    def half(k, win, lst):
        c0, win = 576 * k, view(win, 0, 2304)
        steps = [lambda: [vfetch(view("ow", c0, c0 + 288), win, view(lst, 0, 18)), fetch(view("ow", c0 + 288, c0 + 576), win, view(lst, 18, 36)), spare()]]
        for n in range(16):
            steps.append(lambda q=n // 4, t=n % 4, n=n: move("G" if n == 0 else "S" if n % 3 == 1 else "V", view("tt", c0 + t, c0 + 576, 4, 32 * q, 32 * q + 32), view("ow", c0 + q, c0 + 576, 4, 32 * t, 32 * t + 32)))
        steps.append(lambda: [spare(k), quant("tb" if k else "ta", view("tt", c0, c0 + 576), 0, 144)])
        return steps

    def layer(src, hf):
        def product(q):
            for k in (2 * q, 2 * q + 1):
                mm(2 * (k % 4) + k // 4, H, "eu" if k // 4 else "wl", 128 * (k % 4), src, 0)

        r = [view("rl", 576 * hf + 144 * q, 576 * hf + 144 * q + 144) for q in range(4)]
        o = [view("tw", 576 * hf + 288 * (q // 2) + q % 2, 576 * hf + 288 * (q // 2) + 288, 2) for q in range(4)]
        return ([lambda q=q: product(q) for q in range(4)], [lambda q=q: act(r[q], ps(2 * q, 0, 144), ACT.Relu, 0.03125) for q in range(4)],
                [lambda q=q: tt(o[q], ps(2 * q + 1, 0, 144), r[q], OP.add) for q in range(4)])

    def swap(c0, c1, d0, d1):
        return [lambda: turn(view("tz", 16 + c0, 16 + c1), view("tw", c0, c1)), lambda: turn(view("tw", 1152 + d0, 1152 + d1), view("tz", d0, d1))]

    def home(last):
        win = view("tw", 0, 2336)
        w0, w1 = CUT, C - CUT
        vfetch(view("o2", 0, w0), win, view("hl", 0, AC))
        spare()
        for q in range(1, 4):
            fetch(view("o2", w0 * q, w0 * q + w0), win, view("hl", AC * q, AC * q + AC))
        for q in (0, 2):
            fetch(view("o2", 4 * w0 + w1 * q, 4 * w0 + w1 * q + 2 * w1), win, view("hl", 4 * AC + (18 - AC) * q, 4 * AC + (18 - AC) * (q + 2)))
        for n in range(16):
            q, t = n // 4, n % 4
            move("G" if n in (3, 7) else "V", view("xt", t, 4 * w0, 4, 32 * q, 32 * q + 32), view("o2", w0 * q, w0 * q + w0, 1, 32 * t, 32 * t + 32))
        for n in range(16):
            q, t = n // 4, n % 4
            move("G" if n == 3 or (last and n == 7) else "S" if n > 11 else "V", view("xt", 4 * w0 + t, 1152, 4, 32 * q, 32 * q + 32), view("o2", 4 * w0 + w1 * q, 4 * w0 + w1 * q + w1, 1, 32 * t, 32 * t + 32))
            if n == 3:
                spare()
                quant("x", view("xt", 0, 4 * CUT), 0, CUT)

    def places_out():
        fill(view("ntf", 18, 32), 0.0)
        ts(view("ntf", 0, 18), view("scn", 15, 288, 16), LOW + 0.5, OP.add)
        quant("v", view("vt", 0, 512), 0, 128)

    def places_out2():
        turn(view("ntf", 32, 64), view("ntf", 0, 32))
        for gr in range(8):
            v = view("ntf", 32 + 16 * (gr % 2), 48 + 16 * (gr % 2), 1, 32 * (gr // 2), 32 * (gr // 2) + 18)
            dma("outd", T.pl[gr:gr + 1, :], v[6], [v], [])

    for rnd in range(3):
        local(rnd)
        places(rnd)
        seats(rnd)
        mine, other = half(1, "fw", "tl"), half(0, "fp", "lp%d" % rnd)
        (pb, rb, sb), (pa, ra, sa) = layer("tb", 1), layer("ta", 0)
        one, end, mid, two = swap(576, 1152, 608, 896), swap(0, 0, 896, 1184), swap(0, 288, 0, 288), swap(288, 576, 288, 608)
        for f in (mine[:17] + other[:1] + mine[17:] + pb + other[1:17] + rb + other[17:] + sb + [spare] + pa + ra + one[:1] + [spare]
                  + sa + [spare] + mid[:1] + one[1:] + two[:1] + [lambda: spare(99)] + mid[1:] + end[1:] + two[1:]):
            f()
        if rnd == 2:
            jobs.extend([places_out, places_out2])
        home(rnd == 2)
    mm(0, CUT, "v", 0, "x", 0)
    dma("outd", T.oc[:, 0:4 * CUT], T.x_q[:, 0:CUT].bitcast(dt.uint8), [view("x_q", 0, CUT)], [])
    quant("x", view("xt", 4 * CUT, 1152), CUT, C)
    mm(1, C - CUT, "v", 0, "x", CUT)
    act(view("dm", 0, CUT), ps(0, 0, CUT))
    dma("outd", T.y[:, 0:CUT], T.dm[:, 0:CUT], [view("dm", 0, CUT)], [])
    dma("outd", T.oc[:, 4 * CUT:4 * C], T.x_q[:, CUT:C].bitcast(dt.uint8), [view("x_q", CUT, C)], [])
    for k in range(4):
        v = view("x_s", 0, 288, 1, 32 * k, 32 * k + 4)
        dma("outd", T.osc[4 * k:4 * k + 4, :], v[6], [v], [], "S")
    tc(view("dm", CUT, C), ps(1, 0, C - CUT))
    dma("outd", T.y[:, CUT:C], T.dm[:, CUT:C], [view("dm", CUT, C)], [])
    for sem in SEMAPHORES:
        if known["G"].get(sem, 0) < total[sem]:
            g.wait_ge(T.sem[sem], total[sem])
